import numpy as np, ml_dtypes
CORES = [48,51,52,55]
N = 4
BF = ml_dtypes.bfloat16
def gentries(a):
    return np.ascontiguousarray(a.reshape(8, 16, -1).transpose(0, 2, 1)).reshape(8, -1)
def gtable(e):
    e = np.asarray(e); return np.ascontiguousarray(e.reshape(8, -1, 16).transpose(0, 2, 1)).reshape(128, -1).astype(np.int32)
VA, G, OB, W, CAP, S = 1280, 256, 2048, 4096, 256, 272
E0, M, RO = 3, 14, 6
WA, NIL = VA + G, W - 1
H = NIL - OB
KC = 6
def within(rng, ke, k):
    o = np.argsort(ke, kind="stable"); cnt = np.bincount(ke, minlength=KC); lo = np.add.accumulate(cnt) - cnt
    i = lo[k] + (rng.random(k.shape) * np.maximum(cnt[k], 1)).astype(np.int64)
    return o[np.minimum(i, ke.size - 1)]
def feat(rng, cen, k, a):
    v = np.swapaxes(cen[np.arange(8)[None, :, None], k], 2, 3)
    return v + rng.integers(-a, a + 1, v.shape)
def parts(rng, bd=None):
    if bd is None: bd = np.argsort(rng.random((N, 8, VA)), axis=-1)[..., :G]
    cen = rng.integers(-90, 91, (8, KC, 16)); ka = rng.integers(0, KC, (N, 8, VA)); kb = rng.integers(0, KC, (N, 8, OB))
    kx = np.concatenate([ka, np.take_along_axis(np.roll(ka, 1, axis=0), np.roll(bd, 1, axis=0), 2)], axis=2)
    eo = np.argsort(kx[:, :, None, :] + 1.5 * rng.random((N, 8, 16, WA)), axis=-1); ao = np.argsort(ka[:, :, None, :] + 1.5 * rng.random((N, 8, 16, VA)), axis=-1)
    nba = np.empty((N, 8, 16, VA), np.int64); np.put_along_axis(nba, ao, eo[..., np.arange(VA) * WA // VA], -1)
    ky = np.concatenate([kb, np.roll(kb, -1, axis=0)[..., :H]], axis=2); nbb = np.empty((N, 8, 16, OB), np.int64); f0 = np.empty((N, 8, 16, S), np.int64)
    dens = rng.choice(np.array([0.3, 0.5, 0.8]), (N, 8))
    for r in range(N):
        for g in range(8):
            k = np.where(rng.random((16, OB)) < 0.75, kb[r, g], rng.integers(0, KC, (16, OB)))
            nbb[r, g] = np.where(rng.random((16, OB)) < 0.04, NIL, within(rng, ky[r, g], k))
            keep = (rng.random((16, S)) < dens[r, g]) & (rng.random((1, S)) > 0.1)
            f0[r, g] = np.where(keep, within(rng, ky[r, g], np.broadcast_to(ka[r, g, :S], (16, S))), NIL)
    return dict(cen=cen, ka=ka, kb=kb, bd=bd, nba=nba, nbb=nbb, f0=f0, xa=feat(rng, cen, ka, 3), xb=feat(rng, cen, kb, 3))
def pack(d):
    t = lambda v, w: np.ascontiguousarray(np.reshape(v, (N, 128, w)))
    return {"xa": t(d["xa"], VA).astype(np.float32).astype(BF), "xb": t(d["xb"], OB).astype(np.float32).astype(BF), "nba": t(d["nba"], VA).astype(np.int32),
            "nbb": t(d["nbb"], OB).astype(np.int32), "f0": t(d["f0"], S).astype(np.int32), "bd": np.stack([gtable(a) for a in d["bd"]])}
def put(row, c, v):
    o = np.setdiff1d(np.arange(row.size), c); hit = o[np.isin(row[o], v)]
    row[hit] = np.setdiff1d(row[c], v)[:hit.size]; row[c] = v
def short(rng, d, r, g):
    z1, z2, x = S, S + 1, VA - 1; P = np.array([S // 4, S // 2, 3 * S // 4, VA - 4, VA - 3, VA - 2])
    T = rng.permutation(np.setdiff1d(np.arange(S), P[:3])); D1, D2 = int(T[0]), int(T[1]); T = T[2:]
    f = d["f0"][r, g]; f[:] = rng.integers(0, NIL, f.shape); f[:, P[:3]] = NIL; f[:15, D1] = NIL; f[:15, D2] = NIL
    m = np.concatenate([P[:3], np.arange(S + 2, VA)])
    for p in range(16):
        c, v = [z1, z2], [D1, D2]
        if p == 0: c, v = [z1, z2, x], [x, z1, int(T[0])]
        elif p == 1: v = [z2, D2]
        elif p == 2: c, v = [z1, z2, x], [D1, D2, z1]
        elif p < 9: c, v = [z1, z2, int(P[p - 3])], [D1, D2, z2]
        elif p < 15:
            i = m[(p - 9) * T.size:(p - 8) * T.size]; c, v = np.concatenate([c, i]), np.concatenate([v, T[:i.size]])
        else: v = [z1, z2]
        put(d["nba"][r, g, p], np.array(c, np.int64), np.array(v, np.int64))
def lone(rng, d, r, g, z0, L):
    c, u, w = OB - 1, VA - 1, S
    f = d["f0"][r, g]; nb = d["nba"][r, g]; v = rng.integers(0, NIL - 1, S)
    f[:] = NIL; f[rng.integers(0, 16, S), np.arange(S)] = v + (v >= c); f[:, 64 + rng.permutation(S - 64)[:z0]] = NIL
    f[:, 0] = NIL; f[0, 0] = NIL - 1; f[1:3, 1] = c
    cells = [0, u, w] if L == 0 else [u, u - 1] + [S + i for i in range(L)]
    d["xa"][r, g][:, cells] = 40; d["xb"][r, g][:, c] = 40; d["nbb"][r, g][:, c] = c
    for p in range(16):
        if L == 0:
            to = {u: p}
            if p == 1: to[w] = u
            if p == 2: to[0] = 1
            if p == 3: to[0] = w
        else:
            to = {u: 1 if p == 1 else S, u - 1: S if p == 1 else (1 if p == 2 else p)}
            for i in range(1, L + 1): to[S + i - 1] = u if p == 4 + i else (S + i if p == 3 and i < L else 16 * i + p)
        k = sorted(to); put(nb[p], np.array(k, np.int64), np.array([to[i] for i in k], np.int64))
def quiet(rng, d, r):
    for g in range(8):
        o = rng.permutation(min(S, CAP)); x, y = int(o[0]), int(o[1]); z = int(rng.integers(2 * CAP + 1, VA)); c = int(rng.integers(0, OB))
        d["f0"][r, g] = NIL; d["f0"][r, g][:, y] = c
        for p in range(16):
            d["nba"][r, g, p] = rng.permutation(VA)
            if p == 0: k, v = [x, y], [y, x]
            else: k, v = [x, z, y], [x, y, z]
            put(d["nba"][r, g, p], np.array(k, np.int64), np.array(v, np.int64))
        b = d["xb"][r, g][:, c]; d["xa"][r, g][:, x] = b + (E0 if g < 7 else E0 + 1); d["xa"][r, g][:, z] = b - (E0 + 1)
def setup_inputs(rng):
    return pack(parts(rng))
def setup_inputs_room(rng):
    d = parts(rng); d["xa"] = feat(rng, d["cen"], d["ka"], 1); d["xb"] = feat(rng, d["cen"], d["kb"], 1); z0 = (S - VA) % CAP
    d["xa"][:, ::2, M - 1:] = 127; d["xb"][:, ::2, M - 1:] = -127; d["xa"][:, 1::2, M:] = 127; d["xb"][:, 1::2, M:] = -127
    d["xa"][:, 1::4, :M] = rng.integers(-1, 2, (N, 2, M, VA)); d["xb"][:, 1::4, :M] = rng.integers(-1, 2, (N, 2, M, OB))
    for r in range(N):
        for g in (0, 4):
            z = z0 + (0, 1, -1)[(r + g // 2) % 3]; o = rng.permutation(S)
            d["f0"][r, g][:, o[:z]] = NIL; d["f0"][r, g, rng.integers(0, 16, S - z), o[z:]] = rng.integers(0, NIL, S - z)
        lone(rng, d, r, 2, z0, 0); lone(rng, d, r, 6, z0, RO - (VA - S + z0) // CAP)
        for g in (1, 5): short(rng, d, r, g)
    return pack(d)
def setup_inputs_ties(rng):
    d = parts(rng); d["xb"] = feat(rng, d["cen"], d["kb"], 0); v = feat(rng, d["cen"], d["ka"], 0)
    d["xa"] = v + rng.choice(np.array([0, E0, E0 + 1, E0 + 2]), v.shape, p=[0.3, 0.55, 0.12, 0.03]) * rng.choice(np.array([-1, 1]), v.shape)
    d["f0"][:, ::2] = d["f0"][:, ::2, :1].copy(); d["nbb"][:, 1::2] = d["nbb"][:, 1::2, 5:6].copy(); d["nbb"][:, 0, 15] = np.arange(OB)
    quiet(rng, d, 0)
    return pack(d)
def setup_inputs_ends(rng):
    o = 1 + np.argsort(rng.random((N, 8, VA - 2)), axis=-1)[..., :G - 2]; z = np.zeros((N, 8, 1), np.int64)
    d = parts(rng, np.concatenate([z, o, z + VA - 1], axis=2)); ends = np.array([0, H - 1, H, OB - 1, OB, W - 2, NIL])
    d["cen"][::2] = d["cen"][::2, :1].copy(); d["cen"][4] = 125; d["cen"][6] = -125
    d["xa"] = feat(rng, d["cen"], d["ka"], 2); d["xb"] = feat(rng, d["cen"], d["kb"], 2)
    d["f0"] = np.where(rng.random(d["f0"].shape) < 0.5, rng.choice(ends, d["f0"].shape), d["f0"])
    e = d["nbb"][:, ::2]; d["nbb"][:, ::2] = np.where(rng.random(e.shape) < 0.5, rng.choice(ends, e.shape), e)
    d["nbb"][:, 5] = NIL; d["f0"][0, 7] = NIL; d["nba"][:, 2, 0] = np.arange(VA); d["nba"][:, 2, 1] = WA - 1 - np.arange(VA)
    return pack(d)
def setup_inputs_cross(rng):
    h = min(S, G) // 2; a = np.argsort(rng.random((N, 8, S)), axis=-1)[..., :h]; b = S + np.argsort(rng.random((N, 8, VA - S)), axis=-1)[..., :G - h]
    bd = np.concatenate([a, b], axis=2); bd = np.take_along_axis(bd, np.argsort(rng.random(bd.shape), axis=-1), 2); d = parts(rng, bd)
    noise = np.full((1, 8, 1, 1), 3); noise[:, :2] = 1; d["xa"] = feat(rng, d["cen"], d["ka"], noise); d["xb"] = feat(rng, d["cen"], d["kb"], noise)
    for r in range(N):
        for g in range(8):
            far = OB + within(rng, d["kb"][(r + 1) % N, g, :H], np.broadcast_to(d["ka"][r, g, :S], (16, S))); f = d["f0"][r, g]
            d["f0"][r, g] = np.where((f != NIL) & (rng.random(f.shape) < 0.8), far, f)
    d["f0"][1::2, :4] = NIL; lo = np.arange(VA) < CAP
    for r in range(1, N, 2):
        for g in (0, 1):
            for p in range(16):
                row = d["nba"][r, g, p]; gh = row >= VA
                i = np.flatnonzero(gh & (lo == (g == 0))); j = np.flatnonzero(~gh & (lo == (g == 1))); k = min(i.size, j.size); i = i[:k]; j = j[:k]
                vi = row[i].copy(); row[i] = row[j]; row[j] = vi
    return pack(d)
def setup_inputs_spread(rng):
    d = parts(rng); cen = rng.integers(-127, 128, (8, KC, 16))
    for x, k, n in (("xa", d["ka"], VA), ("xb", d["kb"], OB)):
        v = np.clip(feat(rng, cen, k, rng.choice(np.array([0, 1, 2, 2, 3, 3, 5, 12]), (N, 8, 1, n))), -127, 127)
        v = np.where(rng.random((N, 8, 1, n)) < 0.125, rng.integers(-127, 128, v.shape), v)
        d[x] = v * (rng.random((N, 8, 1, n)) > 0.0625)
    d["nba"][:, :, 4:8] = np.argsort(rng.random((N, 8, 4, WA)), axis=-1)[..., :VA]
    d["nbb"] = np.where(rng.random(d["nbb"].shape) < 0.3, rng.integers(0, W, d["nbb"].shape), d["nbb"])
    return pack(d)
def check_inputs(d):
    bad = []
    for k, hi in (("nba", WA - 1), ("nbb", NIL), ("f0", NIL), ("bd", VA - 1)):
        if np.min(d[k]) < 0 or np.max(d[k]) > hi: bad.append("range of " + k)
    for k in ("xa", "xb"):
        v = d[k].astype(np.float32)
        if not np.all((v >= -127) & (v <= 127) & (np.rint(v) == v)): bad.append("whole numbers of " + k)
    s = np.sort(d["nba"], axis=2)
    if np.any(s[..., 1:] == s[..., :-1]): bad.append("repeated in a row of nba")
    s = np.sort(np.stack([gentries(a) for a in d["bd"]]), axis=2)
    if np.any(s[..., 1:] == s[..., :-1]): bad.append("repeated in bd")
    return bad
def reference(xa, xb, nba, nbb, f0, bd):
    A = xa.astype(np.float32).astype(np.int32).reshape(N, 8, 16, VA); own = xb.astype(np.float32).astype(np.int32).reshape(N, 8, 16, OB)
    na = nba.astype(np.int64).reshape(N, 8, 16, VA); no = nbb.astype(np.int64).reshape(N, 8, 16, OB); bl = np.stack([gentries(a) for a in bd]).astype(np.int64)
    B = np.zeros((N, 8, 16, W), np.int32); NB = np.full((N, 8, 16, W), NIL, np.int64)
    for r in range(N):
        q = (r + 1) % N; n = no[q, :, :, :H]
        B[r, :, :, :OB] = own[r]; B[r, :, :, OB:NIL] = own[q, :, :, :H]
        NB[r, :, :, :OB] = no[r]; NB[r, :, :, OB:NIL] = np.where(n < H, OB + n, NIL)
    F = np.full((N, 8, 16, VA), NIL, np.int64); F[..., :S] = f0.reshape(N, 8, 16, S)
    flag = np.ones((N, 8, VA), bool); e = [E0] * N; rows = np.arange(16)[:, None]
    for wave in range(RO):
        ext = []
        for r in range(N):
            q = (r - 1) % N; n = np.take_along_axis(F[q], bl[q][:, None, :], 2)
            ext.append(np.concatenate([F[r], np.where((n >= OB) & (n < NIL), n - OB, NIL)], axis=2))
        for r in range(N):
            good = 0
            for g in range(8):
                a = np.flatnonzero(flag[r, g] & np.all(F[r, g] == NIL, axis=0))[:CAP]
                x = A[r, g][:, a]; c = ext[r][g][rows, na[r, g][:, a]]; col = np.arange(a.size)
                new = np.full(c.shape, NIL, np.int64)
                for t in range(3):
                    near = (np.abs(B[r, g][:, c] - x[:, None, :]) <= e[r]).astype(np.int32)
                    v = (c != NIL) & (np.add.reduce(near, axis=0) >= M); new = np.where(v, c, new); some = np.any(v, axis=0)
                    if t == 0:
                        ok = some; b = np.where(ok, c[np.argmax(v, axis=0), col], NIL)
                    else:
                        b = np.where(some, c[15 - np.argmax(v[::-1], axis=0), col], b)
                    c = NB[r, g][:, b]
                s = a[ok]; b = b[ok]; F[r, g][:, s] = new[:, ok]
                A[r, g][:, s] = x[:, ok] + np.clip(B[r, g][:, b] - x[:, ok], -2, 2)
                flag[r, g, a] = False
                w = na[r, g][:, s].reshape(-1); flag[r, g, w[w < VA]] = True
                good += int(s.size)
            e[r] = E0 + (good & 1)
    return {"yf": F.reshape(N, 128, VA).astype(np.float32), "ya": A.reshape(N, 128, VA).astype(np.float32).astype(BF)}

@@ -1,0 +1,479 @@
+from concourse.mybir import AluOpType as OPS, ActivationFunctionType as AFT, AxisListType
+
+VA, OB, CAP, S, RO = 1280, 2048, 256, 272, 6
+CH, SUB = 128, 64
+OFF = 7
+HALO = OB + 1 + OFF
+NH = 2047
+C4 = 1.5 * 2.0 ** 26
+C3 = C4 + 8.0
+
+DTS = {"b": "bfloat16", "f": "float32", "h": "float16", "i": "int32", "u": "uint16"}
+BUFS = """AW3584b BW4104b NW4104f NT2048i HN2047f NA1792i F1792f FI272i BDI16i BDU16u IND320b FL3584f EW3584f FR2560f
+IDT1280f PAD256f TN80f FC80f ECW80f EL80f CU80f WT80f PP80f OFS80f OU80u ZZ80f FH256h FRL16u FRF16f NAU256u Ch256h Th256h
+LP256h LU256u SG4096h CB256f CL256u XR4096b D4096b NE4096b VV256b SC256h SA256f SB256f Ra256f Rb256f Rc256f TI16i TM16i
+TU16i UL16u FA16h LS16f LSU16u ES1f EI1i EO1i EC1f DX256b DC256b CI256i CJ256i GS256h YW1792f YT1280i IP1i LPI1i
+GPI1i PCF1f LPC1f GPC1f QE1f LM128f GM128f CM128f SAM128b SGL128b IDM128f IDH128h IDL128b TRI128f LTM128f WK128f TF128b
+TL128b TB128b TC128b BC128b BR128f ONE128b OH128h XL240f HE8f GE8f ZT240f ZM1920h EPM2048b ELM2048h DPM2048h KA128f
+KB256f KC256f"""
+SCRATCH = {}
+for _b in BUFS.split():
+    _n = _b.rstrip("bfhiu").rstrip("0123456789")
+    SCRATCH[_n] = ("sbuf", [128, int(_b[len(_n):-1])], DTS[_b[-1]])
+for _w in range(RO):
+    SCRATCH["LG%d" % _w] = ("sbuf", [128, 256], "float16")
+PS = ("PC0", "PC1", "PQ0", "PQ1", "PR", "PM")
+for _n in PS:
+    SCRATCH[_n] = ("psum", [128, 512], "float32")
+LOADS = ["f0", "nba", "xa", "xb", "bd", "nbb"]
+SEMAPHORES = (["cv", "cs", "cp", "cg", "hb", "hn", "lhb", "lhn", "oy", "oa"] + ["ld_" + n for n in LOADS]
+              + [k + str(w) for k in ("gh", "lg", "xf", "xe") for w in range(RO)])
+
+
+def rank_program(g, core, T, topo):
+    rank = T.rank_of(core)
+    if rank is None:
+        return
+    nxt, prv = T.cores[(rank + 1) % 4], T.cores[(rank + 3) % 4]
+    Q = {"v": g.vector, "s": g.scalar, "p": g.tensor, "g": g, "y": g.sync}
+    CS = {"v": "cv", "s": "cs", "p": "cp", "g": "cg"}
+    cnt = {"cv": 0, "cs": 0, "cp": 0, "cg": 0}
+    known = {q: {} for q in Q}
+    clocks = {}
+    acc = {}
+
+    def need(q, sem, val):
+        if known[q].get(sem, 0) >= val:
+            return
+        Q[q].wait_ge(T.sem[sem], val)
+        known[q][sem] = val
+        for s2, v2 in clocks.get((sem, val), {}).items():
+            if known[q].get(s2, 0) < v2:
+                known[q][s2] = v2
+
+    def deps(q, reads, writes):
+        want = {}
+        for lst, isw in ((reads, False), (writes, True)):
+            for name, lo, hi in lst:
+                ps = name in PS
+                for a in acc.get(name, []):
+                    if not ps and (a[1] <= lo or hi <= a[0]):
+                        continue
+                    if ps and a[2] == q and (q == "p" or not a[5]) or not (isw or a[5] or ps):
+                        continue
+                    if want.get(a[3], 0) < a[4]:
+                        want[a[3]] = a[4]
+        for sem in sorted(want):
+            need(q, sem, want[sem])
+
+    def note(q, reads, writes, sem, val):
+        c = dict(known[q])
+        c[sem] = val
+        clocks[(sem, val)] = c
+        for lst, isw in ((reads, False), (writes, True)):
+            for name, lo, hi in lst:
+                l = acc.setdefault(name, [])
+                if isw or name in PS:
+                    l[:] = [a for a in l if not (name in PS or (lo <= a[0] and a[1] <= hi))]
+                else:
+                    l[:] = [a for a in l if a[5] or a[2] != q or a[3] != sem or not (lo <= a[0] and a[1] <= hi)]
+                l.append([lo, hi, q, sem, val, isw])
+
+    def A(name, lo=0, hi=None, st=1):
+        if hi is None:
+            hi = T[name].shape[1]
+        ap = T[name][:, lo:hi] if st == 1 else T[name][:, lo:hi:st]
+        return (ap, [(name, lo, hi)], [])
+
+    def I(win, w, off, o0, o1):
+        return (T[win][:, 0:w].indirect(T[off][:, o0:o1]), [(win, 0, w)], [(off, o0, o1)])
+
+    def op(q, out, ins, call):
+        reads = list(out[2])
+        for x in ins:
+            reads += x[1] + x[2]
+        deps(q, reads, out[1])
+        sem = CS[q]
+        cnt[sem] += 1
+        call().then_inc(T.sem[sem], 1)
+        note(q, reads, out[1], sem, cnt[sem])
+
+    def u(x):
+        return x[0] if isinstance(x, tuple) else x
+
+    def cp(out, in_):
+        op("v", out, [in_], lambda: g.vector.tensor_copy(out=out[0], in_=in_[0]))
+
+    def tt(out, a, b, o):
+        op("v", out, [a, b], lambda: g.vector.tensor_tensor(out=out[0], in0=a[0], in1=b[0], op=o))
+
+    def ts(out, a, s1, o0, s2=None, o1=None):
+        ins = [a] + [x for x in (s1, s2) if isinstance(x, tuple)]
+        if o1 is None:
+            op("v", out, ins, lambda: g.vector.tensor_scalar(out=out[0], in0=a[0], scalar1=u(s1), scalar2=None, op0=o0))
+        else:
+            op("v", out, ins, lambda: g.vector.tensor_scalar(out=out[0], in0=a[0], scalar1=u(s1), scalar2=u(s2), op0=o0, op1=o1))
+
+    def ms(out, c):
+        op("v", out, [], lambda: g.vector.memset(out[0], c))
+
+    def act(out, in_, f=AFT.Copy, bias=0.0, scale=1.0):
+        if bias == 0.0 and scale == 1.0:
+            op("s", out, [in_], lambda: g.scalar.activation(out=out[0], in_=in_[0], func=f))
+        else:
+            op("s", out, [in_], lambda: g.scalar.activation(out=out[0], in_=in_[0], func=f, bias=bias, scale=scale))
+
+    def mm(out, lhsT, rhs, st, sp):
+        op("p", out, [lhsT, rhs], lambda: g.tensor.matmul(out=out[0], lhsT=lhsT[0], rhs=rhs[0], start=st, stop=sp))
+
+    def io(out, pat, base, cm=0, small=True):
+        if small:
+            op("g", out, [], lambda: g.iota(out[0], pat, base, cm, allow_small_or_imprecise_dtypes=True))
+        else:
+            op("g", out, [], lambda: g.iota(out[0], pat, base, cm))
+
+    def gcopy(out, in_, n):
+        op("g", out, [in_], lambda: g.affine_select(out[0], in_[0], [[0, n]], OPS.is_gt, 0.0, 1, 0))
+
+    def dma(q, out_ap, in_ap, reads, writes, sem):
+        deps(q, reads, writes)
+        Q[q].dma_start(out=out_ap, in_=in_ap).then_inc(T.sem[sem], 16)
+        note(q, reads, writes, sem, 16)
+
+    def send(dst, outp, inp, rsem, lsem):
+        deps("g", inp[1], [])
+        rid, pid, _ = topo.addr(dst)
+        g.remote_dma(out_ap=outp[0], in_ap=inp[0], remote_sem=T.sem[rsem], local_sem=T.sem[lsem], pid=pid, routing_id=rid,
+                     dma_engine_mask=topo.mask(core, dst))
+        note("g", inp[1], [], lsem, len(topo.engines(core, dst)))
+
+    def arrive(src, outp, rsem):
+        acc.setdefault(outp[1][0][0], []).append([outp[1][0][1], outp[1][0][2], "r", rsem, len(topo.engines(src, core)), True])
+
+    dma("s", T.FI[:], T.f0[:], [], [("FI", 0, S)], "ld_f0")
+    dma("s", T.BW[:, 8:8 + OB], T.xb[:], [], [("BW", 8, 8 + OB)], "ld_xb")
+    dma("y", T.BDI[:], T.bd[:], [], [("BDI", 0, 16)], "ld_bd")
+    dma("y", T.NA[:, 0:VA], T.nba[:], [], [("NA", 0, VA)], "ld_nba")
+    dma("s", T.AW[:, 0:VA], T.xa[:], [], [("AW", 0, VA)], "ld_xa")
+    HB, HNB = A("BW", HALO, HALO + NH), A("NW", HALO, HALO + NH)
+    arrive(nxt, HB, "hb")
+    arrive(nxt, HNB, "hn")
+    for w in range(RO):
+        arrive(prv, A("LG%d" % w), "gh%d" % w)
+
+    io(A("IP"), [[0, 1]], 0, 1, False)
+    io(A("LM"), [[0, 8], [1, 16]], 1)
+    io(A("GM"), [[1, 8], [0, 16]], 0)
+    io(A("CM"), [[1, 128]], 0)
+    io(A("TN"), [[1, 80]], VA)
+    io(A("PAD"), [[1, CAP]], 1536 + 64)
+    io(A("IDT"), [[1, 80], [80, 16]], 64)
+    io(A("NA", VA, 1792), [[1, 512]], VA, 0, False)
+    io(A("XL"), [[1, 240]], -112)
+    io(A("HE"), [[1, 8]], 0)
+    send(prv, HB, A("BW", 8, 8 + NH), "hb", "lhb")
+    need("y", "lhb", len(topo.engines(core, prv)))
+    dma("y", T.NT[:], T.nbb[:], [], [("NT", 0, OB)], "ld_nbb")
+    ms(A("FL", 0, VA), 33.0)
+    ms(A("EW", S, VA), 0.0)
+    ms(A("F", S, 1792), 0.0)
+    ms(A("ZZ"), 0.0)
+    ms(A("KB"), 64.0)
+    ms(A("KA"), 33.0)
+    ms(A("KC"), 0.0)
+    ts(A("LPI"), A("IP"), 15, OPS.bitwise_and)
+    ts(A("GPI"), A("IP"), 4, OPS.arith_shift_right)
+    cp(A("PCF"), A("IP"))
+    ts(A("LPC"), A("LPI"), 1.0, OPS.add)
+    cp(A("GPC"), A("GPI"))
+    ts(A("QE"), A("LPI"), 80.0, OPS.mult)
+    ts(A("TN"), A("TN"), A("QE"), OPS.add)
+    ts(A("SAM"), A("GM"), A("GPC"), OPS.is_equal)
+    ts(A("FI"), A("FI"), 1.0, OPS.add)
+    ts(A("IDM"), A("CM"), A("PCF"), OPS.is_equal)
+    ts(A("FI"), A("FI"), 4095, OPS.bitwise_and)
+    ts(A("WK"), A("LM"), A("LPC"), OPS.is_gt)
+    cp(A("F", 0, S), A("FI"))
+    tt(A("TRI"), A("WK"), A("SAM"), OPS.mult)
+    ts(A("IND"), A("F", 0, 320), 0.0, OPS.is_gt)
+    tt(A("SGL"), A("SAM"), A("LM"), OPS.mult)
+    for q in range(4):
+        ts(A("EPM", 128 * q, 128 * q + 128), A("SGL"), float(q + 1), OPS.is_equal, 1024.0, OPS.mult)
+        mm(A("PM", 0, 80), A("EPM", 128 * q, 128 * q + 128), A("IND", 80 * q, 80 * q + 80), q == 0, q == 3)
+    ms(A("FC"), 33.0)
+    tt(A("IDL"), A("IDM"), A("LM"), OPS.mult)
+    ts(A("ECW"), A("PM", 0, 80), 0.5, OPS.is_gt, 64.0, OPS.mult)
+
+    def ghosts_out(w):
+        act(A("GS"), I("F", VA, "BDU", 0, 16), AFT.Relu, -2048.0)
+        send(nxt, A("LG%d" % w), A("GS"), "gh%d" % w, "lg%d" % w)
+
+    def extract(w):
+        dma("y", T.ECW[:], T.EW[0:128:16, 0:VA], [("EW", 0, VA)], [("ECW", 0, 80)], "xe%d" % w)
+        dma("y", T.FC[:], T.FL[0:128:16, 0:VA], [("FL", 0, VA)], [("FC", 0, 80)], "xf%d" % w)
+
+    def select_a():
+        tt(A("EL"), A("FC"), A("ECW"), OPS.is_gt)
+        op("v", A("CU"), [A("EL"), A("ZZ")], lambda: g.vector.tensor_tensor_scan(
+            out=T.CU[:], data0=T.EL[:], data1=T.ZZ[:], initial=0.0, op0=OPS.add, op1=OPS.add))
+        mm(A("PM", 0, 1), A("TRI"), A("CU", 79, 80), True, True)
+        ts(A("WT"), A("EL"), -4096.0, OPS.mult)
+        tt(A("WT"), A("WT"), A("TN"), OPS.add)
+        ts(A("PP"), A("CU"), A("PM", 0, 1), OPS.add, 1.0, OPS.subtract)
+        tt(A("OFS"), A("WT"), A("PP"), OPS.max)
+        cp(A("OU"), A("OFS"))
+        act(A("FR", 0, CAP), A("PAD"))
+        act(I("FR", 2560, "OU", 0, 80), A("IDT"), AFT.Silu)
+
+    def select_b():
+        act(A("FH"), A("FR", 0, CAP))
+        for l in range(16):
+            mm(A("PM", 16, 32), A("DPM", 128 * l, 128 * l + 128), A("FH", l, CAP, 16), l == 0, l == 15)
+        ts(A("FRL"), A("PM", 16, 32), 64.0, OPS.subtract)
+        cp(A("NAU"), I("NA", 1792, "FRL", 0, 16))
+        ts(A("FRF"), A("PM", 16, 32), 64.0, OPS.subtract)
+
+    select_a()
+    cp(A("BDU"), A("BDI"))
+    ghosts_out(0)
+    mm(A("PM", 128, 128 + S), A("SAM"), A("IND", 0, S), True, True)
+    ts(A("EW", 0, S), A("PM", 128, 128 + S), 0.5, OPS.is_gt, 64.0, OPS.mult)
+    for p in range(16):
+        ts(A("DPM", 128 * p, 128 * p + 128), A("IDL"), float(p + 1), OPS.is_equal)
+    ms(A("BW", 0, 8), 1024.0)
+    ms(A("NW", 0, 8), -2048.0)
+    ms(A("AW", VA, 1792), 0.0)
+    ms(A("EC"), C3)
+    for p in range(4, 16):
+        ts(A("EPM", 128 * p, 128 * p + 128), A("SGL"), float(p + 1), OPS.is_equal, 1024.0, OPS.mult)
+    cp(A("IDH"), A("IDM"))
+    ts(A("BR"), A("IDM"), -128.0, OPS.mult)
+    ms(A("ONE"), 1.0)
+    ts(A("WK"), A("LM"), A("LPC"), OPS.is_lt)
+    tt(A("LTM"), A("WK"), A("SAM"), OPS.mult)
+    for m, o, b in (("TRI", "TF", "TB"), ("LTM", "TL", "TC")):
+        tt(A("WK"), A("IDM"), A(m), OPS.subtract)
+        ts(A(o), A("WK"), 512.0, OPS.mult)
+        ts(A(b), A(m), -512.0, OPS.mult)
+        tt(A(b), A(b), A("BR"), OPS.add)
+    select_b()
+
+    def rest():
+        for p in range(16):
+            ts(A("ELM", 128 * p, 128 * p + 128), A("SGL"), float(p + 1), OPS.is_equal, 16.0, OPS.mult)
+        ts(A("OH"), A("ONE"), 1.0 / 256.0, OPS.mult)
+        ts(A("BC"), A("ONE"), -109.0, OPS.mult)
+        ts(A("ZT"), A("XL"), 1.0, OPS.add, A("LPC"), OPS.is_equal)
+        ts(A("GE"), A("HE"), A("GPC"), OPS.is_equal)
+        for h in range(8):
+            ts(A("ZM", 240 * h, 240 * h + 240), A("ZT"), A("GE", h, h + 1), OPS.mult)
+
+    def pc(X, lo, hi):
+        return A("PC%d" % X, lo, hi)
+
+    def seeds(q, X, s):
+        a = CH * X + SUB * s
+        if q == "v":
+            ts(A("SG", 16 * a, 16 * a + 1024), I("F", 1792, "NAU", a, a + SUB), 2048.0, OPS.subtract, 0.0625, OPS.mult)
+        else:
+            act(A("SG", 16 * a, 16 * a + 1024), I("F", 1792, "NAU", a, a + SUB), AFT.Copy, -128.0, 0.0625)
+        for p in range(16):
+            mm(pc(X, SUB * s, SUB * s + SUB), A("DPM", 128 * p, 128 * p + 128), A("SG", 16 * a + p, 16 * a + 1024, 16), p == 0, p == 15)
+
+    def slist(X):
+        ts(A("CL", CH * X, CH * X + CH), pc(X, 0, CH), 16.0, OPS.mult, 2048.0 + OFF, OPS.add)
+        act(A("CB", CH * X, CH * X + CH), pc(X, 0, CH))
+
+    def xrep(X):
+        a, b = 16 * CH * X, 16 * CH * X + 16 * CH
+        (act if X else cp)(A("XR", a, b, 16), I("AW", 1792, "FRL", 8 * X, 8 * X + 8))
+        for k, n in ((8, 128), (4, 256), (2, 512), (1, 1024)):
+            if X:
+                gcopy(A("XR", a + k, b, 2 * k), A("XR", a, b, 2 * k), n)
+            else:
+                cp(A("XR", a + k, b, 2 * k), A("XR", a, b, 2 * k))
+
+    def G(X, s, n=SUB):
+        a = 16 * (CH * X + SUB * s)
+        tt(A("D", a, a + 16 * n), I("BW", 4104, "CL", a // 16, a // 16 + n), A("XR", a, a + 16 * n), OPS.subtract)
+
+    def H(X, s, n=SUB):
+        a, o = 16 * (CH * X + SUB * s), pc(X, SUB * s, SUB * s + n)
+        ts(A("NE", a, a + 16 * n), A("D", a, a + 16 * n), A("EC"), OPS.add, A("EC"), OPS.is_equal)
+        for p in range(16):
+            mm(o, A("EPM", 128 * p, 128 * p + 128), A("NE", a + p, a + 16 * n, 16), p == 0, False)
+        mm(o, A("BC"), A("ONE", 0, n), False, True)
+
+    def o1(t, X):
+        a = CH * X
+        act(A("VV", a, a + CH), pc(X, 0, CH), AFT.Sign)
+        mm(A("PQ%d" % X, 0, CH), A("TF" if t == 0 else "TL"), A("VV", a, a + CH), True, False)
+        mm(A("PQ%d" % X, 0, CH), A("TB" if t == 0 else "TC"), A("ONE"), False, True)
+
+    def o5(t, X):
+        a = CH * X
+        tt(A("SC", a, a + CH), A("PQ%d" % X, 0, CH), A("CB", a, a + CH), OPS.min)
+        for l in range(16):
+            mm(A("PQ%d" % X, 128, 136), A("ELM", 128 * l, 128 * l + 128), A("SC", a + l, a + CH, 16), l == 0, l == 15)
+
+    def tiny(t, X):
+        lo, hi = 8 * X, 8 * X + 8
+        cp(A("TI", lo, hi), A("PQ%d" % X, 128, 136))
+        if t > 0:
+            ts(A("TM", lo, hi), A("TI", lo, hi), 16383, OPS.bitwise_and)
+            tt(A("TI", lo, hi), A("TM", lo, hi), A("TU", lo, hi), OPS.max)
+        ts(A("TU", lo, hi), A("TI", lo, hi), 4095, OPS.bitwise_and)
+        ts(A("UL", lo, hi), A("TU", lo, hi), float(OFF), OPS.add)
+
+    pend, pcopy = [], []
+
+    def drain(n):
+        for _ in range(min(n, len(pend))):
+            pend.pop(0)()
+
+    def fails(w, X):
+        lo, hi, a = 8 * X, 8 * X + 8, CH * X
+        ts(A("FA", lo, hi), A("TU", lo, hi), 0.0, OPS.is_equal, 1792.0, OPS.mult)
+        if w < RO - 1:
+            mm(A("PR", a, a + CH), A("IDH"), A("LP", a, a + CH), True, False)
+            for p in range(16):
+                mm(A("PR", a + 8 * p, a + 8 * p + 8), A("IDH"), A("FA", lo, hi), False, p == 15)
+            pcopy.append(lambda: cp(A("LU", a, a + CH), A("PR", a, a + CH)))
+            for p in range(16):
+                pend.append(lambda p=p: act(I("FL", 3584, "LU", a + 8 * p, a + 8 * p + 8), A("KA"), AFT.Silu))
+        if X == 1:
+            tt(A("LS"), A("FRF"), A("FA"), OPS.add)
+            cp(A("LSU"), A("LS"))
+            if w < RO - 1:
+                pend.append(lambda: act(I("EW", 3584, "LSU", 0, 16), A("KB"), AFT.Silu))
+
+    def nbg(X):
+        a, nb = CH * X, I("NW", HALO + NH, "UL", 8 * X, 8 * X + 8)
+        ts(A("CL", a, a + CH), nb, 2048.0 + OFF, OPS.add)
+        act(A("CB", a, a + CH), nb, AFT.Copy, 0.0, 0.0625)
+
+    def rt(t, X):
+        a, b, r = CH * X, CH * X + CH, ("Ra", "Rb")[t]
+        tt(A(r, a, b), pc(X, 0, CH), A("CB", a, b), OPS.min)
+        act(A(("SA", "SB")[t], a, b), A(r, a, b), AFT.Copy, (-512.0, -256.0)[t])
+
+    def relay_a():
+        cp(A("Ch"), A("NAU"))
+        for h in range(2):
+            for k in range(8):
+                mm(A("PR", 32 * k + 16 * h, 32 * k + 16 * h + 16), A("Ch", 128 * h, 128 * h + 128), A("IDH", 16 * k, 16 * k + 16), True, True)
+
+    def relay_b(h0, h1):
+        for h in range(h0, h1):
+            for k in range(8):
+                mm(A("PR", 256 + h, 512, 8), A("ZM", 240 * h + 112 - 16 * k, 240 * h + 240 - 16 * k), A("Th", 32 * k, 32 * k + 32), k == 0, k == 7)
+
+    def decode(w, X):
+        a, b = CH * X, CH * X + CH
+        tt(pc(X, CH, 2 * CH), pc(X, 0, CH), A("CB", a, b), OPS.min)
+        tt(A("Rc", a, b), pc(X, CH, 2 * CH), A("Ra", a, b), OPS.max)
+        ts(A("CI", a, b), A("Rc", a, b), 16.0, OPS.mult, 2048.0, OPS.add)
+        ts(A("CJ", a, b), A("CI", a, b), 4095, OPS.bitwise_and)
+        if w < RO - 1:
+            cp(I("F", 1792, "FRL", 8 * X, 8 * X + 8), A("CJ", a, b))
+        else:
+            ts(A("CI", a, b), A("CJ", a, b), 1.0, OPS.subtract)
+            ts(A("CJ", a, b), A("CI", a, b), 4095, OPS.bitwise_and)
+            cp(I("YW", 1792, "FRL", 8 * X, 8 * X + 8), A("CJ", a, b))
+
+    def update_a():
+        xs = A("XR", 0, 4096, 16)
+        tt(A("DX"), I("BW", 4104, "UL", 0, 16), xs, OPS.subtract)
+        ts(A("DC"), A("DX"), -2.0, OPS.max, 2.0, OPS.min)
+        tt(I("AW", 3584, "LSU", 0, 16), A("DC"), xs, OPS.add)
+
+    def parity():
+        mm(A("PM", 64, 80), A("OH"), A("FA"), True, True)
+        op("v", A("ES"), [A("PM", 64, 80)], lambda: g.vector.tensor_reduce(out=T.ES[:], in_=T.PM[:, 64:80], axis=AxisListType.X, op=OPS.add))
+        cp(A("EI"), A("ES"))
+        ts(A("EO"), A("EI"), 1, OPS.bitwise_and)
+        ts(A("EC"), A("EO"), -8.0, OPS.mult, C3, OPS.add)
+
+    for w in range(RO):
+        last = w == RO - 1
+        act(A("F", VA, VA + 256), A("LG%d" % w))
+        if not last:
+            relay_a()
+        seeds("v", 0, 0)
+        seeds("s", 0, 1)
+        xrep(1)
+        seeds("s", 1, 0)
+        seeds("s", 1, 1)
+        if w == 0:
+            rest()
+        xrep(0)
+        slist(0)
+        if not last:
+            act(A("Th"), A("PR", 0, 256))
+            relay_b(0, 4)
+        if w == 0:
+            op("v", (T.BW[:, 4103:4104], [("BW", 4096, 4104)], []), [], lambda: g.vector.memset(T.BW[:, 4103:4104], 1024.0))
+        G(0, 0)
+        G(0, 1)
+        slist(1)
+        H(0, 0)
+        H(0, 1)
+        if not last:
+            act(I("FL", 3584, "FRL", 0, 16), A("KC"), AFT.Silu)
+        if w == 0:
+            ts(A("HN"), A("NT", 0, NH), 2047.0, OPS.min, 1.0, OPS.add)
+            send(prv, HNB, A("HN"), "hn", "lhn")
+            ts(A("NW", 8, 8 + OB), A("NT"), 2047.0, OPS.subtract)
+        for slot in range(5):
+            t, X = slot // 2, slot % 2
+            nX = 1 - X
+            o1(t, X)
+            if slot == 0 and not last:
+                relay_b(4, 8)
+                act(A("LP"), A("PR", 256, 512))
+            G(nX, 0, CH)
+            if pcopy:
+                pcopy.pop(0)()
+            if slot > 0:
+                drain((8, 9, 9, 99)[slot - 1])
+            o5(t, X)
+            H(nX, 0, CH)
+            tiny(t, X)
+            if t < 2:
+                rt(t, X)
+                nbg(X)
+            if t == 0:
+                fails(w, X)
+        o1(2, 1)
+        tt(A("Ra"), A("SA"), A("SB"), OPS.max)
+        decode(w, 0)
+        if not last:
+            extract(w + 1)
+        decode(w, 1)
+        if not last:
+            ghosts_out(w + 1)
+            select_a()
+        else:
+            dma("y", T.yf[:], T.YW[:, 0:VA], [("YW", 0, VA)], [], "oy")
+        o5(2, 1)
+        if not last:
+            parity()
+        tiny(2, 1)
+        update_a()
+        if last:
+            dma("y", T.ya[:], T.AW[:, 0:VA], [("AW", 0, VA)], [], "oa")
+        else:
+            if w == RO - 2:
+                ts(A("YT"), A("F", 0, VA), 1.0, OPS.subtract)
+                ts(A("YT"), A("YT"), 4095, OPS.bitwise_and)
+                cp(A("YW", 0, VA), A("YT"))
+            select_b()
+
+    need("y", "oy", 16)
+    need("y", "oa", 16)
+    for w in range(RO):
+        need("g", "lg%d" % w, 16)
+    need("g", "lhb", 16)
+    need("g", "lhn", 16)
+    for s in ("cv", "cs", "cp", "cg"):
+        need("y", s, cnt[s])

@@ -1,33 +1,37 @@
-from concourse.mybir import AluOpType as OPS, ActivationFunctionType as AFT, AxisListType
+from concourse.mybir import AluOpType as OPS, ActivationFunctionType as AFT
 
 VA, OB, CAP, S, RO = 1280, 2048, 256, 272, 6
 CH, SUB = 128, 64
 OFF = 7
 HALO = OB + 1 + OFF
 NH = 2047
+FIRST = S + CAP
 C4 = 1.5 * 2.0 ** 26
 C3 = C4 + 8.0
+WZ, THR = 16384.0, 18432.0
 
 DTS = {"b": "bfloat16", "f": "float32", "h": "float16", "i": "int32", "u": "uint16"}
-BUFS = """AW3584b BW4104b NW4104f NT2048i HN2047f NA1792i F1792f FI272i BDI16i BDU16u IND320b FL3584f EW3584f FR2560f
-IDT1280f PAD256f TN80f FC80f ECW80f EL80f CU80f WT80f PP80f OFS80f OU80u ZZ80f FH256h FRL16u FRF16f NAU256u Ch256h Th256h
-LP256h LU256u SG4096h CB256f CL256u XR4096b D4096b NE4096b VV256b SC256h SA256f SB256f Ra256f Rb256f Rc256f TI16i TM16i
-TU16i UL16u FA16h LS16f LSU16u ES1f EI1i EO1i EC1f DX256b DC256b CI256i CJ256i GS256h YW1792f YT1280i IP1i LPI1i
-GPI1i PCF1f LPC1f GPC1f QE1f LM128f GM128f CM128f SAM128b SGL128b IDM128f IDH128h IDL128b TRI128f LTM128f WK128f TF128b
-TL128b TB128b TC128b BC128b BR128f ONE128b OH128h XL240f HE8f GE8f ZT240f ZM1920h EPM2048b ELM2048h DPM2048h KA128f
-KB256f KC256f"""
+BUFS = """AW1792b YA3584b BW4104b NW4104i HS2048u HR2048u NA1792i F1792f FI272i BDI16i BDU16u IND320h W3584f FR3768f
+IDT1280f PAD256f DD80f WC80f EL80h CU80h MX80f OU80u INF80h SU480h KT400h ZF256f LP256h FH256h FRL16u NAU256u Ch256h Th256h
+LU256u SG4096h CB768h CL256u XR4096b D4096h NE4096h VV768h SC256h AB512f KY16f KM16f TI16i TM16i UL16u UF16u FA16h FS2f
+LSU16u EI1i EO1i EC1f DX256b DC256b GS256h YW1792f IP1i LPI1i GPI1i PCF1f LPC1f GPC1f QE1f CF1f CB1f
+LM128h CM128f XG144f XH144h EP144h EQ144h SAM128h IDM128f IDH128h IDN128h IDL128h TRI128h LTM128h WK128h TF128h TL128h PA128h PB128h
+PN128h ONE128h KC128h OH128f ZM1920h ZO1920h DPM2048h KA640f""".replace("CB1f", "CG1f")
 SCRATCH = {}
 for _b in BUFS.split():
     _n = _b.rstrip("bfhiu").rstrip("0123456789")
     SCRATCH[_n] = ("sbuf", [128, int(_b[len(_n):-1])], DTS[_b[-1]])
 for _w in range(RO):
     SCRATCH["LG%d" % _w] = ("sbuf", [128, 256], "float16")
-PS = ("PC0", "PC1", "PQ0", "PQ1", "PR", "PM")
+PS = ("PC0", "PC1", "PQ0", "PQ1", "PL", "PR", "PM", "PT")
 for _n in PS:
     SCRATCH[_n] = ("psum", [128, 512], "float32")
-LOADS = ["f0", "nba", "xa", "xb", "bd", "nbb"]
-SEMAPHORES = (["cv", "cs", "cp", "cg", "hb", "hn", "lhb", "lhn", "oy", "oa"] + ["ld_" + n for n in LOADS]
-              + [k + str(w) for k in ("gh", "lg", "xf", "xe") for w in range(RO)])
+LOADS = ["f0", "bd", "xb", "nba", "xa", "nb0", "nb1", "nba2", "xa2", "ya"]
+SEMAPHORES = (["cv", "cs", "cp", "cg", "hb", "hn0", "hn1", "lhb", "lhn0", "lhn1", "oy", "oa"] + ["ld_" + n for n in LOADS]
+              + [k + str(w) for k in ("gh", "lg", "xf") for w in range(RO)])
+
+VVE, KE = "ssvvvv", "..ssvv"
+DRAIN = {"a": 7, "b": 2, "c": 9, "d": 8}
 
 
 def rank_program(g, core, T, topo):
@@ -88,15 +92,17 @@ def rank_program(g, core, T, topo):
     def I(win, w, off, o0, o1):
         return (T[win][:, 0:w].indirect(T[off][:, o0:o1]), [(win, 0, w)], [(off, o0, o1)])
 
-    def op(q, out, ins, call):
-        reads = list(out[2])
+    def op(q, out, ins, call, outs=()):
+        reads, writes = list(out[2]), list(out[1])
         for x in ins:
             reads += x[1] + x[2]
-        deps(q, reads, out[1])
+        for x in outs:
+            writes += x[1]
+        deps(q, reads, writes)
         sem = CS[q]
         cnt[sem] += 1
         call().then_inc(T.sem[sem], 1)
-        note(q, reads, out[1], sem, cnt[sem])
+        note(q, reads, writes, sem, cnt[sem])
 
     def u(x):
         return x[0] if isinstance(x, tuple) else x
@@ -117,8 +123,10 @@ def rank_program(g, core, T, topo):
     def ms(out, c):
         op("v", out, [], lambda: g.vector.memset(out[0], c))
 
-    def act(out, in_, f=AFT.Copy, bias=0.0, scale=1.0):
-        if bias == 0.0 and scale == 1.0:
+    def act(out, in_, f=AFT.Copy, bias=0.0, scale=1.0, total=None):
+        if total is not None:
+            op("s", out, [in_], lambda: g.scalar.activation(out=out[0], in_=in_[0], func=f, bias=bias, scale=scale, accum_out=total[0]), [total])
+        elif bias == 0.0 and scale == 1.0:
             op("s", out, [in_], lambda: g.scalar.activation(out=out[0], in_=in_[0], func=f))
         else:
             op("s", out, [in_], lambda: g.scalar.activation(out=out[0], in_=in_[0], func=f, bias=bias, scale=scale))
@@ -126,19 +134,26 @@ def rank_program(g, core, T, topo):
     def mm(out, lhsT, rhs, st, sp):
         op("p", out, [lhsT, rhs], lambda: g.tensor.matmul(out=out[0], lhsT=lhsT[0], rhs=rhs[0], start=st, stop=sp))
 
+    def msum(out, terms, st=True, sp=True):
+        for k, (l, r) in enumerate(terms):
+            mm(out, l, r, st and k == 0, sp and k == len(terms) - 1)
+
     def io(out, pat, base, cm=0, small=True):
         if small:
             op("g", out, [], lambda: g.iota(out[0], pat, base, cm, allow_small_or_imprecise_dtypes=True))
         else:
             op("g", out, [], lambda: g.iota(out[0], pat, base, cm))
 
-    def gcopy(out, in_, n):
-        op("g", out, [in_], lambda: g.affine_select(out[0], in_[0], [[0, n]], OPS.is_gt, 0.0, 1, 0))
+    def gsel(out, in_, pat, base, cm):
+        op("g", out, [in_], lambda: g.affine_select(out[0], in_[0], pat, OPS.is_equal, 0.0, base, cm))
 
     def dma(q, out_ap, in_ap, reads, writes, sem):
         deps(q, reads, writes)
         Q[q].dma_start(out=out_ap, in_=in_ap).then_inc(T.sem[sem], 16)
         note(q, reads, writes, sem, 16)
+
+    def load(q, name, lo, hi, src, s0, sem):
+        dma(q, T[name][:, lo:hi], src[:, s0:s0 + hi - lo], [], [(name, lo, hi)], "ld_" + sem)
 
     def send(dst, outp, inp, rsem, lsem):
         deps("g", inp[1], [])
@@ -150,330 +165,463 @@ def rank_program(g, core, T, topo):
     def arrive(src, outp, rsem):
         acc.setdefault(outp[1][0][0], []).append([outp[1][0][1], outp[1][0][2], "r", rsem, len(topo.engines(src, core)), True])
 
-    dma("s", T.FI[:], T.f0[:], [], [("FI", 0, S)], "ld_f0")
-    dma("s", T.BW[:, 8:8 + OB], T.xb[:], [], [("BW", 8, 8 + OB)], "ld_xb")
-    dma("y", T.BDI[:], T.bd[:], [], [("BDI", 0, 16)], "ld_bd")
-    dma("y", T.NA[:, 0:VA], T.nba[:], [], [("NA", 0, VA)], "ld_nba")
-    dma("s", T.AW[:, 0:VA], T.xa[:], [], [("AW", 0, VA)], "ld_xa")
-    HB, HNB = A("BW", HALO, HALO + NH), A("NW", HALO, HALO + NH)
+    def EP(p, name="EP"):
+        return A(name, 15 - p, 143 - p)
+
+    def DP(p):
+        return A("DPM", 128 * p, 128 * p + 128)
+
+    load("s", "FI", 0, S, T.f0, 0, "f0")
+    load("y", "BDI", 0, 16, T.bd, 0, "bd")
+    load("y", "BW", 8, 8 + OB, T.xb, 0, "xb")
+    load("s", "NA", 0, FIRST, T.nba, 0, "nba")
+    load("s", "AW", 0, FIRST, T.xa, 0, "xa")
+    HB = A("BW", HALO, HALO + NH)
     arrive(nxt, HB, "hb")
-    arrive(nxt, HNB, "hn")
+    for h in range(2):
+        arrive(nxt, A("HR", 1024 * h, 1024 * h + 1024), "hn%d" % h)
     for w in range(RO):
         arrive(prv, A("LG%d" % w), "gh%d" % w)
 
     io(A("IP"), [[0, 1]], 0, 1, False)
-    io(A("LM"), [[0, 8], [1, 16]], 1)
-    io(A("GM"), [[1, 8], [0, 16]], 0)
+    io(A("XG"), [[1, 144]], -15)
     io(A("CM"), [[1, 128]], 0)
-    io(A("TN"), [[1, 80]], VA)
-    io(A("PAD"), [[1, CAP]], 1536 + 64)
+    io(A("DD"), [[1, 80]], VA + 1)
     io(A("IDT"), [[1, 80], [80, 16]], 64)
-    io(A("NA", VA, 1792), [[1, 512]], VA, 0, False)
-    io(A("XL"), [[1, 240]], -112)
-    io(A("HE"), [[1, 8]], 0)
-    send(prv, HB, A("BW", 8, 8 + NH), "hb", "lhb")
-    need("y", "lhb", len(topo.engines(core, prv)))
-    dma("y", T.NT[:], T.nbb[:], [], [("NT", 0, OB)], "ld_nbb")
-    ms(A("FL", 0, VA), 33.0)
-    ms(A("EW", S, VA), 0.0)
+    io(A("PAD"), [[1, CAP]], 1536 + 64)
     ms(A("F", S, 1792), 0.0)
-    ms(A("ZZ"), 0.0)
-    ms(A("KB"), 64.0)
-    ms(A("KA"), 33.0)
-    ms(A("KC"), 0.0)
+    ms(A("ZF"), 0.0)
+    ms(A("IND", S, 320), 0.0)
+    ms(A("ONE"), 1.0)
     ts(A("LPI"), A("IP"), 15, OPS.bitwise_and)
-    ts(A("GPI"), A("IP"), 4, OPS.arith_shift_right)
+    ts(A("GPI"), A("IP"), 112, OPS.bitwise_and)
     cp(A("PCF"), A("IP"))
-    ts(A("LPC"), A("LPI"), 1.0, OPS.add)
     cp(A("GPC"), A("GPI"))
-    ts(A("QE"), A("LPI"), 80.0, OPS.mult)
-    ts(A("TN"), A("TN"), A("QE"), OPS.add)
-    ts(A("SAM"), A("GM"), A("GPC"), OPS.is_equal)
-    ts(A("FI"), A("FI"), 1.0, OPS.add)
-    ts(A("IDM"), A("CM"), A("PCF"), OPS.is_equal)
-    ts(A("FI"), A("FI"), 4095, OPS.bitwise_and)
-    ts(A("WK"), A("LM"), A("LPC"), OPS.is_gt)
-    cp(A("F", 0, S), A("FI"))
-    tt(A("TRI"), A("WK"), A("SAM"), OPS.mult)
-    ts(A("IND"), A("F", 0, 320), 0.0, OPS.is_gt)
-    tt(A("SGL"), A("SAM"), A("LM"), OPS.mult)
+    ts(A("LPC"), A("LPI"), 1.0, OPS.add)
+    ts(A("EP"), A("XG"), A("GPC"), OPS.is_equal)
+    ts(A("IND", 0, S), A("FI"), 4095.0, OPS.not_equal)
     for q in range(4):
-        ts(A("EPM", 128 * q, 128 * q + 128), A("SGL"), float(q + 1), OPS.is_equal, 1024.0, OPS.mult)
-        mm(A("PM", 0, 80), A("EPM", 128 * q, 128 * q + 128), A("IND", 80 * q, 80 * q + 80), q == 0, q == 3)
-    ms(A("FC"), 33.0)
-    tt(A("IDL"), A("IDM"), A("LM"), OPS.mult)
-    ts(A("ECW"), A("PM", 0, 80), 0.5, OPS.is_gt, 64.0, OPS.mult)
+        mm(A("PM", 160, 240), EP(q), A("IND", 80 * q, 80 * q + 80), q == 0, q == 3)
+    ts(A("QE"), A("LPI"), 80.0, OPS.mult)
+    ts(A("IDM"), A("CM"), A("PCF"), OPS.is_equal)
+    ts(A("DD"), A("DD"), A("QE"), OPS.add)
+    ts(A("PN"), A("IDM"), -2048.0, OPS.mult)
+    ts(A("XH", 0, 128), A("CM"), A("GPC"), OPS.subtract)
+    ts(A("WK"), A("XH", 0, 128), A("LPC"), OPS.is_ge)
+    ts(A("SAM"), A("XH", 0, 128), 15.5, OPS.is_lt)
+    tt(A("TRI"), A("WK"), A("SAM"), OPS.mult)
+    ts(A("EL"), A("PM", 160, 240), 0.5, OPS.is_lt)
+    ts(A("SU", 0, 80), A("PM", 160, 240), 0.5, OPS.is_gt)
 
     def ghosts_out(w):
-        act(A("GS"), I("F", VA, "BDU", 0, 16), AFT.Relu, -2048.0)
+        ts(A("GS"), I("F", VA, "BDU", 0, 16), -2048.0, OPS.add, 0.0, OPS.max)
         send(nxt, A("LG%d" % w), A("GS"), "gh%d" % w, "lg%d" % w)
 
     def extract(w):
-        dma("y", T.ECW[:], T.EW[0:128:16, 0:VA], [("EW", 0, VA)], [("ECW", 0, 80)], "xe%d" % w)
-        dma("y", T.FC[:], T.FL[0:128:16, 0:VA], [("FL", 0, VA)], [("FC", 0, 80)], "xf%d" % w)
+        dma("y", T.WC[:], T.W[0:128:16, 0:VA], [("W", 0, VA)], [("WC", 0, 80)], "xf%d" % w)
 
-    def select_a():
-        tt(A("EL"), A("FC"), A("ECW"), OPS.is_gt)
-        op("v", A("CU"), [A("EL"), A("ZZ")], lambda: g.vector.tensor_tensor_scan(
-            out=T.CU[:], data0=T.EL[:], data1=T.ZZ[:], initial=0.0, op0=OPS.add, op1=OPS.add))
-        mm(A("PM", 0, 1), A("TRI"), A("CU", 79, 80), True, True)
-        ts(A("WT"), A("EL"), -4096.0, OPS.mult)
-        tt(A("WT"), A("WT"), A("TN"), OPS.add)
-        ts(A("PP"), A("CU"), A("PM", 0, 1), OPS.add, 1.0, OPS.subtract)
-        tt(A("OFS"), A("WT"), A("PP"), OPS.max)
-        cp(A("OU"), A("OFS"))
-        act(A("FR", 0, CAP), A("PAD"))
-        act(I("FR", 2560, "OU", 0, 80), A("IDT"), AFT.Silu)
+    BASE = A("PM", 256, 257)
 
-    def select_b():
-        act(A("FH"), A("FR", 0, CAP))
+    def select_a(w):
+        if w:
+            tt(A("EL"), A("WC"), A("PM", 160, 240), OPS.is_gt)
+        op("v", A("CU"), [A("EL"), A("ZF", 0, 80)], lambda: g.vector.tensor_tensor_scan(
+            out=T.CU[:], data0=T.EL[:], data1=T.ZF[:, 0:80], initial=0.0, op0=OPS.add, op1=OPS.add))
+        msum(A("PM", 0, 80), [(A("IDM"), A("DD")), (A("PN"), A("EL")), (A("PN"), A("EL"))])
+        mm(BASE, A("TRI"), A("CU", 79, 80), True, True)
+
+    def select_a2():
+        tt(A("MX"), A("PM", 0, 80), A("CU"), OPS.max)
+        ts(A("OU"), A("MX"), BASE, OPS.add)
+
+    def select_s():
+        act(I("FR", 3768, "OU", 0, 80), A("IDT"), AFT.Silu)
+        act(A("FH"), A("FR", 1, CAP + 1))
+
+    def select_p():
         for l in range(16):
-            mm(A("PM", 16, 32), A("DPM", 128 * l, 128 * l + 128), A("FH", l, CAP, 16), l == 0, l == 15)
-        ts(A("FRL"), A("PM", 16, 32), 64.0, OPS.subtract)
-        cp(A("NAU"), I("NA", 1792, "FRL", 0, 16))
-        ts(A("FRF"), A("PM", 16, 32), 64.0, OPS.subtract)
+            mm(A("PM", 272, 288), DP(l), A("FH", l, CAP, 16), l == 0, l == 15)
 
-    select_a()
-    cp(A("BDU"), A("BDI"))
-    ghosts_out(0)
-    mm(A("PM", 128, 128 + S), A("SAM"), A("IND", 0, S), True, True)
-    ts(A("EW", 0, S), A("PM", 128, 128 + S), 0.5, OPS.is_gt, 64.0, OPS.mult)
-    for p in range(16):
-        ts(A("DPM", 128 * p, 128 * p + 128), A("IDL"), float(p + 1), OPS.is_equal)
-    ms(A("BW", 0, 8), 1024.0)
-    ms(A("NW", 0, 8), -2048.0)
-    ms(A("AW", VA, 1792), 0.0)
-    ms(A("EC"), C3)
-    for p in range(4, 16):
-        ts(A("EPM", 128 * p, 128 * p + 128), A("SGL"), float(p + 1), OPS.is_equal, 1024.0, OPS.mult)
-    cp(A("IDH"), A("IDM"))
-    ts(A("BR"), A("IDM"), -128.0, OPS.mult)
-    ms(A("ONE"), 1.0)
-    ts(A("WK"), A("LM"), A("LPC"), OPS.is_lt)
-    tt(A("LTM"), A("WK"), A("SAM"), OPS.mult)
-    for m, o, b in (("TRI", "TF", "TB"), ("LTM", "TL", "TC")):
-        tt(A("WK"), A("IDM"), A(m), OPS.subtract)
-        ts(A(o), A("WK"), 512.0, OPS.mult)
-        ts(A(b), A(m), -512.0, OPS.mult)
-        tt(A(b), A(b), A("BR"), OPS.add)
-    select_b()
+    def select_b(w):
+        n = 1792 if w else FIRST
+        ts(A("FRL"), A("PM", 272, 288), 64.0, OPS.subtract)
+        cp(A("NAU"), I("NA", n, "FRL", 0, 16))
+        cp(A("XR", 0, 4096, 16), I("AW", n, "FRL", 0, 16))
 
-    def rest():
-        for p in range(16):
-            ts(A("ELM", 128 * p, 128 * p + 128), A("SGL"), float(p + 1), OPS.is_equal, 16.0, OPS.mult)
-        ts(A("OH"), A("ONE"), 1.0 / 256.0, OPS.mult)
-        ts(A("BC"), A("ONE"), -109.0, OPS.mult)
-        ts(A("ZT"), A("XL"), 1.0, OPS.add, A("LPC"), OPS.is_equal)
-        ts(A("GE"), A("HE"), A("GPC"), OPS.is_equal)
-        for h in range(8):
-            ts(A("ZM", 240 * h, 240 * h + 240), A("ZT"), A("GE", h, h + 1), OPS.mult)
-
-    def pc(X, lo, hi):
-        return A("PC%d" % X, lo, hi)
-
-    def seeds(q, X, s):
-        a = CH * X + SUB * s
-        if q == "v":
-            ts(A("SG", 16 * a, 16 * a + 1024), I("F", 1792, "NAU", a, a + SUB), 2048.0, OPS.subtract, 0.0625, OPS.mult)
-        else:
-            act(A("SG", 16 * a, 16 * a + 1024), I("F", 1792, "NAU", a, a + SUB), AFT.Copy, -128.0, 0.0625)
-        for p in range(16):
-            mm(pc(X, SUB * s, SUB * s + SUB), A("DPM", 128 * p, 128 * p + 128), A("SG", 16 * a + p, 16 * a + 1024, 16), p == 0, p == 15)
-
-    def slist(X):
-        ts(A("CL", CH * X, CH * X + CH), pc(X, 0, CH), 16.0, OPS.mult, 2048.0 + OFF, OPS.add)
-        act(A("CB", CH * X, CH * X + CH), pc(X, 0, CH))
+    def state(w):
+        ts(A("INF"), A("MX"), BASE, OPS.add, CAP + 0.5, OPS.is_lt)
+        if w:
+            ts(A("SU", 80 * w, 80 * w + 80), A("WC"), 8.0, OPS.is_lt)
+        msum(A("PM", 160, 240), [(A("IDH"), A("KT", 80 * w, 80 * w + 80)), (A("PN"), A("EL")), (A("PA"), A("INF"))]
+             + [(A("PA"), A("SU", 80 * k, 80 * k + 80)) for k in range(w + 1)])
 
     def xrep(X):
         a, b = 16 * CH * X, 16 * CH * X + 16 * CH
-        (act if X else cp)(A("XR", a, b, 16), I("AW", 1792, "FRL", 8 * X, 8 * X + 8))
         for k, n in ((8, 128), (4, 256), (2, 512), (1, 1024)):
             if X:
-                gcopy(A("XR", a + k, b, 2 * k), A("XR", a, b, 2 * k), n)
+                gsel(A("XR", a + k, b, 2 * k), A("XR", a, b, 2 * k), [[0, n]], 0, 0)
             else:
                 cp(A("XR", a + k, b, 2 * k), A("XR", a, b, 2 * k))
+
+    def relay_a():
+        cp(A("Ch"), A("NAU"))
+        for h in range(2):
+            for k in range(8):
+                mm(A("PT", 32 * k + 16 * h, 32 * k + 16 * h + 16), A("Ch", 128 * h, 128 * h + 128), A("IDH", 16 * k, 16 * k + 16), True, True)
+
+    def relay_b(h0, h1):
+        for h in range(h0, h1):
+            for k in range(8):
+                mm(A("PR", h, 256, 8), A("ZM", 240 * h + 112 - 16 * k, 240 * h + 240 - 16 * k), A("Th", 32 * k, 32 * k + 32), k == 0, k == 7)
+        if h1 == 8:
+            act(A("LP"), A("PR", 0, 256))
+
+    act(A("FR", 1, CAP + 1), A("PAD"))
+    select_a(0)
+    select_a2()
+    cp(A("BDU"), A("BDI"))
+    ts(A("FI"), A("FI"), 1.0, OPS.add)
+    ts(A("FI"), A("FI"), 4095, OPS.bitwise_and)
+    cp(A("F", 0, S), A("FI"))
+    send(prv, HB, A("BW", 8, 8 + NH), "hb", "lhb")
+    ghosts_out(0)
+    need("y", "lhb", len(topo.engines(core, prv)))
+    for h in range(2):
+        load("y", "NW", 8 + 1024 * h, 8 + 1024 * h + 1024, T.nbb, 1024 * h, "nb%d" % h)
+    ts(A("IDL"), A("IDM"), A("LPC"), OPS.mult)
+    for p in range(16):
+        ts(DP(p), A("IDL"), float(p + 1), OPS.is_equal)
+    select_s()
+    select_p()
+    io(A("KT"), [[16, 5], [0, 80]], 24)
+    io(A("KA"), [[16, 5], [0, 128]], 32)
+    io(A("ZO"), [[0, 1920]], 1)
+    gsel(A("ZM"), A("ZO"), [[-16, 8], [256, 15], [-1, 16]], -7 * 256, 1)
+    io(A("NA", 1536, 1792), [[1, CAP]], 1536, 0, False)
+    cp(A("IDH"), A("IDM"))
+    ts(A("EQ"), A("EP"), 2.0, OPS.mult)
+    ms(A("KC"), -27.0)
+    ms(A("EC"), C3)
+    ms(A("BW", 0, 8), 1024.0)
+    ts(A("PA"), A("IDM"), 2048.0, OPS.mult)
+    ts(A("PB"), A("IDM"), 4096.0, OPS.mult)
+    ts(A("WK"), A("XH", 0, 128), -0.5, OPS.is_gt)
+    ts(A("LM"), A("XH", 0, 128), 2.0, OPS.add, A("LPC"), OPS.is_le)
+    tt(A("LTM"), A("WK"), A("LM"), OPS.mult)
+    for m, o in (("TRI", "TF"), ("LTM", "TL")):
+        tt(A("WK"), A(m), A("IDH"), OPS.subtract)
+        ts(A(o), A("WK"), WZ, OPS.mult)
+    ts(A("CF"), A("LPC"), WZ, OPS.mult)
+    ts(A("CG"), A("LPC"), -WZ, OPS.mult, 17 * WZ, OPS.add)
+    ms(A("OH"), 1.0 / 256.0)
+    ms(A("NW", 0, 8), 4095)
+    ms(A("W", 0, VA), 16.0)
+    ms(A("AW", VA, 1792), 0.0)
+    select_b(0)
+
+    def late_loads():
+        need("y", "lhn1", len(topo.engines(core, prv)))
+        load("y", "NA", FIRST, VA, T.nba, FIRST, "nba2")
+        load("y", "AW", FIRST, VA, T.xa, FIRST, "xa2")
+        load("y", "YA", 0, VA, T.xa, 0, "ya")
+
+    def halo_out(h):
+        a = 1024 * h
+        ts(A("HS", a, a + 1024), A("NW", 8 + a, 8 + a + 1024), 2047.0, OPS.min, 2048.0, OPS.add)
+        if h:
+            ms(A("HS", 2047, 2048), 4095)
+        send(prv, A("HR", a, a + 1024), A("HS", a, a + 1024), "hn%d" % h, "lhn%d" % h)
+
+    def halo_in(h):
+        a = 1024 * h
+        cp(A("NW", HALO + a, HALO + a + 1024), A("HR", a, a + 1024))
+
+    def cb(t, X):
+        return A("CB", 256 * t + CH * X, 256 * t + CH * X + CH)
+
+    def vv(t, X, l=0, st=1):
+        return A("VV", 256 * t + CH * X + l, 256 * t + CH * X + CH, st)
+
+    def pq(X, k, n=1):
+        return A("PQ%d" % X, CH * k, CH * (k + n))
+
+    def sbank(s):
+        return A(("PC0", "PQ0", "PC1", "PQ1")[s], 384, 384 + SUB)
+
+    def seeds(s):
+        a = SUB * s
+        act(A("SG", 16 * a, 16 * a + 1024), I("F", 1792, "NAU", a, a + SUB), AFT.Copy, -2048.0)
+
+    def diag(s):
+        a = SUB * s
+        for p in range(16):
+            mm(sbank(s), DP(p), A("SG", 16 * a + p, 16 * a + 1024, 16), p == 0, p == 15)
+
+    def slist(s):
+        ts(A("CL", SUB * s, SUB * s + SUB), sbank(s), 2048.0 + OFF, OPS.add)
+
+    def numbers(t, X):
+        ts(cb(t, X), A("CL", CH * X, CH * X + CH), -2048.0 - OFF, OPS.add)
 
     def G(X, s, n=SUB):
         a = 16 * (CH * X + SUB * s)
         tt(A("D", a, a + 16 * n), I("BW", 4104, "CL", a // 16, a // 16 + n), A("XR", a, a + 16 * n), OPS.subtract)
 
     def H(X, s, n=SUB):
-        a, o = 16 * (CH * X + SUB * s), pc(X, SUB * s, SUB * s + n)
+        a = 16 * (CH * X + SUB * s)
         ts(A("NE", a, a + 16 * n), A("D", a, a + 16 * n), A("EC"), OPS.add, A("EC"), OPS.is_equal)
-        for p in range(16):
-            mm(o, A("EPM", 128 * p, 128 * p + 128), A("NE", a + p, a + 16 * n, 16), p == 0, False)
-        mm(o, A("BC"), A("ONE", 0, n), False, True)
 
-    def o1(t, X):
+    def count(X, s, n=SUB):
+        a, o = 16 * (CH * X + SUB * s), A("PC%d" % X, SUB * s, SUB * s + n)
+        msum(o, [(A("IDH"), A("KC", 0, n))] + [(EP(p, "EQ"), A("NE", a + p, a + 16 * n, 16)) for p in range(16)])
+
+    def sign(t, X):
+        if VVE[2 * t + X] == "s":
+            act(vv(t, X), A("PC%d" % X, 0, CH), AFT.Sign)
+        else:
+            ts(vv(t, X), A("PC%d" % X, 0, CH), -1.0, OPS.max, 1.0, OPS.min)
+
+    def rank_p(t, X):
+        msum(pq(X, 0), [(A("IDH"), cb(t, X)), (A("TL" if t else "TF"), vv(t, X))])
+
+    def choose(t, X):
         a = CH * X
-        act(A("VV", a, a + CH), pc(X, 0, CH), AFT.Sign)
-        mm(A("PQ%d" % X, 0, CH), A("TF" if t == 0 else "TL"), A("VV", a, a + CH), True, False)
-        mm(A("PQ%d" % X, 0, CH), A("TB" if t == 0 else "TC"), A("ONE"), False, True)
+        ts(A("SC", a, a + CH), pq(X, 0), A("CG" if t else "CF"), OPS.add, THR, OPS.min)
+        msum(A("PL", 16 * t + 8 * X, 16 * t + 8 * X + 8), [(A("PB"), A("ONE", 0, 8))] * (2 - t)
+             + [(EP(l), A("SC", a + l, a + CH, 16)) for l in range(16)])
 
-    def o5(t, X):
-        a = CH * X
-        tt(A("SC", a, a + CH), A("PQ%d" % X, 0, CH), A("CB", a, a + CH), OPS.min)
-        for l in range(16):
-            mm(A("PQ%d" % X, 128, 136), A("ELM", 128 * l, 128 * l + 128), A("SC", a + l, a + CH, 16), l == 0, l == 15)
+    def nbg(t, X):
+        lo = 8 * X
+        ts(A("UL", lo, lo + 8), A("PL", 16 * t + lo, 16 * t + lo + 8), 2048.0 + OFF - 15 * THR - 4096.0 * (2 - t), OPS.add, 4103.0, OPS.min)
+        ts(A("CL", CH * X, CH * X + CH), I("NW", 4104, "UL", lo, lo + 8), 8.0, OPS.add)
 
-    def tiny(t, X):
-        lo, hi = 8 * X, 8 * X + 8
-        cp(A("TI", lo, hi), A("PQ%d" % X, 128, 136))
-        if t > 0:
-            ts(A("TM", lo, hi), A("TI", lo, hi), 16383, OPS.bitwise_and)
-            tt(A("TI", lo, hi), A("TM", lo, hi), A("TU", lo, hi), OPS.max)
-        ts(A("TU", lo, hi), A("TI", lo, hi), 4095, OPS.bitwise_and)
-        ts(A("UL", lo, hi), A("TU", lo, hi), float(OFF), OPS.add)
+    def relu(t, X):
+        o = A("AB", 256 * X, 256 * X + 256)
+        if KE[2 * t + X] == "s":
+            act(o, pq(X, 1, 2), AFT.Relu, -2048.0)
+        else:
+            ts(o, pq(X, 1, 2), -2048.0, OPS.add, 0.0, OPS.max)
 
-    pend, pcopy = [], []
+    def keep_a(X, idn):
+        msum(pq(X, 1), [(idn, cb(0, X)), (A("PA"), vv(0, X)), (A("PN"), vv(1, X))])
+        msum(pq(X, 2), [(idn, cb(1, X)), (A("PB"), vv(1, X))])
+
+    def keep_b(X):
+        a = 256 * X
+        msum(pq(X, 1), [(A("IDM"), A("AB", a, a + CH)), (A("IDM"), A("AB", a + CH, a + 2 * CH))], True, False)
+
+    def keep_c(X, idn):
+        mm(pq(X, 1), A("PN"), vv(2, X), False, True)
+        msum(pq(X, 2), [(idn, cb(2, X)), (A("PB"), vv(2, X))])
+
+    def store(w, X):
+        a = 256 * X
+        old, new = A("AB", a, a + CH), A("AB", a + CH, a + 2 * CH)
+        if w < RO - 1:
+            tt(I("F", 1792, "FRL", 8 * X, 8 * X + 8), old, new, OPS.add)
+        else:
+            ts(old, old, -1.0, OPS.mult, 4095.0, OPS.add)
+            tt(I("YW", 1792, "FRL", 8 * X, 8 * X + 8), old, new, OPS.subtract)
+
+    pend = []
 
     def drain(n):
         for _ in range(min(n, len(pend))):
             pend.pop(0)()
 
-    def fails(w, X):
+    def fails_p(X):
+        msum(A("PL", 48 + 8 * X, 56 + 8 * X), [(EP(l), vv(0, X, l, 16)) for l in range(16)])
+
+    def fails_s(w, X):
         lo, hi, a = 8 * X, 8 * X + 8, CH * X
-        ts(A("FA", lo, hi), A("TU", lo, hi), 0.0, OPS.is_equal, 1792.0, OPS.mult)
+        act(A("FA", lo, hi), A("PL", 48 + lo, 48 + hi), AFT.Relu, -896.0 * 14, -896.0, A("FS", X, X + 1))
         if w < RO - 1:
             mm(A("PR", a, a + CH), A("IDH"), A("LP", a, a + CH), True, False)
             for p in range(16):
                 mm(A("PR", a + 8 * p, a + 8 * p + 8), A("IDH"), A("FA", lo, hi), False, p == 15)
-            pcopy.append(lambda: cp(A("LU", a, a + CH), A("PR", a, a + CH)))
-            for p in range(16):
-                pend.append(lambda p=p: act(I("FL", 3584, "LU", a + 8 * p, a + 8 * p + 8), A("KA"), AFT.Silu))
-        if X == 1:
-            tt(A("LS"), A("FRF"), A("FA"), OPS.add)
-            cp(A("LSU"), A("LS"))
-            if w < RO - 1:
-                pend.append(lambda: act(I("EW", 3584, "LSU", 0, 16), A("KB"), AFT.Silu))
+        if X:
+            msum(A("PR", 256, 272), [(DP(l), A("FH", l, CAP, 16)) for l in range(16)] + [(A("IDH"), A("FA"))])
 
-    def nbg(X):
-        a, nb = CH * X, I("NW", HALO + NH, "UL", 8 * X, 8 * X + 8)
-        ts(A("CL", a, a + CH), nb, 2048.0 + OFF, OPS.add)
-        act(A("CB", a, a + CH), nb, AFT.Copy, 0.0, 0.0625)
-
-    def rt(t, X):
-        a, b, r = CH * X, CH * X + CH, ("Ra", "Rb")[t]
-        tt(A(r, a, b), pc(X, 0, CH), A("CB", a, b), OPS.min)
-        act(A(("SA", "SB")[t], a, b), A(r, a, b), AFT.Copy, (-512.0, -256.0)[t])
-
-    def relay_a():
-        cp(A("Ch"), A("NAU"))
-        for h in range(2):
-            for k in range(8):
-                mm(A("PR", 32 * k + 16 * h, 32 * k + 16 * h + 16), A("Ch", 128 * h, 128 * h + 128), A("IDH", 16 * k, 16 * k + 16), True, True)
-
-    def relay_b(h0, h1):
-        for h in range(h0, h1):
-            for k in range(8):
-                mm(A("PR", 256 + h, 512, 8), A("ZM", 240 * h + 112 - 16 * k, 240 * h + 240 - 16 * k), A("Th", 32 * k, 32 * k + 32), k == 0, k == 7)
-
-    def decode(w, X):
-        a, b = CH * X, CH * X + CH
-        tt(pc(X, CH, 2 * CH), pc(X, 0, CH), A("CB", a, b), OPS.min)
-        tt(A("Rc", a, b), pc(X, CH, 2 * CH), A("Ra", a, b), OPS.max)
-        ts(A("CI", a, b), A("Rc", a, b), 16.0, OPS.mult, 2048.0, OPS.add)
-        ts(A("CJ", a, b), A("CI", a, b), 4095, OPS.bitwise_and)
+    def fails_v(w, X):
+        a = CH * X
         if w < RO - 1:
-            cp(I("F", 1792, "FRL", 8 * X, 8 * X + 8), A("CJ", a, b))
-        else:
-            ts(A("CI", a, b), A("CJ", a, b), 1.0, OPS.subtract)
-            ts(A("CJ", a, b), A("CI", a, b), 4095, OPS.bitwise_and)
-            cp(I("YW", 1792, "FRL", 8 * X, 8 * X + 8), A("CJ", a, b))
+            cp(A("LU", a, a + CH), A("PR", a, a + CH))
+            for p in range(16):
+                pend.append(lambda p=p: act(I("W", 3584, "LU", a + 8 * p, a + 8 * p + 8), A("KA", 128 * w, 128 * w + 128), AFT.Silu))
+        if X:
+            ts(A("LSU"), A("PR", 256, 272), 64.0, OPS.subtract)
+            if w < RO - 1:
+                pend.append(lambda: act(I("W", 3584, "LSU", 0, 16), A("ZF"), AFT.Silu))
 
-    def update_a():
+    def update():
+        cp(A("KY"), A("PL", 0, 16))
+        tt(A("KM"), A("PL", 16, 32), A("KY"), OPS.min)
+        tt(A("TI"), A("PL", 32, 48), A("KM"), OPS.min)
+        ts(A("TM"), A("TI"), 4095, OPS.bitwise_and)
+        ts(A("UF"), A("TM"), float(OFF), OPS.add)
         xs = A("XR", 0, 4096, 16)
-        tt(A("DX"), I("BW", 4104, "UL", 0, 16), xs, OPS.subtract)
+        tt(A("DX"), I("BW", 4104, "UF", 0, 16), xs, OPS.subtract)
         ts(A("DC"), A("DX"), -2.0, OPS.max, 2.0, OPS.min)
-        tt(I("AW", 3584, "LSU", 0, 16), A("DC"), xs, OPS.add)
+        tt(I("YA", 3584, "LSU", 0, 16), A("DC"), xs, OPS.add)
 
     def parity():
-        mm(A("PM", 64, 80), A("OH"), A("FA"), True, True)
-        op("v", A("ES"), [A("PM", 64, 80)], lambda: g.vector.tensor_reduce(out=T.ES[:], in_=T.PM[:, 64:80], axis=AxisListType.X, op=OPS.add))
-        cp(A("EI"), A("ES"))
+        msum(A("PM", 300, 301), [(A("OH"), A("FS", 0, 1)), (A("OH"), A("FS", 1, 2))])
+        cp(A("EI"), A("PM", 300, 301))
         ts(A("EO"), A("EI"), 1, OPS.bitwise_and)
         ts(A("EC"), A("EO"), -8.0, OPS.mult, C3, OPS.add)
 
+    def old_out():
+        act(A("SG", 0, VA), A("F", 0, VA), AFT.Copy, -2048.0)
+        act(A("SG", VA, 2 * VA), A("F", 0, VA), AFT.Relu, 1.0, -1.0)
+        for k, (a, b) in enumerate(((0, 512), (512, 1024), (1024, VA))):
+            o = A(("PT", "PM")[k % 2], 0, b - a)
+            msum(o, [(A("IDH"), A("SG", a, b)), (A("PB"), A("SG", VA + a, VA + b))])
+            pend.append(lambda a=a, b=b, o=o: act(A("YW", a, b), o, AFT.Copy, 2047.0))
+            if k:
+                drain(1)
+
+    def front(w):
+        xrep(1)
+        xrep(0)
+        if w < RO - 1:
+            relay_a()
+
+    def HC(X):
+        for s in range(2):
+            H(X, s)
+            count(X, s)
+
     for w in range(RO):
         last = w == RO - 1
-        act(A("F", VA, VA + 256), A("LG%d" % w))
-        if not last:
-            relay_a()
-        seeds("v", 0, 0)
-        seeds("s", 0, 1)
-        xrep(1)
-        seeds("s", 1, 0)
-        seeds("s", 1, 1)
+        idn = A("IDN") if last else A("IDH")
         if w == 0:
-            rest()
-        xrep(0)
-        slist(0)
+            act(A("F", VA, VA + 256), A("LG0"))
+        seeds(0)
+        front(w)
+        diag(0)
+        seeds(1)
         if not last:
-            act(A("Th"), A("PR", 0, 256))
-            relay_b(0, 4)
+            act(A("Th"), A("PT", 0, 256))
+        slist(0)
         if w == 0:
             op("v", (T.BW[:, 4103:4104], [("BW", 4096, 4104)], []), [], lambda: g.vector.memset(T.BW[:, 4103:4104], 1024.0))
         G(0, 0)
-        G(0, 1)
-        slist(1)
-        H(0, 0)
-        H(0, 1)
+        diag(1)
+        seeds(2)
         if not last:
-            act(I("FL", 3584, "FRL", 0, 16), A("KC"), AFT.Silu)
+            relay_b(0, 3)
+        H(0, 0)
+        slist(1)
+        G(0, 1)
+        count(0, 0)
+        diag(2)
+        seeds(3)
+        if not last:
+            relay_b(3, 5)
+        numbers(0, 0)
+        slist(2)
+        H(0, 1)
+        diag(3)
+        count(0, 1)
+        if not last:
+            relay_b(5, 8)
         if w == 0:
-            ts(A("HN"), A("NT", 0, NH), 2047.0, OPS.min, 1.0, OPS.add)
-            send(prv, HNB, A("HN"), "hn", "lhn")
-            ts(A("NW", 8, 8 + OB), A("NT"), 2047.0, OPS.subtract)
-        for slot in range(5):
-            t, X = slot // 2, slot % 2
-            nX = 1 - X
-            o1(t, X)
-            if slot == 0 and not last:
-                relay_b(4, 8)
-                act(A("LP"), A("PR", 256, 512))
-            G(nX, 0, CH)
-            if pcopy:
-                pcopy.pop(0)()
-            if slot > 0:
-                drain((8, 9, 9, 99)[slot - 1])
-            o5(t, X)
-            H(nX, 0, CH)
-            tiny(t, X)
-            if t < 2:
-                rt(t, X)
-                nbg(X)
-            if t == 0:
-                fails(w, X)
-        o1(2, 1)
-        tt(A("Ra"), A("SA"), A("SB"), OPS.max)
-        decode(w, 0)
+            halo_out(0)
+            halo_out(1)
+            late_loads()
+            ts(A("IDN"), A("IDM"), -1.0, OPS.mult)
+        sign(0, 0)
+        fails_p(0)
+        rank_p(0, 0)
+        fails_s(w, 0)
+        if not last:
+            act(A("FR", 1, CAP + 1), A("PAD"))
+        G(1, 0)
+        slist(3)
+        choose(0, 0)
+        fails_v(w, 0)
+        if last:
+            old_out()
+        else:
+            state(w)
+        drain(DRAIN["a"])
+        G(1, 1)
+        numbers(0, 1)
+        if w == 0:
+            halo_in(0)
+            halo_in(1)
+        nbg(0, 0)
+        HC(1)
+        numbers(1, 0)
+        sign(0, 1)
+        fails_p(1)
+        rank_p(0, 1)
+        drain(DRAIN["b"])
+        fails_s(w, 1)
+        G(0, 0, CH)
+        choose(0, 1)
+        fails_v(w, 1)
+        HC(0)
+        nbg(0, 1)
+        numbers(1, 1)
+        for X in range(2):
+            G(1 - X, 0)
+            sign(1, X)
+            rank_p(1, X)
+            keep_a(X, idn)
+            drain(DRAIN["cd"[X]])
+            relu(1, X)
+            G(1 - X, 1)
+            choose(1, X)
+            HC(1 - X)
+            keep_b(X)
+            nbg(1, X)
+            numbers(2, X)
+        drain(99)
         if not last:
             extract(w + 1)
-        decode(w, 1)
+        G(1, 0)
+        sign(2, 0)
+        keep_c(0, idn)
+        rank_p(2, 0)
+        G(1, 1)
+        relu(2, 0)
+        if not last:
+            select_a(w + 1)
+        H(1, 0)
+        count(1, 0)
+        if not last:
+            select_a2()
+            select_s()
+        H(1, 1)
+        count(1, 1)
+        store(w, 0)
+        sign(2, 1)
+        keep_c(1, idn)
+        rank_p(2, 1)
+        choose(2, 0)
+        relu(2, 1)
+        store(w, 1)
         if not last:
             ghosts_out(w + 1)
-            select_a()
         else:
             dma("y", T.yf[:], T.YW[:, 0:VA], [("YW", 0, VA)], [], "oy")
-        o5(2, 1)
+        choose(2, 1)
         if not last:
             parity()
-        tiny(2, 1)
-        update_a()
+        update()
         if last:
-            dma("y", T.ya[:], T.AW[:, 0:VA], [("AW", 0, VA)], [], "oa")
+            dma("y", T.ya[:], T.YA[:, 0:VA], [("YA", 0, VA)], [], "oa")
         else:
-            if w == RO - 2:
-                ts(A("YT"), A("F", 0, VA), 1.0, OPS.subtract)
-                ts(A("YT"), A("YT"), 4095, OPS.bitwise_and)
-                cp(A("YW", 0, VA), A("YT"))
-            select_b()
+            select_p()
+            cp(A("F", VA, VA + 256), A("LG%d" % (w + 1)))
+            select_b(w + 1)
 
     need("y", "oy", 16)
     need("y", "oa", 16)
     for w in range(RO):
         need("g", "lg%d" % w, 16)
-    need("g", "lhb", 16)
-    need("g", "lhn", 16)
+    for s in ("lhb", "lhn0", "lhn1"):
+        need("g", s, 16)
     for s in ("cv", "cs", "cp", "cg"):
         need("y", s, cnt[s])

@@ -11,12 +11,14 @@ C3 = C4 + 8.0
 WZ, THR = 16384.0, 18432.0
 
 DTS = {"b": "bfloat16", "f": "float32", "h": "float16", "i": "int32", "u": "uint16"}
-BUFS = """AW1792b YA3584b BW4104b NW4104i HS2048u HR2048u NA1792i F1792f FI272i BDI16i BDU16u IND320h W3584f FR3768f
-IDT1280f PAD256f DD80f WC80f EL80h CU80h MX80f OU80u INF80h SU480h KT400h ZF256f LP256h FH256h FRL16u NAU256u Ch256h Th256h
-LU256u SG4096h CB768h CL256u XR4096b D4096h NE4096h VV768h SC256h AB512f KY16f KM16f TI16i TM16i UL16u UF16u FA16h FS2f
-LSU16u EI1i EO1i EC1f DX256b DC256b GS256h YW1792f IP1i LPI1i GPI1i PCF1f LPC1f GPC1f QE1f CF1f CB1f
-LM128h CM128f XG144f XH144h EP144h EQ144h SAM128h IDM128f IDH128h IDN128h IDL128h TRI128h LTM128h WK128h TF128h TL128h PA128h PB128h
-PN128h ONE128h KC128h OH128f ZM1920h ZO1920h DPM2048h KA640f""".replace("CB1f", "CG1f")
+BUFS = """AW1792b YA3584b BW4104b NW4104i HS2048u HR2048u NA1792i F1792f FI272i BDI16i BDU16u IND320h W14336f WB3584f
+IDT1280f PAD256f DD80f WC320f WD80f EL80h CU80h MX80f OU80u INF80h SU80h KT400h ZF320f LP256h FH256h FRL16u NAU256u Ch256h
+Th256h LU256u SG4096h CB768h CL256u XR4096b D4096h VV768h SC256h AB512f KY16f KM16f TI16i TM16i UL16u UF16u FA16h
+LSU32u YF3584f XN256f XS256b IDB128b IDC128b EI1i EO1i EC1f DX256b DC256b GS256h YW1792f IP1i LPI1i GPI1i PCF1f LPC1f GPC1f QE1f CF1f CG1f
+LM128h CM128f XG144f XH144h EP144h EQ144h SAM128h IDM128f IDX128f IDH128h IDN128h IDL128h TRI128h LTM128h WK128h TF128h TL128h
+PA128h PB128h PN128h PG128h PH128h P4128h ONE128h KC128h CO128h OH128h ZM1920h XL240h HE8f DPM2048h KA2560f KB256f""".replace("P4", "PF")
+FR, FV, FW = 5120, 8896, 3768
+STAMP = [32.0 * 5 ** w for w in range(RO - 1)]
 SCRATCH = {}
 for _b in BUFS.split():
     _n = _b.rstrip("bfhiu").rstrip("0123456789")
@@ -26,12 +28,15 @@ for _w in range(RO):
 PS = ("PC0", "PC1", "PQ0", "PQ1", "PL", "PR", "PM", "PT")
 for _n in PS:
     SCRATCH[_n] = ("psum", [128, 512], "float32")
-LOADS = ["f0", "bd", "xb", "nba", "xa", "nb0", "nb1", "nba2", "xa2", "ya"]
-SEMAPHORES = (["cv", "cs", "cp", "cg", "hb", "hn0", "hn1", "lhb", "lhn0", "lhn1", "oy", "oa"] + ["ld_" + n for n in LOADS]
-              + [k + str(w) for k in ("gh", "lg", "xf") for w in range(RO)])
+LOADS = ["f0", "bd", "xb0", "xb1", "nba", "xa", "nb0", "nb1", "nba2", "xa2"]
+SEMAPHORES = (["cv", "cs", "cp", "cg", "hb0", "hb1", "hn0", "hn1", "lhb0", "lhb1", "lhn0", "lhn1", "oy", "oa"] + ["ld_" + n for n in LOADS]
+              + ["zw", "zb"] + [k + str(w) for k in ("gh", "lg", "xf", "xd") for w in range(RO)])
 
-VVE, KE = "ssvvvv", "..ssvv"
-DRAIN = {"a": 7, "b": 2, "c": 9, "d": 8}
+VVE, KE = "svvvsv", "..sssv"
+DRAIN = 3
+VSEED = 24
+VFR = 26
+FORCE = False
 
 
 def rank_program(g, core, T, topo):
@@ -89,8 +94,8 @@ def rank_program(g, core, T, topo):
         ap = T[name][:, lo:hi] if st == 1 else T[name][:, lo:hi:st]
         return (ap, [(name, lo, hi)], [])
 
-    def I(win, w, off, o0, o1):
-        return (T[win][:, 0:w].indirect(T[off][:, o0:o1]), [(win, 0, w)], [(off, o0, o1)])
+    def I(win, w, off, o0, o1, a=0):
+        return (T[win][:, a:a + w].indirect(T[off][:, o0:o1]), [(win, a, a + w)], [(off, o0, o1)])
 
     def op(q, out, ins, call, outs=()):
         reads, writes = list(out[2]), list(out[1])
@@ -100,6 +105,8 @@ def rank_program(g, core, T, topo):
             writes += x[1]
         deps(q, reads, writes)
         sem = CS[q]
+        if FORCE and q == "v" and cnt[sem]:
+            need(q, sem, cnt[sem])
         cnt[sem] += 1
         call().then_inc(T.sem[sem], 1)
         note(q, reads, writes, sem, cnt[sem])
@@ -171,14 +178,15 @@ def rank_program(g, core, T, topo):
     def DP(p):
         return A("DPM", 128 * p, 128 * p + 128)
 
+    load("y", "BW", 8, 8 + 1024, T.xb, 0, "xb0")
     load("s", "FI", 0, S, T.f0, 0, "f0")
-    load("y", "BDI", 0, 16, T.bd, 0, "bd")
-    load("y", "BW", 8, 8 + OB, T.xb, 0, "xb")
+    load("s", "BDI", 0, 16, T.bd, 0, "bd")
+    load("y", "BW", 8 + 1024, 8 + OB, T.xb, 1024, "xb1")
     load("s", "NA", 0, FIRST, T.nba, 0, "nba")
     load("s", "AW", 0, FIRST, T.xa, 0, "xa")
-    HB = A("BW", HALO, HALO + NH)
-    arrive(nxt, HB, "hb")
+    HB = [A("BW", HALO, HALO + 1024), A("BW", HALO + 1024, HALO + NH)]
     for h in range(2):
+        arrive(nxt, HB[h], "hb%d" % h)
         arrive(nxt, A("HR", 1024 * h, 1024 * h + 1024), "hn%d" % h)
     for w in range(RO):
         arrive(prv, A("LG%d" % w), "gh%d" % w)
@@ -205,61 +213,79 @@ def rank_program(g, core, T, topo):
     ts(A("QE"), A("LPI"), 80.0, OPS.mult)
     ts(A("IDM"), A("CM"), A("PCF"), OPS.is_equal)
     ts(A("DD"), A("DD"), A("QE"), OPS.add)
-    ts(A("PN"), A("IDM"), -2048.0, OPS.mult)
+    ts(A("PH"), A("IDM"), -32768.0, OPS.mult)
     ts(A("XH", 0, 128), A("CM"), A("GPC"), OPS.subtract)
     ts(A("WK"), A("XH", 0, 128), A("LPC"), OPS.is_ge)
     ts(A("SAM"), A("XH", 0, 128), 15.5, OPS.is_lt)
     tt(A("TRI"), A("WK"), A("SAM"), OPS.mult)
     ts(A("EL"), A("PM", 160, 240), 0.5, OPS.is_lt)
-    ts(A("SU", 0, 80), A("PM", 160, 240), 0.5, OPS.is_gt)
+    ts(A("SU"), A("PM", 160, 240), 0.5, OPS.is_gt, 64.0, OPS.mult)
+    for w in range(RO - 1):
+        act(A("KA", 512 * w, 512 * w + 512), A("F", 512, 1024), AFT.Copy, STAMP[w])
+        act(A("KT", 80 * w, 80 * w + 80), A("ZF", 0, 80), AFT.Copy, -0.875 * STAMP[w])
+    act(A("KB"), A("ZF", 0, CAP), AFT.Copy, 131072.0)
 
     def ghosts_out(w):
         ts(A("GS"), I("F", VA, "BDU", 0, 16), -2048.0, OPS.add, 0.0, OPS.max)
         send(nxt, A("LG%d" % w), A("GS"), "gh%d" % w, "lg%d" % w)
 
     def extract(w):
-        dma("y", T.WC[:], T.W[0:128:16, 0:VA], [("W", 0, VA)], [("WC", 0, 80)], "xf%d" % w)
+        dma("y", T.WC[:], T.W[0:128:16, 0:4 * VA], [("W", 0, 4 * VA)], [("WC", 0, 320)], "xf%d" % w)
+
+    def extract_b(w):
+        dma("y", T.WD[:], T.WB[0:128:16, 0:VA], [("WB", 0, VA)], [("WD", 0, 80)], "xd%d" % w)
 
     BASE = A("PM", 256, 257)
 
-    def select_a(w):
-        if w:
-            tt(A("EL"), A("WC"), A("PM", 160, 240), OPS.is_gt)
+    def select_z(w):
+        msum(A("PM", 160, 240), [(A("IDH"), A("KT", 80 * w - 80, 80 * w)), (A("PG"), A("EL")), (A("PH"), A("INF")), (A("PN"), A("SU")),
+                                 (A("IDX"), A("WD"))] + [(A("IDM"), A("WC", r, 320, 4)) for r in range(4)])
+
+    def select_1():
+        ts(A("EL"), A("PM", 160, 240), 0.0, OPS.is_gt)
+
+    def select_2():
         op("v", A("CU"), [A("EL"), A("ZF", 0, 80)], lambda: g.vector.tensor_tensor_scan(
             out=T.CU[:], data0=T.EL[:], data1=T.ZF[:, 0:80], initial=0.0, op0=OPS.add, op1=OPS.add))
-        msum(A("PM", 0, 80), [(A("IDM"), A("DD")), (A("PN"), A("EL")), (A("PN"), A("EL"))])
+        msum(A("PM", 0, 80), [(A("IDM"), A("DD")), (A("PH"), A("EL"))])
         mm(BASE, A("TRI"), A("CU", 79, 80), True, True)
 
-    def select_a2():
+    def select_3():
         tt(A("MX"), A("PM", 0, 80), A("CU"), OPS.max)
+
+    def select_4():
         ts(A("OU"), A("MX"), BASE, OPS.add)
 
+    def pads():
+        act(A("W", FR + 1, FR + CAP + 1), A("PAD"))
+        act(A("W", FV + 1, FV + CAP + 1), A("KB"))
+
     def select_s():
-        act(I("FR", 3768, "OU", 0, 80), A("IDT"), AFT.Silu)
-        act(A("FH"), A("FR", 1, CAP + 1))
+        act(I("W", FW, "OU", VFR, 80, FR), A("IDT", 16 * VFR, VA), AFT.Silu)
+
+    def select_v():
+        cp(I("W", FW, "OU", 0, VFR, FV), A("IDT", 0, 16 * VFR))
 
     def select_p():
+        tt(A("FH"), A("W", FR + 1, FR + CAP + 1), A("W", FV + 1, FV + CAP + 1), OPS.min)
         for l in range(16):
             mm(A("PM", 272, 288), DP(l), A("FH", l, CAP, 16), l == 0, l == 15)
 
     def select_b(w):
-        n = 1792 if w else FIRST
         ts(A("FRL"), A("PM", 272, 288), 64.0, OPS.subtract)
-        cp(A("NAU"), I("NA", n, "FRL", 0, 16))
-        cp(A("XR", 0, 4096, 16), I("AW", n, "FRL", 0, 16))
+        act(A("XR", 0, 4096, 16), I("AW", 1792 if w else FIRST, "FRL", 0, 16))
 
-    def state(w):
+    def select_n(w):
+        cp(A("NAU"), I("NA", 1792 if w else FIRST, "FRL", 0, 16))
+
+    def state():
         ts(A("INF"), A("MX"), BASE, OPS.add, CAP + 0.5, OPS.is_lt)
-        if w:
-            ts(A("SU", 80 * w, 80 * w + 80), A("WC"), 8.0, OPS.is_lt)
-        msum(A("PM", 160, 240), [(A("IDH"), A("KT", 80 * w, 80 * w + 80)), (A("PN"), A("EL")), (A("PA"), A("INF"))]
-             + [(A("PA"), A("SU", 80 * k, 80 * k + 80)) for k in range(w + 1)])
 
-    def xrep(X):
-        a, b = 16 * CH * X, 16 * CH * X + 16 * CH
-        for k, n in ((8, 128), (4, 256), (2, 512), (1, 1024)):
-            if X:
-                gsel(A("XR", a + k, b, 2 * k), A("XR", a, b, 2 * k), [[0, n]], 0, 0)
+    def xrep(q, s, ks=(8, 4, 2, 1)):
+        a, b = 16 * SUB * s, 16 * SUB * s + 16 * SUB
+        for k in ks:
+            if q == "g":
+                gsel(A("XR", a + k, b, 2 * k), A("XR", a, b, 2 * k), [[0, 8 * SUB // k]], 0, 0)
             else:
                 cp(A("XR", a + k, b, 2 * k), A("XR", a, b, 2 * k))
 
@@ -276,29 +302,33 @@ def rank_program(g, core, T, topo):
         if h1 == 8:
             act(A("LP"), A("PR", 0, 256))
 
-    act(A("FR", 1, CAP + 1), A("PAD"))
-    select_a(0)
-    select_a2()
-    cp(A("BDU"), A("BDI"))
+    pads()
+    select_2()
     ts(A("FI"), A("FI"), 1.0, OPS.add)
+    select_3()
     ts(A("FI"), A("FI"), 4095, OPS.bitwise_and)
+    select_4()
     cp(A("F", 0, S), A("FI"))
-    send(prv, HB, A("BW", 8, 8 + NH), "hb", "lhb")
+    cp(A("BDU"), A("BDI"))
+    select_s()
+    select_v()
+    send(prv, HB[0], A("BW", 8, 8 + 1024), "hb0", "lhb0")
     ghosts_out(0)
-    need("y", "lhb", len(topo.engines(core, prv)))
+    send(prv, HB[1], A("BW", 8 + 1024, 8 + NH), "hb1", "lhb1")
+    need("y", "lhb0", len(topo.engines(core, prv)))
     for h in range(2):
         load("y", "NW", 8 + 1024 * h, 8 + 1024 * h + 1024, T.nbb, 1024 * h, "nb%d" % h)
     ts(A("IDL"), A("IDM"), A("LPC"), OPS.mult)
     for p in range(16):
         ts(DP(p), A("IDL"), float(p + 1), OPS.is_equal)
-    select_s()
-    select_p()
-    io(A("KT"), [[16, 5], [0, 80]], 24)
-    io(A("KA"), [[16, 5], [0, 128]], 32)
-    io(A("ZO"), [[0, 1920]], 1)
-    gsel(A("ZM"), A("ZO"), [[-16, 8], [256, 15], [-1, 16]], -7 * 256, 1)
+    io(A("XL"), [[1, 240]], -111)
+    io(A("HE"), [[16, 8]], 0)
+    io(A("CO"), [[0, 4], [1, 4], [0, 8]], 0)
     io(A("NA", 1536, 1792), [[1, CAP]], 1536, 0, False)
     cp(A("IDH"), A("IDM"))
+    state()
+    for name, c in (("PN", -2048.0), ("PG", 32768.0), ("PF", 4.0), ("IDX", -1.0), ("IDN", -1.0), ("IDB", 1.0), ("IDC", -1.0)):
+        ts(A(name), A("IDM"), c, OPS.mult)
     ts(A("EQ"), A("EP"), 2.0, OPS.mult)
     ms(A("KC"), -27.0)
     ms(A("EC"), C3)
@@ -315,15 +345,20 @@ def rank_program(g, core, T, topo):
     ts(A("CG"), A("LPC"), -WZ, OPS.mult, 17 * WZ, OPS.add)
     ms(A("OH"), 1.0 / 256.0)
     ms(A("NW", 0, 8), 4095)
-    ms(A("W", 0, VA), 16.0)
-    ms(A("AW", VA, 1792), 0.0)
+    select_p()
+    ts(A("HE"), A("HE"), A("GPC"), OPS.not_equal, 1000.0, OPS.mult)
+    ms(A("AW", 1536, 1792), 0.0)
+    ts(A("HE"), A("HE"), A("LPC"), OPS.add)
     select_b(0)
+    for h in range(8):
+        ts(A("ZM", 240 * h, 240 * h + 240), A("XL"), A("HE", h, h + 1), OPS.is_equal)
 
     def late_loads():
+        dma("y", T.W[0:128:16, 0:4 * VA], T.ZF[:], [("ZF", 0, 320)], [("W", 0, 4 * VA)], "zw")
+        dma("y", T.WB[0:128:16, 0:VA], T.ZF[0:32, :], [("ZF", 0, 320)], [("WB", 0, VA)], "zb")
         need("y", "lhn1", len(topo.engines(core, prv)))
         load("y", "NA", FIRST, VA, T.nba, FIRST, "nba2")
         load("y", "AW", FIRST, VA, T.xa, FIRST, "xa2")
-        load("y", "YA", 0, VA, T.xa, 0, "ya")
 
     def halo_out(h):
         a = 1024 * h
@@ -334,7 +369,7 @@ def rank_program(g, core, T, topo):
 
     def halo_in(h):
         a = 1024 * h
-        cp(A("NW", HALO + a, HALO + a + 1024), A("HR", a, a + 1024))
+        act(A("NW", HALO + a, HALO + a + 1024), A("HR", a, a + 1024))
 
     def cb(t, X):
         return A("CB", 256 * t + CH * X, 256 * t + CH * X + CH)
@@ -350,7 +385,10 @@ def rank_program(g, core, T, topo):
 
     def seeds(s):
         a = SUB * s
-        act(A("SG", 16 * a, 16 * a + 1024), I("F", 1792, "NAU", a, a + SUB), AFT.Copy, -2048.0)
+        if s == 0 and VSEED:
+            ts(A("SG", 0, 16 * VSEED), I("F", 1792, "NAU", 0, VSEED), -2048.0, OPS.add)
+            a = VSEED
+        act(A("SG", 16 * a, 16 * SUB * (s + 1)), I("F", 1792, "NAU", a, SUB * (s + 1)), AFT.Copy, -2048.0)
 
     def diag(s):
         a = SUB * s
@@ -363,17 +401,17 @@ def rank_program(g, core, T, topo):
     def numbers(t, X):
         ts(cb(t, X), A("CL", CH * X, CH * X + CH), -2048.0 - OFF, OPS.add)
 
-    def G(X, s, n=SUB):
-        a = 16 * (CH * X + SUB * s)
-        tt(A("D", a, a + 16 * n), I("BW", 4104, "CL", a // 16, a // 16 + n), A("XR", a, a + 16 * n), OPS.subtract)
+    def G(X, lo, hi):
+        a, b = CH * X + lo, CH * X + hi
+        tt(A("D", 16 * a, 16 * b), I("BW", 4104, "CL", a, b), A("XR", 16 * a, 16 * b), OPS.subtract)
 
     def H(X, s, n=SUB):
         a = 16 * (CH * X + SUB * s)
-        ts(A("NE", a, a + 16 * n), A("D", a, a + 16 * n), A("EC"), OPS.add, A("EC"), OPS.is_equal)
+        ts(A("D", a, a + 16 * n), A("D", a, a + 16 * n), A("EC"), OPS.add, A("EC"), OPS.is_equal)
 
     def count(X, s, n=SUB):
         a, o = 16 * (CH * X + SUB * s), A("PC%d" % X, SUB * s, SUB * s + n)
-        msum(o, [(A("IDH"), A("KC", 0, n))] + [(EP(p, "EQ"), A("NE", a + p, a + 16 * n, 16)) for p in range(16)])
+        msum(o, [(A("IDH"), A("KC", 0, n))] + [(EP(p, "EQ"), A("D", a + p, a + 16 * n, 16)) for p in range(16)])
 
     def sign(t, X):
         if VVE[2 * t + X] == "s":
@@ -390,9 +428,12 @@ def rank_program(g, core, T, topo):
         msum(A("PL", 16 * t + 8 * X, 16 * t + 8 * X + 8), [(A("PB"), A("ONE", 0, 8))] * (2 - t)
              + [(EP(l), A("SC", a + l, a + CH, 16)) for l in range(16)])
 
-    def nbg(t, X):
+    def blist(t, X):
         lo = 8 * X
         ts(A("UL", lo, lo + 8), A("PL", 16 * t + lo, 16 * t + lo + 8), 2048.0 + OFF - 15 * THR - 4096.0 * (2 - t), OPS.add, 4103.0, OPS.min)
+
+    def nbg(X):
+        lo = 8 * X
         ts(A("CL", CH * X, CH * X + CH), I("NW", 4104, "UL", lo, lo + 8), 8.0, OPS.add)
 
     def relu(t, X):
@@ -434,41 +475,66 @@ def rank_program(g, core, T, topo):
 
     def fails_s(w, X):
         lo, hi, a = 8 * X, 8 * X + 8, CH * X
-        act(A("FA", lo, hi), A("PL", 48 + lo, 48 + hi), AFT.Relu, -896.0 * 14, -896.0, A("FS", X, X + 1))
-        if w < RO - 1:
-            mm(A("PR", a, a + CH), A("IDH"), A("LP", a, a + CH), True, False)
-            for p in range(16):
-                mm(A("PR", a + 8 * p, a + 8 * p + 8), A("IDH"), A("FA", lo, hi), False, p == 15)
         if X:
-            msum(A("PR", 256, 272), [(DP(l), A("FH", l, CAP, 16)) for l in range(16)] + [(A("IDH"), A("FA"))])
+            ts(A("FA", lo, hi), A("PL", 48 + lo, 48 + hi), -15.0, OPS.is_lt, 1792.0, OPS.mult)
+        else:
+            act(A("FA", lo, hi), A("PL", 48 + lo, 48 + hi), AFT.Relu, -896.0 * 14, -896.0)
+        if w < RO - 1:
+            msum(A("PR", a, a + CH), [(A("PF"), A("LP", a, a + CH)), (A("IDH"), A("CO"))], True, False)
+            for p in range(16):
+                mm(A("PR", a + 8 * p, a + 8 * p + 8), A("PF"), A("FA", lo, hi), False, p == 15)
+        if X:
+            msum(A("PT", 256, 272), [(DP(l), A("FH", l, CAP, 16)) for l in range(16)] + [(A("IDH"), A("FA"))])
 
-    def fails_v(w, X):
+    def fails_l(w, X):
         a = CH * X
         if w < RO - 1:
-            cp(A("LU", a, a + CH), A("PR", a, a + CH))
-            for p in range(16):
-                pend.append(lambda p=p: act(I("W", 3584, "LU", a + 8 * p, a + 8 * p + 8), A("KA", 128 * w, 128 * w + 128), AFT.Silu))
-        if X:
-            ts(A("LSU"), A("PR", 256, 272), 64.0, OPS.subtract)
-            if w < RO - 1:
-                pend.append(lambda: act(I("W", 3584, "LSU", 0, 16), A("ZF"), AFT.Silu))
+            act(A("LU", a, a + CH), A("PR", a, a + CH))
+            for m in range(4):
+                pend.append(lambda m=m: act(I("W", 14336, "LU", a + 32 * m, a + 32 * m + 32), A("KA", 512 * w, 512 * w + 512), AFT.Silu))
 
-    def update():
-        cp(A("KY"), A("PL", 0, 16))
-        tt(A("KM"), A("PL", 16, 32), A("KY"), OPS.min)
-        tt(A("TI"), A("PL", 32, 48), A("KM"), OPS.min)
-        ts(A("TM"), A("TI"), 4095, OPS.bitwise_and)
-        ts(A("UF"), A("TM"), float(OFF), OPS.add)
-        xs = A("XR", 0, 4096, 16)
-        tt(A("DX"), I("BW", 4104, "UF", 0, 16), xs, OPS.subtract)
-        ts(A("DC"), A("DX"), -2.0, OPS.max, 2.0, OPS.min)
-        tt(I("YA", 3584, "LSU", 0, 16), A("DC"), xs, OPS.add)
+    def fails_b(w):
+        a = 16 * (w % 2)
+        act(A("LSU", a, a + 16), A("PT", 256, 272), AFT.Copy, -64.0)
+        if w < RO - 1:
+            drain(1)
+            act(I("WB", 3584, "LSU", a, a + 16), A("KB"), AFT.Silu)
+            extract_b(w + 1)
 
-    def parity():
-        msum(A("PM", 300, 301), [(A("OH"), A("FS", 0, 1)), (A("OH"), A("FS", 1, 2))])
-        cp(A("EI"), A("PM", 300, 301))
-        ts(A("EO"), A("EI"), 1, OPS.bitwise_and)
-        ts(A("EC"), A("EO"), -8.0, OPS.mult, C3, OPS.add)
+    xs = A("XR", 0, 4096, 16)
+    update = [lambda: tt(A("TI"), A("PL", 32, 48), A("KM"), OPS.min),
+              lambda: ts(A("TM"), A("TI"), 4095, OPS.bitwise_and),
+              lambda: ts(A("UF"), A("TM"), float(OFF), OPS.add),
+              lambda: tt(A("DX"), I("BW", 4104, "UF", 0, 16), xs, OPS.subtract),
+              lambda: ts(A("DC"), A("DX"), -2.0, OPS.max, 2.0, OPS.min),
+              lambda: tt(I("YA", 3584, "LSU", 16, 32), A("DC"), xs, OPS.add)]
+
+    def move_a():
+        act(A("XS"), xs)
+        act(A("DX"), I("BW", 4104, "UF", 0, 16))
+        msum(pq(0, 1, 2), [(A("IDB"), A("DX")), (A("IDC"), A("XS"))])
+
+    def move_b():
+        act(A("DX"), pq(0, 1, 2), AFT.Relu, 2.0)
+        act(A("DC"), pq(0, 1, 2), AFT.Relu, -2.0)
+
+    def move_c():
+        msum(A("PT", 0, CAP), [(A("IDB"), A("DX")), (A("IDC"), A("DC")), (A("IDB"), A("XS"))])
+        act(A("XN"), A("PT", 0, CAP), AFT.Copy, 254.0)
+
+    def move_d(w):
+        act(I("YF", 3584, "LSU", 16 * (w % 2), 16 * (w % 2) + 16), A("XN"), AFT.Silu)
+
+    def moved_out():
+        act(A("YF", 0, VA), A("YF", 0, VA), AFT.Copy, 1.5 * 2.0 ** 23 - 256.0)
+        act(A("YA", 0, VA), A("YF", 0, VA), AFT.Copy, -1.5 * 2.0 ** 23)
+
+    def parity_p():
+        msum(A("PM", 300, 301), [(A("OH"), A("FA", k, k + 1)) for k in range(16)])
+
+    parity = [lambda: cp(A("EI"), A("PM", 300, 301)),
+              lambda: ts(A("EO"), A("EI"), 1, OPS.bitwise_and),
+              lambda: ts(A("EC"), A("EO"), -8.0, OPS.mult, C3, OPS.add)]
 
     def old_out():
         act(A("SG", 0, VA), A("F", 0, VA), AFT.Copy, -2048.0)
@@ -480,148 +546,163 @@ def rank_program(g, core, T, topo):
             if k:
                 drain(1)
 
-    def front(w):
-        xrep(1)
-        xrep(0)
-        if w < RO - 1:
-            relay_a()
-
-    def HC(X):
-        for s in range(2):
-            H(X, s)
-            count(X, s)
+    def HC(X, s):
+        H(X, s)
+        count(X, s)
 
     for w in range(RO):
         last = w == RO - 1
+        more = (lambda f, *a: None) if last else (lambda f, *a: f(*a))
         idn = A("IDN") if last else A("IDH")
         if w == 0:
             act(A("F", VA, VA + 256), A("LG0"))
+        select_n(w)
+        xrep("v", 0, (8,))
+        xrep("g", 1)
+        xrep("g", 2)
         seeds(0)
-        front(w)
         diag(0)
+        xrep("v", 0, (4,))
+        more(relay_a)
+        xrep("v", 0, (2,))
+        xrep("v", 3, (8,))
+        xrep("v", 0, (1,))
         seeds(1)
-        if not last:
-            act(A("Th"), A("PT", 0, 256))
+        more(act, A("Th"), A("PT", 0, 256))
         slist(0)
+        xrep("v", 3, (4,))
         if w == 0:
             op("v", (T.BW[:, 4103:4104], [("BW", 4096, 4104)], []), [], lambda: g.vector.memset(T.BW[:, 4103:4104], 1024.0))
-        G(0, 0)
+        G(0, 0, 64)
         diag(1)
         seeds(2)
-        if not last:
-            relay_b(0, 3)
-        H(0, 0)
+        more(relay_b, 0, 2)
+        xrep("v", 3, (2,))
         slist(1)
-        G(0, 1)
-        count(0, 0)
+        HC(0, 0)
+        G(0, 64, 128)
+        more(relay_b, 2, 4)
         diag(2)
         seeds(3)
-        if not last:
-            relay_b(3, 5)
+        if w:
+            move_b()
+        more(relay_b, 4, 8)
         numbers(0, 0)
+        xrep("v", 3, (1,))
         slist(2)
-        H(0, 1)
+        HC(0, 1)
         diag(3)
-        count(0, 1)
-        if not last:
-            relay_b(5, 8)
         if w == 0:
             halo_out(0)
             halo_out(1)
             late_loads()
-            ts(A("IDN"), A("IDM"), -1.0, OPS.mult)
-        sign(0, 0)
-        fails_p(0)
-        rank_p(0, 0)
-        fails_s(w, 0)
-        if not last:
-            act(A("FR", 1, CAP + 1), A("PAD"))
-        G(1, 0)
-        slist(3)
-        choose(0, 0)
-        fails_v(w, 0)
-        if last:
-            old_out()
-        else:
-            state(w)
-        drain(DRAIN["a"])
-        G(1, 1)
-        numbers(0, 1)
-        if w == 0:
-            halo_in(0)
-            halo_in(1)
-        nbg(0, 0)
-        HC(1)
-        numbers(1, 0)
-        sign(0, 1)
-        fails_p(1)
-        rank_p(0, 1)
-        drain(DRAIN["b"])
-        fails_s(w, 1)
-        G(0, 0, CH)
-        choose(0, 1)
-        fails_v(w, 1)
-        HC(0)
-        nbg(0, 1)
-        numbers(1, 1)
-        for X in range(2):
-            G(1 - X, 0)
-            sign(1, X)
-            rank_p(1, X)
-            keep_a(X, idn)
-            drain(DRAIN["cd"[X]])
-            relu(1, X)
-            G(1 - X, 1)
-            choose(1, X)
-            HC(1 - X)
-            keep_b(X)
-            nbg(1, X)
-            numbers(2, X)
+        for slot in range(4):
+            t, X = slot // 2, slot % 2
+            if slot == 0:
+                sign(0, 0)
+                fails_p(0)
+                rank_p(0, 0)
+                fails_s(w, 0)
+                fails_l(w, 0)
+                if last:
+                    move_c()
+                    move_d(w - 1)
+                    old_out()
+                    drain(9)
+                    moved_out()
+                if w == 0:
+                    drain(1)
+                    halo_in(0)
+                    halo_in(1)
+            G(1 - X, 0, 48)
+            if slot == 0:
+                slist(3)
+            else:
+                sign(t, X)
+                if slot == 1:
+                    fails_p(1)
+                rank_p(t, X)
+            G(1 - X, 48, 80)
+            if slot == 0:
+                numbers(0, 1)
+            if slot == 1:
+                fails_s(w, 1)
+            choose(t, X)
+            if slot == 1:
+                drain(4)
+                fails_l(w, 1)
+                fails_b(w)
+            if t:
+                keep_a(X, idn)
+            G(1 - X, 80, 128)
+            blist(t, X)
+            HC(1 - X, 0)
+            nbg(X)
+            HC(1 - X, 1)
+            if slot == 2:
+                more(parity_p)
+            numbers(t + 1, X)
         drain(99)
-        if not last:
-            extract(w + 1)
-        G(1, 0)
+        more(extract, w + 1)
+        relu(1, 0)
+        keep_b(0)
         sign(2, 0)
         keep_c(0, idn)
         rank_p(2, 0)
-        G(1, 1)
+        relu(1, 1)
+        keep_b(1)
         relu(2, 0)
-        if not last:
-            select_a(w + 1)
-        H(1, 0)
-        count(1, 0)
-        if not last:
-            select_a2()
-            select_s()
-        H(1, 1)
-        count(1, 1)
+        act(A("KY"), A("PL", 0, 16))
+        more(pads)
+        if w == 0:
+            act(A("YF", 0, VA), A("AW", 0, VA), AFT.Copy, 256.0)
+        elif not last:
+            move_c()
+            move_d(w - 1)
+        G(1, 0, 64)
+        more(parity[0])
+        G(1, 64, 128)
+        more(parity[1])
+        more(select_z, w + 1)
+        HC(1, 0)
+        HC(1, 1)
+        more(select_1)
+        tt(A("KM"), A("PL", 16, 32), A("KY"), OPS.min)
+        more(parity[2])
+        more(select_2)
         store(w, 0)
         sign(2, 1)
         keep_c(1, idn)
         rank_p(2, 1)
+        more(select_3)
         choose(2, 0)
+        more(select_4)
+        more(select_s)
         relu(2, 1)
-        store(w, 1)
-        if not last:
-            ghosts_out(w + 1)
-        else:
-            dma("y", T.yf[:], T.YW[:, 0:VA], [("YW", 0, VA)], [], "oy")
         choose(2, 1)
-        if not last:
-            parity()
-        update()
+        store(w, 1)
+        more(state)
         if last:
+            dma("y", T.yf[:], T.YW[:, 0:VA], [("YW", 0, VA)], [], "oy")
+            for f in update:
+                f()
             dma("y", T.ya[:], T.YA[:, 0:VA], [("YA", 0, VA)], [], "oa")
         else:
+            ghosts_out(w + 1)
+            update[0]()
+            select_v()
+            update[1]()
             select_p()
-            cp(A("F", VA, VA + 256), A("LG%d" % (w + 1)))
+            update[2]()
+            move_a()
+            act(A("F", VA, VA + 256), A("LG%d" % (w + 1)))
             select_b(w + 1)
 
     need("y", "oy", 16)
     need("y", "oa", 16)
     for w in range(RO):
         need("g", "lg%d" % w, 16)
-    for s in ("lhb", "lhn0", "lhn1"):
+    for s in ("lhb0", "lhb1", "lhn0", "lhn1"):
         need("g", s, 16)
     for s in ("cv", "cs", "cp", "cg"):
         need("y", s, cnt[s])

@@ -15,8 +15,8 @@ BUFS = """AW1792b YA3584b BW4104b NW4104i HS2048u HR2048u NA1792i F1792f FI272i 
 IDT1280f PAD256f DD80f WC320f WD80f EL80h CU80h MX80f OU80u INF80h SU80h KT400h ZF320f LP256h FH256h FRL16u NAU256u Ch256h
 Th256h LU256u SG4096h CB768h CL256u XR4096b D4096h VV768h SC256h AB512f KY16f KM16f TI16i TM16i UL16u UF16u FA16h
 LSU32u YF3584f XN256f XS256b IDB128b IDC128b EI1i EO1i EC1f DX256b DC256b GS256h YW1792f IP1i LPI1i GPI1i PCF1f LPC1f GPC1f QE1f CF1f CG1f
-LM128h CM128f XG144f XH144h EP144h EQ144h SAM128h IDM128f IDX128f IDH128h IDN128h IDL128h TRI128h LTM128h WK128h TF128h TL128h
-PA128h PB128h PN128h PG128h PH128h P4128h ONE128h KC128h CO128h OH128h ZM1920h XL240h HE8f DPM2048h KA2560f KB256f""".replace("P4", "PF")
+LM128h CM128f XG144f XH144h EP144h EQ144h SAM128h IDM128f IDH128h IDN128h IDL128h TRI128h LTM128h WK128h TF128h TL128h
+PA128h PB128h PN128h PG128h PH128h P4128h ONE128h KC128h CO128h OH128h ZM384h XL48h HE8f DPM2048h KA2560f KB256f""".replace("P4", "PF")
 FR, FV, FW = 5120, 8896, 3768
 STAMP = [32.0 * 5 ** w for w in range(RO - 1)]
 SCRATCH = {}
@@ -28,8 +28,10 @@ for _w in range(RO):
 PS = ("PC0", "PC1", "PQ0", "PQ1", "PL", "PR", "PM", "PT")
 for _n in PS:
     SCRATCH[_n] = ("psum", [128, 512], "float32")
-LOADS = ["f0", "bd", "xb0", "xb1", "nba", "xa", "nb0", "nb1", "nba2", "xa2"]
-SEMAPHORES = (["cv", "cs", "cp", "cg", "hb0", "hb1", "hn0", "hn1", "lhb0", "lhb1", "lhn0", "lhn1", "oy", "oa"] + ["ld_" + n for n in LOADS]
+XB = (0, 512, 1024, OB)
+LOADS = ["f0", "bd", "xb0", "xb1", "xb2", "nba", "xa", "nb0", "nb1", "nb2", "nb3", "nba2", "xa2"]
+HALOS = ["hb0", "hb1", "hb2", "hn0", "hn1", "hn2", "hn3"]
+SEMAPHORES = (["cv", "cs", "cp", "cg", "oy", "oa"] + HALOS + ["l" + n for n in HALOS] + ["ld_" + n for n in LOADS]
               + ["zw", "zb"] + [k + str(w) for k in ("gh", "lg", "xf", "xd") for w in range(RO)])
 
 VVE, KE = "svvvsv", "..sssv"
@@ -37,6 +39,8 @@ DRAIN = 3
 VSEED = 24
 VFR = 26
 FORCE = False
+ORDER = 2
+HELP = 2
 
 
 def rank_program(g, core, T, topo):
@@ -178,52 +182,62 @@ def rank_program(g, core, T, topo):
     def DP(p):
         return A("DPM", 128 * p, 128 * p + 128)
 
-    load("y", "BW", 8, 8 + 1024, T.xb, 0, "xb0")
+    load("y", "BW", 8, 8 + XB[1], T.xb, 0, "xb0")
     load("s", "FI", 0, S, T.f0, 0, "f0")
     load("s", "BDI", 0, 16, T.bd, 0, "bd")
-    load("y", "BW", 8 + 1024, 8 + OB, T.xb, 1024, "xb1")
+    for k in (1, 2):
+        load("y", "BW", 8 + XB[k], 8 + XB[k + 1], T.xb, XB[k], "xb%d" % k)
     load("s", "NA", 0, FIRST, T.nba, 0, "nba")
-    load("s", "AW", 0, FIRST, T.xa, 0, "xa")
-    HB = [A("BW", HALO, HALO + 1024), A("BW", HALO + 1024, HALO + NH)]
-    for h in range(2):
-        arrive(nxt, HB[h], "hb%d" % h)
-        arrive(nxt, A("HR", 1024 * h, 1024 * h + 1024), "hn%d" % h)
+    for k in range(3):
+        arrive(nxt, A("BW", HALO + XB[k], HALO + min(XB[k + 1], NH)), "hb%d" % k)
+    for h in range(4):
+        arrive(nxt, A("HR", 512 * h, 512 * h + 512), "hn%d" % h)
     for w in range(RO):
         arrive(prv, A("LG%d" % w), "gh%d" % w)
+
+    def numbers_out(k):
+        n = min(XB[k + 1], NH)
+        send(prv, A("BW", HALO + XB[k], HALO + n), A("BW", 8 + XB[k], 8 + n), "hb%d" % k, "lhb%d" % k)
 
     io(A("IP"), [[0, 1]], 0, 1, False)
     io(A("XG"), [[1, 144]], -15)
     io(A("CM"), [[1, 128]], 0)
     io(A("DD"), [[1, 80]], VA + 1)
     io(A("IDT"), [[1, 80], [80, 16]], 64)
-    io(A("PAD"), [[1, CAP]], 1536 + 64)
-    ms(A("F", S, 1792), 0.0)
+    numbers_out(0)
     ms(A("ZF"), 0.0)
-    ms(A("IND", S, 320), 0.0)
-    ms(A("ONE"), 1.0)
     ts(A("LPI"), A("IP"), 15, OPS.bitwise_and)
     ts(A("GPI"), A("IP"), 112, OPS.bitwise_and)
     cp(A("PCF"), A("IP"))
+    ms(A("IND", S, 320), 0.0)
     cp(A("GPC"), A("GPI"))
     ts(A("LPC"), A("LPI"), 1.0, OPS.add)
+    ts(A("QE"), A("LPI"), 80.0, OPS.mult)
+    ts(A("IDM"), A("CM"), A("PCF"), OPS.is_equal)
     ts(A("EP"), A("XG"), A("GPC"), OPS.is_equal)
+    ts(A("XH", 0, 128), A("CM"), A("GPC"), OPS.subtract)
+    ts(A("DD"), A("DD"), A("QE"), OPS.add)
+    ts(A("PH"), A("IDM"), -32768.0, OPS.mult)
+    ts(A("WK"), A("XH", 0, 128), A("LPC"), OPS.is_ge)
+    ts(A("SAM"), A("XH", 0, 128), 15.5, OPS.is_lt)
+    ts(A("IDL"), A("IDM"), A("LPC"), OPS.mult)
+    tt(A("TRI"), A("WK"), A("SAM"), OPS.mult)
+    ts(A("LM"), A("XH", 0, 128), 2.0, OPS.add, A("LPC"), OPS.is_le)
+    ts(A("WK"), A("XH", 0, 128), -0.5, OPS.is_gt)
+    cp(A("IDH"), A("IDM"))
+    tt(A("LTM"), A("WK"), A("LM"), OPS.mult)
+    for a in range(S, 1792, 320):
+        act(A("F", a, min(a + 320, 1792)), A("ZF", 0, min(320, 1792 - a)))
+    act(A("KB"), A("ZF", 0, CAP), AFT.Copy, 131072.0)
+    for k in range(2):
+        act(A("PAD", 128 * k, 128 * k + 128), A("CM"), AFT.Copy, 1536.0 + 64 + 128 * k)
     ts(A("IND", 0, S), A("FI"), 4095.0, OPS.not_equal)
     for q in range(4):
         mm(A("PM", 160, 240), EP(q), A("IND", 80 * q, 80 * q + 80), q == 0, q == 3)
-    ts(A("QE"), A("LPI"), 80.0, OPS.mult)
-    ts(A("IDM"), A("CM"), A("PCF"), OPS.is_equal)
-    ts(A("DD"), A("DD"), A("QE"), OPS.add)
-    ts(A("PH"), A("IDM"), -32768.0, OPS.mult)
-    ts(A("XH", 0, 128), A("CM"), A("GPC"), OPS.subtract)
-    ts(A("WK"), A("XH", 0, 128), A("LPC"), OPS.is_ge)
-    ts(A("SAM"), A("XH", 0, 128), 15.5, OPS.is_lt)
-    tt(A("TRI"), A("WK"), A("SAM"), OPS.mult)
+    ts(A("FI"), A("FI"), 1.0, OPS.add)
+    ms(A("ONE"), 1.0)
     ts(A("EL"), A("PM", 160, 240), 0.5, OPS.is_lt)
     ts(A("SU"), A("PM", 160, 240), 0.5, OPS.is_gt, 64.0, OPS.mult)
-    for w in range(RO - 1):
-        act(A("KA", 512 * w, 512 * w + 512), A("F", 512, 1024), AFT.Copy, STAMP[w])
-        act(A("KT", 80 * w, 80 * w + 80), A("ZF", 0, 80), AFT.Copy, -0.875 * STAMP[w])
-    act(A("KB"), A("ZF", 0, CAP), AFT.Copy, 131072.0)
 
     def ghosts_out(w):
         ts(A("GS"), I("F", VA, "BDU", 0, 16), -2048.0, OPS.add, 0.0, OPS.max)
@@ -238,11 +252,11 @@ def rank_program(g, core, T, topo):
     BASE = A("PM", 256, 257)
 
     def select_z(w):
-        msum(A("PM", 160, 240), [(A("IDH"), A("KT", 80 * w - 80, 80 * w)), (A("PG"), A("EL")), (A("PH"), A("INF")), (A("PN"), A("SU")),
-                                 (A("IDX"), A("WD"))] + [(A("IDM"), A("WC", r, 320, 4)) for r in range(4)])
+        msum(A("PM", 160, 240), [(A("IDH"), A("KT", 80 * w - 80, 80 * w)), (A("PG"), A("EL")), (A("PH"), A("INF")), (A("PN"), A("SU"))]
+             + [(A("IDM"), A("WC", r, 320, 4)) for r in range(4)])
 
     def select_1():
-        ts(A("EL"), A("PM", 160, 240), 0.0, OPS.is_gt)
+        tt(A("EL"), A("PM", 160, 240), A("WD"), OPS.is_gt)
 
     def select_2():
         op("v", A("CU"), [A("EL"), A("ZF", 0, 80)], lambda: g.vector.tensor_tensor_scan(
@@ -266,17 +280,24 @@ def rank_program(g, core, T, topo):
     def select_v():
         cp(I("W", FW, "OU", 0, VFR, FV), A("IDT", 0, 16 * VFR))
 
-    def select_p():
-        tt(A("FH"), A("W", FR + 1, FR + CAP + 1), A("W", FV + 1, FV + CAP + 1), OPS.min)
-        for l in range(16):
-            mm(A("PM", 272, 288), DP(l), A("FH", l, CAP, 16), l == 0, l == 15)
+    PART = ((0, SUB, "PM"), (SUB, CAP, "PL"))
 
-    def select_b(w):
-        ts(A("FRL"), A("PM", 272, 288), 64.0, OPS.subtract)
-        act(A("XR", 0, 4096, 16), I("AW", 1792 if w else FIRST, "FRL", 0, 16))
+    def select_p(k):
+        a, b, bank = PART[k]
+        tt(A("FH", a, b), A("W", FR + 1 + a, FR + 1 + b), A("W", FV + 1 + a, FV + 1 + b), OPS.min)
+        msum(A(bank, 272 + a // 16, 272 + b // 16), [(DP(l), A("FH", a + l, b, 16)) for l in range(16)])
 
-    def select_n(w):
-        cp(A("NAU"), I("NA", 1792 if w else FIRST, "FRL", 0, 16))
+    def select_b(k):
+        a, b, bank = PART[k]
+        ts(A("FRL", a // 16, b // 16), A(bank, 272 + a // 16, 272 + b // 16), 64.0, OPS.subtract)
+
+    def select_x(w, k):
+        a, b, bank = PART[k]
+        act(A("XR", 16 * a, 16 * b, 16), I("AW", 1792 if w else FIRST, "FRL", a // 16, b // 16))
+
+    def select_n(w, k):
+        a, b, bank = PART[k]
+        cp(A("NAU", a, b), I("NA", 1792 if w else FIRST, "FRL", a // 16, b // 16))
 
     def state():
         ts(A("INF"), A("MX"), BASE, OPS.add, CAP + 0.5, OPS.is_lt)
@@ -286,6 +307,8 @@ def rank_program(g, core, T, topo):
         for k in ks:
             if q == "g":
                 gsel(A("XR", a + k, b, 2 * k), A("XR", a, b, 2 * k), [[0, 8 * SUB // k]], 0, 0)
+            elif q == "s":
+                act(A("XR", a + k, b, 2 * k), A("XR", a, b, 2 * k))
             else:
                 cp(A("XR", a + k, b, 2 * k), A("XR", a, b, 2 * k))
 
@@ -298,78 +321,78 @@ def rank_program(g, core, T, topo):
     def relay_b(h0, h1):
         for h in range(h0, h1):
             for k in range(8):
-                mm(A("PR", h, 256, 8), A("ZM", 240 * h + 112 - 16 * k, 240 * h + 240 - 16 * k), A("Th", 32 * k, 32 * k + 32), k == 0, k == 7)
-        if h1 == 8:
-            act(A("LP"), A("PR", 0, 256))
+                out = (T.PR[32 * (k // 2):32 * (k // 2) + 32, h:256:8], [("PR", h, 256)], [])
+                a = 48 * h + 16 - 16 * (k % 2)
+                mm(out, A("ZM", a, a + 32), A("Th", 32 * k, 32 * k + 32), k % 2 == 0, k % 2 == 1)
 
     pads()
     select_2()
-    ts(A("FI"), A("FI"), 1.0, OPS.add)
-    select_3()
     ts(A("FI"), A("FI"), 4095, OPS.bitwise_and)
-    select_4()
+    select_3()
     cp(A("F", 0, S), A("FI"))
+    select_4()
     cp(A("BDU"), A("BDI"))
     select_s()
-    select_v()
-    send(prv, HB[0], A("BW", 8, 8 + 1024), "hb0", "lhb0")
+    numbers_out(1)
     ghosts_out(0)
-    send(prv, HB[1], A("BW", 8 + 1024, 8 + NH), "hb1", "lhb1")
+    numbers_out(2)
+    select_v()
+    need("y", "ld_xb2", 16)
+    load("y", "AW", 0, FIRST, T.xa, 0, "xa")
     need("y", "lhb0", len(topo.engines(core, prv)))
-    for h in range(2):
-        load("y", "NW", 8 + 1024 * h, 8 + 1024 * h + 1024, T.nbb, 1024 * h, "nb%d" % h)
-    ts(A("IDL"), A("IDM"), A("LPC"), OPS.mult)
-    for p in range(16):
-        ts(DP(p), A("IDL"), float(p + 1), OPS.is_equal)
-    io(A("XL"), [[1, 240]], -111)
+    for h in range(4):
+        load("y", "NW", 8 + 512 * h, 8 + 512 * h + 512, T.nbb, 512 * h, "nb%d" % h)
+    dma("y", T.W[0:128:16, 0:4 * VA], T.ZF[:], [("ZF", 0, 320)], [("W", 0, 4 * VA)], "zw")
+    io(A("XL"), [[1, 48]], -15)
     io(A("HE"), [[16, 8]], 0)
     io(A("CO"), [[0, 4], [1, 4], [0, 8]], 0)
     io(A("NA", 1536, 1792), [[1, CAP]], 1536, 0, False)
-    cp(A("IDH"), A("IDM"))
+    for p in range(16):
+        ts(DP(p), A("IDL"), float(p + 1), OPS.is_equal)
     state()
-    for name, c in (("PN", -2048.0), ("PG", 32768.0), ("PF", 4.0), ("IDX", -1.0), ("IDN", -1.0), ("IDB", 1.0), ("IDC", -1.0)):
-        ts(A(name), A("IDM"), c, OPS.mult)
-    ts(A("EQ"), A("EP"), 2.0, OPS.mult)
-    ms(A("KC"), -27.0)
+    tt(A("WK"), A("TRI"), A("IDH"), OPS.subtract)
+    tt(A("LM"), A("LTM"), A("IDH"), OPS.subtract)
     ms(A("EC"), C3)
     ms(A("BW", 0, 8), 1024.0)
-    ts(A("PA"), A("IDM"), 2048.0, OPS.mult)
-    ts(A("PB"), A("IDM"), 4096.0, OPS.mult)
-    ts(A("WK"), A("XH", 0, 128), -0.5, OPS.is_gt)
-    ts(A("LM"), A("XH", 0, 128), 2.0, OPS.add, A("LPC"), OPS.is_le)
-    tt(A("LTM"), A("WK"), A("LM"), OPS.mult)
-    for m, o in (("TRI", "TF"), ("LTM", "TL")):
-        tt(A("WK"), A(m), A("IDH"), OPS.subtract)
-        ts(A(o), A("WK"), WZ, OPS.mult)
-    ts(A("CF"), A("LPC"), WZ, OPS.mult)
-    ts(A("CG"), A("LPC"), -WZ, OPS.mult, 17 * WZ, OPS.add)
-    ms(A("OH"), 1.0 / 256.0)
-    ms(A("NW", 0, 8), 4095)
-    select_p()
-    ts(A("HE"), A("HE"), A("GPC"), OPS.not_equal, 1000.0, OPS.mult)
-    ms(A("AW", 1536, 1792), 0.0)
-    ts(A("HE"), A("HE"), A("LPC"), OPS.add)
+    ts(A("TF"), A("WK"), WZ, OPS.mult)
+    ts(A("TL"), A("LM"), WZ, OPS.mult)
+    select_p(0)
+    select_p(1)
+    for name, c in (("PN", -2048.0), ("PG", 32768.0), ("PF", 4.0), ("IDN", -1.0), ("IDB", 1.0), ("IDC", -1.0),
+                    ("PA", 2048.0), ("PB", 4096.0)):
+        ts(A(name), A("IDH"), c, OPS.mult)
+    for w in range(RO - 1):
+        act(A("KA", 512 * w, 512 * w + 512), A("F", 512, 1024), AFT.Copy, STAMP[w])
+        act(A("KT", 80 * w, 80 * w + 80), A("ZF", 0, 80), AFT.Copy, -0.875 * STAMP[w])
     select_b(0)
-    for h in range(8):
-        ts(A("ZM", 240 * h, 240 * h + 240), A("XL"), A("HE", h, h + 1), OPS.is_equal)
+
+    def constants():
+        ts(A("HE"), A("HE"), A("GPC"), OPS.not_equal, 1000.0, OPS.mult)
+        ts(A("EQ"), A("EP"), 2.0, OPS.mult)
+        ms(A("KC"), -27.0)
+        ts(A("HE"), A("HE"), A("LPC"), OPS.add)
+        ts(A("CF"), A("LPC"), WZ, OPS.mult)
+        ts(A("CG"), A("LPC"), -WZ, OPS.mult, 17 * WZ, OPS.add)
+        for h in range(8):
+            ts(A("ZM", 48 * h, 48 * h + 48), A("XL"), A("HE", h, h + 1), OPS.is_equal)
+        ms(A("OH"), 1.0 / 256.0)
+        ms(A("NW", 0, 8), 4095)
+        ms(A("AW", 1536, 1792), 0.0)
 
     def late_loads():
-        dma("y", T.W[0:128:16, 0:4 * VA], T.ZF[:], [("ZF", 0, 320)], [("W", 0, 4 * VA)], "zw")
+        need("y", "lhn3", len(topo.engines(core, prv)))
         dma("y", T.WB[0:128:16, 0:VA], T.ZF[0:32, :], [("ZF", 0, 320)], [("WB", 0, VA)], "zb")
-        need("y", "lhn1", len(topo.engines(core, prv)))
         load("y", "NA", FIRST, VA, T.nba, FIRST, "nba2")
         load("y", "AW", FIRST, VA, T.xa, FIRST, "xa2")
 
     def halo_out(h):
-        a = 1024 * h
-        ts(A("HS", a, a + 1024), A("NW", 8 + a, 8 + a + 1024), 2047.0, OPS.min, 2048.0, OPS.add)
-        if h:
-            ms(A("HS", 2047, 2048), 4095)
-        send(prv, A("HR", a, a + 1024), A("HS", a, a + 1024), "hn%d" % h, "lhn%d" % h)
+        a = 512 * h
+        ts(A("HS", a, a + 512 - h // 3), A("NW", 8 + a, 8 + a + 512 - h // 3), 2047.0, OPS.min, 2048.0, OPS.add)
+        send(prv, A("HR", a, a + 512), A("HS", a, a + 512), "hn%d" % h, "lhn%d" % h)
 
     def halo_in(h):
-        a = 1024 * h
-        act(A("NW", HALO + a, HALO + a + 1024), A("HR", a, a + 1024))
+        a = 512 * h
+        cp(A("NW", HALO + a, HALO + a + 512), A("HR", a, a + 512))
 
     def cb(t, X):
         return A("CB", 256 * t + CH * X, 256 * t + CH * X + CH)
@@ -396,10 +419,16 @@ def rank_program(g, core, T, topo):
             mm(sbank(s), DP(p), A("SG", 16 * a + p, 16 * a + 1024, 16), p == 0, p == 15)
 
     def slist(s):
-        ts(A("CL", SUB * s, SUB * s + SUB), sbank(s), 2048.0 + OFF, OPS.add)
+        if s == 3:
+            act(A("CL", SUB * s, SUB * s + SUB), sbank(s), AFT.Copy, 2048.0 + OFF)
+        else:
+            ts(A("CL", SUB * s, SUB * s + SUB), sbank(s), 2048.0 + OFF, OPS.add)
 
     def numbers(t, X):
-        ts(cb(t, X), A("CL", CH * X, CH * X + CH), -2048.0 - OFF, OPS.add)
+        if t == 0:
+            act(cb(t, X), A("CL", CH * X, CH * X + CH), AFT.Copy, -2048.0 - OFF)
+        else:
+            ts(cb(t, X), A("CL", CH * X, CH * X + CH), -2048.0 - OFF, OPS.add)
 
     def G(X, lo, hi):
         a, b = CH * X + lo, CH * X + hi
@@ -409,12 +438,24 @@ def rank_program(g, core, T, topo):
         a = 16 * (CH * X + SUB * s)
         ts(A("D", a, a + 16 * n), A("D", a, a + 16 * n), A("EC"), OPS.add, A("EC"), OPS.is_equal)
 
+    def Gs(X, k):
+        a, b = CH * X + 32 * k, 2560 + 512 * (k - 1)
+        act(A("SG", b, b + 512), I("BW", 4104, "CL", a, a + 32))
+
+    def Gp(X, k, odd="PM"):
+        a, b = CH * X + 32 * k, 2560 + 512 * (k - 1)
+        msum(A(("PR", odd)[k % 2]), [(A("IDC"), A("XR", 16 * a, 16 * a + 512)), (A("IDH"), A("SG", b, b + 512))])
+
+    def Hs(X, k, odd="PM"):
+        a = 16 * (CH * X + 32 * k)
+        ts(A("D", a, a + 512), A(("PR", odd)[k % 2]), A("EC"), OPS.add, A("EC"), OPS.is_equal)
+
     def count(X, s, n=SUB):
         a, o = 16 * (CH * X + SUB * s), A("PC%d" % X, SUB * s, SUB * s + n)
         msum(o, [(A("IDH"), A("KC", 0, n))] + [(EP(p, "EQ"), A("D", a + p, a + 16 * n, 16)) for p in range(16)])
 
-    def sign(t, X):
-        if VVE[2 * t + X] == "s":
+    def sign(t, X, q=None):
+        if (q or VVE[2 * t + X]) == "s":
             act(vv(t, X), A("PC%d" % X, 0, CH), AFT.Sign)
         else:
             ts(vv(t, X), A("PC%d" % X, 0, CH), -1.0, OPS.max, 1.0, OPS.min)
@@ -455,13 +496,14 @@ def rank_program(g, core, T, topo):
         mm(pq(X, 1), A("PN"), vv(2, X), False, True)
         msum(pq(X, 2), [(idn, cb(2, X)), (A("PB"), vv(2, X))])
 
-    def store(w, X):
+    def store(w, X, between=None):
         a = 256 * X
         old, new = A("AB", a, a + CH), A("AB", a + CH, a + 2 * CH)
         if w < RO - 1:
             tt(I("F", 1792, "FRL", 8 * X, 8 * X + 8), old, new, OPS.add)
         else:
             ts(old, old, -1.0, OPS.mult, 4095.0, OPS.add)
+            between()
             tt(I("YW", 1792, "FRL", 8 * X, 8 * X + 8), old, new, OPS.subtract)
 
     pend = []
@@ -479,6 +521,9 @@ def rank_program(g, core, T, topo):
             ts(A("FA", lo, hi), A("PL", 48 + lo, 48 + hi), -15.0, OPS.is_lt, 1792.0, OPS.mult)
         else:
             act(A("FA", lo, hi), A("PL", 48 + lo, 48 + hi), AFT.Relu, -896.0 * 14, -896.0)
+
+    def fails_m(w, X):
+        lo, hi, a = 8 * X, 8 * X + 8, CH * X
         if w < RO - 1:
             msum(A("PR", a, a + CH), [(A("PF"), A("LP", a, a + CH)), (A("IDH"), A("CO"))], True, False)
             for p in range(16):
@@ -496,27 +541,30 @@ def rank_program(g, core, T, topo):
     def fails_b(w):
         a = 16 * (w % 2)
         act(A("LSU", a, a + 16), A("PT", 256, 272), AFT.Copy, -64.0)
-        if w < RO - 1:
-            drain(1)
-            act(I("WB", 3584, "LSU", a, a + 16), A("KB"), AFT.Silu)
-            extract_b(w + 1)
+
+    def full(w):
+        act(I("WB", 3584, "LSU", 16 * (w % 2), 16 * (w % 2) + 16), A("KB"), AFT.Silu)
+        extract_b(w + 1)
 
     xs = A("XR", 0, 4096, 16)
-    update = [lambda: tt(A("TI"), A("PL", 32, 48), A("KM"), OPS.min),
-              lambda: ts(A("TM"), A("TI"), 4095, OPS.bitwise_and),
-              lambda: ts(A("UF"), A("TM"), float(OFF), OPS.add),
-              lambda: tt(A("DX"), I("BW", 4104, "UF", 0, 16), xs, OPS.subtract),
-              lambda: ts(A("DC"), A("DX"), -2.0, OPS.max, 2.0, OPS.min),
-              lambda: tt(I("YA", 3584, "LSU", 16, 32), A("DC"), xs, OPS.add)]
+
+    def update(lo, hi):
+        a, b = 16 * lo, 16 * hi
+        x = A("XR", 16 * a, 16 * b, 16)
+        return [lambda: tt(A("TI", lo, hi), A("PL", 32 + lo, 32 + hi), A("KM", lo, hi), OPS.min),
+                lambda: ts(A("TM", lo, hi), A("TI", lo, hi), 4095, OPS.bitwise_and),
+                lambda: ts(A("UF", lo, hi), A("TM", lo, hi), float(OFF), OPS.add),
+                lambda: tt(A("DX", a, b), I("BW", 4104, "UF", lo, hi), x, OPS.subtract),
+                lambda: ts(A("DC", a, b), A("DX", a, b), -2.0, OPS.max, 2.0, OPS.min),
+                lambda: tt(I("YA", 3584, "LSU", 16 + lo, 16 + hi), A("DC", a, b), x, OPS.add)]
 
     def move_a():
-        act(A("XS"), xs)
         act(A("DX"), I("BW", 4104, "UF", 0, 16))
-        msum(pq(0, 1, 2), [(A("IDB"), A("DX")), (A("IDC"), A("XS"))])
+        msum(A("PT", CAP, 2 * CAP), [(A("IDC"), A("XS")), (A("IDB"), A("DX"))])
 
     def move_b():
-        act(A("DX"), pq(0, 1, 2), AFT.Relu, 2.0)
-        act(A("DC"), pq(0, 1, 2), AFT.Relu, -2.0)
+        act(A("DX"), A("PT", CAP, 2 * CAP), AFT.Relu, 2.0)
+        act(A("DC"), A("PT", CAP, 2 * CAP), AFT.Relu, -2.0)
 
     def move_c():
         msum(A("PT", 0, CAP), [(A("IDB"), A("DX")), (A("IDC"), A("DC")), (A("IDB"), A("XS"))])
@@ -526,109 +574,152 @@ def rank_program(g, core, T, topo):
         act(I("YF", 3584, "LSU", 16 * (w % 2), 16 * (w % 2) + 16), A("XN"), AFT.Silu)
 
     def moved_out():
-        act(A("YF", 0, VA), A("YF", 0, VA), AFT.Copy, 1.5 * 2.0 ** 23 - 256.0)
-        act(A("YA", 0, VA), A("YF", 0, VA), AFT.Copy, -1.5 * 2.0 ** 23)
+        return [lambda: act(A("YF", 0, VA), A("YF", 0, VA), AFT.Copy, 1.5 * 2.0 ** 23 - 256.0),
+                lambda: act(A("YA", 0, VA), A("YF", 0, VA), AFT.Copy, -1.5 * 2.0 ** 23)]
 
     def parity_p():
         msum(A("PM", 300, 301), [(A("OH"), A("FA", k, k + 1)) for k in range(16)])
 
-    parity = [lambda: cp(A("EI"), A("PM", 300, 301)),
+    parity = [lambda: act(A("EI"), A("PM", 300, 301)),
               lambda: ts(A("EO"), A("EI"), 1, OPS.bitwise_and),
-              lambda: ts(A("EC"), A("EO"), -8.0, OPS.mult, C3, OPS.add)]
+              lambda: act(A("EC"), A("EO"), AFT.Copy, C3, -8.0)]
 
     def old_out():
-        act(A("SG", 0, VA), A("F", 0, VA), AFT.Copy, -2048.0)
-        act(A("SG", VA, 2 * VA), A("F", 0, VA), AFT.Relu, 1.0, -1.0)
-        for k, (a, b) in enumerate(((0, 512), (512, 1024), (1024, VA))):
-            o = A(("PT", "PM")[k % 2], 0, b - a)
-            msum(o, [(A("IDH"), A("SG", a, b)), (A("PB"), A("SG", VA + a, VA + b))])
-            pend.append(lambda a=a, b=b, o=o: act(A("YW", a, b), o, AFT.Copy, 2047.0))
-            if k:
-                drain(1)
+        def piece(a, b):
+            msum(A("PT", 0, b - a), [(A("IDH"), A("SG", a, b)), (A("PB"), A("SG", VA + a, VA + b))])
+            act(A("YW", a, b), A("PT", 0, b - a), AFT.Copy, 2047.0)
+        return [lambda: act(A("SG", 0, VA), A("F", 0, VA), AFT.Copy, -2048.0),
+                lambda: act(A("SG", VA, 2 * VA), A("F", 0, VA), AFT.Relu, 1.0, -1.0),
+                lambda: piece(0, 512), lambda: piece(512, 1024), lambda: piece(1024, VA)]
 
     def HC(X, s):
         H(X, s)
         count(X, s)
 
+    def slot_last(t, X):
+        Y, idn = 1 - X, A("IDN")
+        G(Y, 0, 32)
+        sign(t, X)
+        Gp(Y, 2)
+        rank_p(t, X)
+        if t == 0:
+            fails_p(1)
+        G(Y, 32, 64)
+        choose(t, X)
+        Gp(Y, 3)
+        if t:
+            keep_a(X, idn)
+            relu(1, X)
+        Hs(Y, 2)
+        HC(Y, 0)
+        if t == 0 and X:
+            fails_s(RO - 1, 1)
+            fails_m(RO - 1, 1)
+            fails_b(RO - 1)
+        blist(t, X)
+        Hs(Y, 3)
+        nbg(X)
+        count(Y, 1)
+        if t:
+            keep_b(X)
+        if t and X:
+            cp(A("KY"), A("PL", 0, 16))
+        numbers(t + 1, X)
+        Gs(X, 2)
+        Gs(X, 3)
+        drain(1 if t and X else 2)
+        if t and X:
+            tt(A("KM"), A("PL", 16, 32), A("KY"), OPS.min)
+
     for w in range(RO):
         last = w == RO - 1
         more = (lambda f, *a: None) if last else (lambda f, *a: f(*a))
         idn = A("IDN") if last else A("IDH")
+        select_x(w, 0)
+        select_n(w, 0)
+        select_b(1)
         if w == 0:
-            act(A("F", VA, VA + 256), A("LG0"))
-        select_n(w)
-        xrep("v", 0, (8,))
+            ms(A("HS", 2047, 2048), 4095)
+            constants()
+        act(A("F", VA, VA + 256), A("LG%d" % w))
+        select_x(w, 1)
         xrep("g", 1)
         xrep("g", 2)
+        xrep("v", 0, (8,))
         seeds(0)
         diag(0)
+        select_n(w, 1)
         xrep("v", 0, (4,))
         more(relay_a)
         xrep("v", 0, (2,))
-        xrep("v", 3, (8,))
+        if w:
+            update(0, 16)[2]()
         xrep("v", 0, (1,))
         seeds(1)
         more(act, A("Th"), A("PT", 0, 256))
-        slist(0)
-        xrep("v", 3, (4,))
         if w == 0:
             op("v", (T.BW[:, 4103:4104], [("BW", 4096, 4104)], []), [], lambda: g.vector.memset(T.BW[:, 4103:4104], 1024.0))
+        slist(0)
         G(0, 0, 64)
         diag(1)
         seeds(2)
-        more(relay_b, 0, 2)
-        xrep("v", 3, (2,))
+        more(relay_b, 0, 5)
         slist(1)
-        HC(0, 0)
-        G(0, 64, 128)
-        more(relay_b, 2, 4)
-        diag(2)
-        seeds(3)
-        if w:
-            move_b()
-        more(relay_b, 4, 8)
-        numbers(0, 0)
-        xrep("v", 3, (1,))
-        slist(2)
-        HC(0, 1)
-        diag(3)
         if w == 0:
             halo_out(0)
+        HC(0, 0)
+        G(0, 64, 128)
+        if w == 0:
             halo_out(1)
-            late_loads()
+        diag(2)
+        seeds(3)
+        more(relay_b, 5, 8)
+        xrep("s", 3, (8,))
+        numbers(0, 0)
+        xrep("s", 3, (4,))
+        more(act, A("LP"), A("PR", 0, 256))
+        xrep("s", 3, (2,))
+        slist(2)
+        diag(3)
+        slist(3)
+        HC(0, 1)
+        if w == 0:
+            halo_out(2)
         for slot in range(4):
             t, X = slot // 2, slot % 2
             if slot == 0:
                 sign(0, 0)
+                xrep("s", 3, (1,))
+                numbers(0, 1)
                 fails_p(0)
                 rank_p(0, 0)
                 fails_s(w, 0)
+                fails_m(w, 0)
                 fails_l(w, 0)
                 if last:
-                    move_c()
-                    move_d(w - 1)
-                    old_out()
-                    drain(9)
-                    moved_out()
-                if w == 0:
-                    drain(1)
-                    halo_in(0)
-                    halo_in(1)
-            G(1 - X, 0, 48)
+                    old, moved = old_out(), moved_out()
+                    pend.extend([move_a, old[0], move_b, old[1], lambda: (move_c(), move_d(RO - 2)), moved[0], old[2], moved[1],
+                                 old[3], old[4]])
+                    drain(2)
+            elif last:
+                slot_last(t, X)
+                continue
+            G(1 - X, 0, 48 if slot else 64)
             if slot == 0:
-                slist(3)
+                if w == 0:
+                    halo_out(3)
+                    late_loads()
             else:
                 sign(t, X)
                 if slot == 1:
                     fails_p(1)
                 rank_p(t, X)
-            G(1 - X, 48, 80)
-            if slot == 0:
-                numbers(0, 1)
+            G(1 - X, 48 if slot else 64, 80)
             if slot == 1:
                 fails_s(w, 1)
             choose(t, X)
             if slot == 1:
+                fails_m(w, 1)
                 drain(4)
                 fails_l(w, 1)
                 fails_b(w)
@@ -637,13 +728,25 @@ def rank_program(g, core, T, topo):
             G(1 - X, 80, 128)
             blist(t, X)
             HC(1 - X, 0)
+            if w == 0 and slot == 0:
+                HC(1, 1)
+                for h in range(4):
+                    halo_in(h)
             nbg(X)
-            HC(1 - X, 1)
+            if last:
+                Gs(0, 2)
+                Gs(0, 3)
+                drain(2)
+            if w or slot:
+                HC(1 - X, 1)
             if slot == 2:
                 more(parity_p)
             numbers(t + 1, X)
+        if last:
+            break
         drain(99)
         more(extract, w + 1)
+        more(full, w)
         relu(1, 0)
         keep_b(0)
         sign(2, 0)
@@ -651,58 +754,118 @@ def rank_program(g, core, T, topo):
         rank_p(2, 0)
         relu(1, 1)
         keep_b(1)
+        if w:
+            move_a()
+        parity[0]()
         relu(2, 0)
         act(A("KY"), A("PL", 0, 16))
+        if w:
+            move_b()
         more(pads)
         if w == 0:
             act(A("YF", 0, VA), A("AW", 0, VA), AFT.Copy, 256.0)
-        elif not last:
+        G(1, 0, 128)
+        parity[1]()
+        select_z(w + 1)
+        if w:
             move_c()
             move_d(w - 1)
-        G(1, 0, 64)
-        more(parity[0])
-        G(1, 64, 128)
-        more(parity[1])
-        more(select_z, w + 1)
         HC(1, 0)
-        HC(1, 1)
-        more(select_1)
-        tt(A("KM"), A("PL", 16, 32), A("KY"), OPS.min)
-        more(parity[2])
-        more(select_2)
-        store(w, 0)
-        sign(2, 1)
-        keep_c(1, idn)
-        rank_p(2, 1)
-        more(select_3)
-        choose(2, 0)
-        more(select_4)
-        more(select_s)
+        if ORDER == 2:
+            HC(1, 1)
+            select_1()
+            tt(A("KM"), A("PL", 16, 32), A("KY"), OPS.min)
+            select_2()
+            store(w, 0)
+            sign(2, 1)
+            select_3()
+            keep_c(1, idn)
+            rank_p(2, 1)
+            choose(2, 0)
+            select_4()
+            parity[2]()
+            select_s()
+            state()
+        elif ORDER == 0:
+            select_1()
+            H(1, 1)
+            select_2()
+            count(1, 1)
+            store(w, 0)
+            select_3()
+            tt(A("KM"), A("PL", 16, 32), A("KY"), OPS.min)
+            select_4()
+            parity[2]()
+            select_s()
+            sign(2, 1)
+            keep_c(1, idn)
+            rank_p(2, 1)
+            choose(2, 0)
+            state()
+        else:
+            HC(1, 1)
+            select_1()
+            store(w, 0)
+            select_2()
+            sign(2, 1)
+            keep_c(1, idn)
+            rank_p(2, 1)
+            select_3()
+            choose(2, 0)
+            select_4()
+            parity[2]()
+            select_s()
+            tt(A("KM"), A("PL", 16, 32), A("KY"), OPS.min)
+            state()
         relu(2, 1)
         choose(2, 1)
         store(w, 1)
-        more(state)
-        if last:
-            dma("y", T.yf[:], T.YW[:, 0:VA], [("YW", 0, VA)], [], "oy")
-            for f in update:
-                f()
-            dma("y", T.ya[:], T.YA[:, 0:VA], [("YA", 0, VA)], [], "oa")
-        else:
-            ghosts_out(w + 1)
-            update[0]()
-            select_v()
-            update[1]()
-            select_p()
-            update[2]()
-            move_a()
-            act(A("F", VA, VA + 256), A("LG%d" % (w + 1)))
-            select_b(w + 1)
+        ghosts_out(w + 1)
+        select_v()
+        update(0, 16)[0]()
+        act(A("XS"), xs)
+        select_p(0)
+        select_p(1)
+        update(0, 16)[1]()
+        select_b(0)
+
+    first, second = update(0, 8), update(8, 16)
+    G(1, 0, 32)
+    sign(2, 0, "v")
+    Gp(1, 2)
+    keep_c(0, idn)
+    rank_p(2, 0)
+    Gp(1, 3)
+    relu(2, 0)
+    drain(99)
+    G(1, 32, 64)
+    choose(2, 0)
+    Hs(1, 2)
+    HC(1, 0)
+    first[0]()
+    Hs(1, 3)
+    count(1, 1)
+    first[1]()
+    store(w, 0, first[2])
+    first[3]()
+    sign(2, 1)
+    keep_c(1, idn)
+    rank_p(2, 1)
+    first[4]()
+    relu(2, 1)
+    first[5]()
+    choose(2, 1)
+    store(w, 1, lambda: None)
+    dma("y", T.yf[:], T.YW[:, 0:VA], [("YW", 0, VA)], [], "oy")
+    for f in second:
+        f()
+    dma("y", T.ya[:], T.YA[:, 0:VA], [("YA", 0, VA)], [], "oa")
 
     need("y", "oy", 16)
     need("y", "oa", 16)
     for w in range(RO):
         need("g", "lg%d" % w, 16)
-    for s in ("lhb0", "lhb1", "lhn0", "lhn1"):
-        need("g", s, 16)
+    for s in HALOS:
+        need("g", "l" + s, len(topo.engines(core, prv)))
     for s in ("cv", "cs", "cp", "cg"):
         need("y", s, cnt[s])

@@ -1,46 +1,292 @@
-from concourse.mybir import AluOpType as OPS, ActivationFunctionType as AFT
+from concourse.mybir import AluOpType as OPS, ActivationFunctionType as AFT, AxisListType as AXL
 
 VA, OB, CAP, S, RO = 1280, 2048, 256, 272, 6
 CH, SUB = 128, 64
 OFF = 7
 HALO = OB + 1 + OFF
 NH = 2047
-FIRST = S + CAP
+A0, AG, AE = CAP, CAP + VA, 2 * CAP + VA
+FIRST = A0 + S + CAP
 C4 = 1.5 * 2.0 ** 26
 C3 = C4 + 8.0
 WZ, THR = 16384.0, 18432.0
 
 DTS = {"b": "bfloat16", "f": "float32", "h": "float16", "i": "int32", "u": "uint16"}
-BUFS = """AW1792b YA3584b BW4104b NW4104i HS2048u HR2048u NA1792i F1792f FI272i BDI16i BDU16u IND320h W14336f WB3584f
-IDT1280f PAD256f DD80f WC320f WD80f EL80h CU80h MX80f OU80u INF80h SU80h KT400h ZF320f LP256h FH256h FRL16u NAU256u Ch256h
-Th256h LU256u SG4096h CB768h CL256u XR4096b D4096h VV768h SC256h AB512f KY16f KM16f TI16i TM16i UL16u UF16u FA16h
-LSU32u YF3584f XN256f XS256b IDB128b IDC128b EI1i EO1i EC1f DX256b DC256b GS256h YW1792f IP1i LPI1i GPI1i PCF1f LPC1f GPC1f QE1f CF1f CG1f
+BUFS = """AW1536b YA3584b BW4104b NW4104i HS2048i NA1536i F1792f FI272i BDI16i BDU16u IND272h W14336f WB3584f YF3584f XN256f
+WC448f WD112f EL96h CU96h INF80h SU80h KT400b ZF320f FH16h FRL32u NAU256u JJ256h CA256h TA16f GT96f SL16u SH16h CC16h DH16h LSP16u
+HI256h DG16h T0X1f D6X128h NLT128h I6X128h I16X128h I112X128h IM128h
+Ch256h Th256h LP256h LU256u SG4096h CB768h CL256u XR4096b D4096h VV768h SC256h AB512f AC512f KY16f KM16f TI16i TM16i UL16u UF16u FA16h
+LSU32u XS512b IDB128b IDC128b EI1i EO1i EC1f DB256b DC256b GS256f YW1536f IP1i LPI1i GPI1i PCF1f LPC1f GPC1f CF1f CG1f
 LM128h CM128f XG144f XH144h EP144h EQ144h SAM128h IDM128f IDH128h IDN128h IDL128h TRI128h LTM128h WK128h TF128h TL128h
-PA128h PB128h PN128h PG128h PH128h P4128h ONE128h KC128h CO128h OH128h ZM384h XL48h HE8f DPM2048h KA2560f KB256f""".replace("P4", "PF")
-FR, FV, FW = 5120, 8896, 3768
-STAMP = [32.0 * 5 ** w for w in range(RO - 1)]
+PA128h PB128h PN128h PG128b PF128h ONE128h KC128h CO256h OH128h ZM384h XL48h HE8f DPM2048h KA1280f KB256f"""
+WW = 7168
+FR, FV, FW = 0, 1544, 1544
+STAMP = [32.0 * 8 ** w for w in range(RO - 1)]
 SCRATCH = {}
 for _b in BUFS.split():
     _n = _b.rstrip("bfhiu").rstrip("0123456789")
-    SCRATCH[_n] = ("sbuf", [128, int(_b[len(_n):-1])], DTS[_b[-1]])
-for _w in range(RO):
-    SCRATCH["LG%d" % _w] = ("sbuf", [128, 256], "float16")
+    SCRATCH[_n.rstrip("X")] = ("sbuf", [128, int(_b[len(_n):-1])], DTS[_b[-1]])
 PS = ("PC0", "PC1", "PQ0", "PQ1", "PL", "PR", "PM", "PT")
 for _n in PS:
     SCRATCH[_n] = ("psum", [128, 512], "float32")
-XB = (0, 512, 1024, OB)
-LOADS = ["f0", "bd", "xb0", "xb1", "xb2", "nba", "xa", "nb0", "nb1", "nb2", "nb3", "nba2", "xa2"]
-HALOS = ["hb0", "hb1", "hb2", "hn0", "hn1", "hn2", "hn3"]
-SEMAPHORES = (["cv", "cs", "cp", "cg", "oy", "oa"] + HALOS + ["l" + n for n in HALOS] + ["ld_" + n for n in LOADS]
-              + ["zw", "zb"] + [k + str(w) for k in ("gh", "lg", "xf", "xd") for w in range(RO)])
+XB = (0, 512, 1024, 1536, OB)
+LOADS = ["f0", "bd", "xb0", "xb1", "xb2", "xb3", "nba", "xa", "nb0", "nb1", "nb2", "nb3", "nba2", "xa2"]
+HALOS = ["hb0", "hb1", "hb2", "hb3", "hn0", "hn1", "hn2", "hn3"]
+QUARTER = ["hb0", "hb1", "hb2", "gh0"]
+SEMAPHORES = (["cv", "cs", "cp", "cg", "oy", "oa", "lc"] + HALOS + ["l" + n for n in HALOS] + ["ld_" + n for n in LOADS]
+              + ["zw0", "zw1", "zw2", "zb"] + [k + str(w) for k in ("gh", "lg", "cr", "xe", "xf", "xv", "xd") for w in range(RO)])
 
-VVE, KE = "svvvsv", "..sssv"
-DRAIN = 3
+SIGNQ = "svvvvs"
+KEEPQ = "..ssss"
+SHARE = (0, 0, 0, 0, 1, 2)
+SHARE_LAST = (0, 2, 2, 2, 2, 2)
 VSEED = 24
-VFR = 26
-FORCE = False
-ORDER = 2
-HELP = 2
+VFR = 16
+WBQ = "s"
+VFL = 0
+UNITS = ((0, 128), (128, 128))
+PIECES = ((("g", 0, 64), ("h", 0, 64), ("g", 64, 128), ("h", 64, 128)),
+          (("g", 0, 64), ("g", 64, 80), ("g", 80, 128), ("h", 0, 64), ("h", 64, 128)),
+          (("g", 0, 48), ("g", 48, 80), ("g", 80, 128), ("h", 0, 64), ("h", 64, 128)))
+PASSES = 3
+
+CYC, GATHER, PECYC = 0.83, 1.56, 0.45
+SCATTER = 3.8
+WAKE = 150.0
+TWO = 1.8
+VTAKES = ()
+MID = 6
+ENDS = (((0, 128),), ((0, 128),))
+MB = "PT"
+SQ = "sssssss"
+NUMQ = "svsv"
+KB_LATE = 1
+LB = "PC0"
+RATE = 300.0
+ONCE = 5000.0
+LATE = 1
+OUFIRST = 0
+ELAFTER = "own test"
+LSQ = "v"
+EARLY = 2
+AHEAD = 8
+RERUN = (1,)
+SHORT = 300.0
+SLACK = 3000.0
+FIT = 100.0
+WEIGH = 1.0
+CASES = ((1.56, 3.8, 0.0), (1.4, 5.3, 0.0), (1.95, 2.2, 0.0), (1.15, 2.0, 0.0))
+TRIES = (((1, 2), (1, 2, 3, 4), 26000), ((-1, 0), (-1, 0), 5000), ((4, 5), (5,), 6000))
+HEAT = 0.002
+VFIX, SFIX = 25.0, 35.0
+SEED = 1
+ORDER = {}
+
+
+def place(tasks, before, seq):
+    start, busy = {}, {}
+    for j in seq:
+        q, dur, banks = tasks[j]["q"], tasks[j]["dur"], tasks[j]["banks"]
+        t = max([start[i] + tasks[i]["dur"] + d for i, d in before[j]] + [0.0])
+        moved = True
+        while moved:
+            moved = False
+            for r in [q] + banks:
+                l = busy.setdefault(r, [])
+                k = len(l)
+                while k and l[k - 1][1] + WAKE > t:
+                    k -= 1
+                for a, b, q2 in l[k:]:
+                    pad = WAKE if q2 != q else 0.0
+                    if a - pad >= t + dur:
+                        break
+                    if t < b + pad:
+                        t, moved = b + pad, True
+        start[j] = t
+        for r in [q] + banks:
+            l = busy[r]
+            k = len(l)
+            while k and l[k - 1][0] > t:
+                k -= 1
+            l.insert(k, (t, t + dur, q))
+    return start
+
+
+def run_through(tasks, before, after, way):
+    n = len(tasks)
+    end, free, bank, seq = {}, {}, {}, []
+    left = [len(b) for b in before]
+    mine = {q: sorted([j for j in range(n) if tasks[j]["q"] == q], key=lambda j: -way[j]) for q in "vspgy"}
+    for q in mine:
+        free[q] = 0.0
+
+    def ready(j, memo):
+        if j not in memo:
+            t = free[tasks[j]["q"]]
+            for i, d in before[j]:
+                t = max(t, (end[i] if i in end else ready(i, memo) + tasks[i]["dur"]) + d)
+            for r in tasks[j]["banks"]:
+                if r in bank and bank[r][1] != tasks[j]["q"]:
+                    t = max(t, bank[r][0] + WAKE)
+            memo[j] = t
+        return memo[j]
+
+    while len(seq) < n:
+        memo, pick = {}, None
+        for q in sorted(mine, key=lambda q: free[q]):
+            near = mine[q][:AHEAD]
+            if not near:
+                continue
+            goal = max(near, key=lambda j: way[j] - WEIGH * ready(j, memo))
+            open_ = [j for j in near if not left[j]]
+            first = min([ready(j, memo) for j in open_] + [ready(goal, memo)])
+            short = [j for j in open_ if tasks[j]["dur"] < SHORT and ready(j, memo) <= first + 1.0 and way[j] > way[goal] - SLACK]
+            fits = [j for j in open_ if ready(j, memo) + tasks[j]["dur"] <= ready(goal, memo) + FIT]
+            j = max(short, key=lambda j: way[j]) if short else max(fits, key=lambda j: way[j] - WEIGH * ready(j, memo)) if fits else goal
+            if not left[j] and (pick is None or ready(j, memo) < pick[0]):
+                pick = (ready(j, memo), j)
+        if pick is None:
+            pick = min((ready(j, memo), j) for q in mine for j in mine[q] if not left[j])
+        t, j = pick
+        q = tasks[j]["q"]
+        end[j] = free[q] = t + tasks[j]["dur"]
+        for r in tasks[j]["banks"]:
+            bank[r] = (end[j], q)
+        for k, _ in after[j]:
+            left[k] -= 1
+        mine[q].remove(j)
+        seq.append(j)
+    return seq
+
+
+def arrange(tasks, before):
+    n = len(tasks)
+    after = [[] for _ in range(n)]
+    for j in range(n):
+        for i, d in before[j]:
+            after[i].append((j, d))
+    way = [0.0] * n
+    for i in range(n - 1, -1, -1):
+        way[i] = tasks[i]["dur"] + max([way[j] + d for j, d in after[i]] + [tasks[i]["lat"]])
+    start = place(tasks, before, run_through(tasks, before, after, way))
+    best = start
+    for k in range(PASSES):
+        back = place(tasks, after, sorted(range(n), key=lambda j: -start[j] - tasks[j]["dur"]))
+        way = [back[j] + tasks[j]["dur"] for j in range(n)]
+        start = place(tasks, before, run_through(tasks, before, after, way) if k in RERUN else sorted(range(n), key=lambda j: -way[j]))
+        if max(start.values()) < max(best.values()):
+            best = start
+    ORDER["span"] = max(best.values())
+    return polish(tasks, before, best)
+
+
+def polish(tasks, before, start):
+    n, res = len(tasks), {}
+    qi = [res.setdefault(t["q"], len(res)) for t in tasks]
+    bk = [[res.setdefault(b, len(res)) for b in t["banks"]] for t in tasks]
+    kinds = {}
+    wave, kind = [t["wave"] for t in tasks], [kinds.setdefault(t["kind"], len(kinds)) for t in tasks]
+    near, pre = list(before), [[i for i, _ in b] for b in before]
+    head = [min(start[j] for j in range(n) if tasks[j]["mark"] == "seeds" and wave[j] == w) for w in range(RO)]
+    origin = {w: head[1] + (w - 1) * (head[3] - head[2]) for w in range(1, RO)}
+    origin[0], origin[-1] = head[0], 0.0
+    base_of, place_of = [origin[w] for w in wave], [0.0] * len(kinds)
+    for j in sorted(range(n), key=lambda j: wave[j] == 2):
+        place_of[kind[j]] = start[j] - (head[wave[j]] if wave[j] >= 0 else 0.0)
+    seed = [SEED]
+
+    def rand(k):
+        seed[0] = (seed[0] * 1103515245 + 12345) % 2147483648
+        return (seed[0] >> 8) % k
+
+    def order(part, pl):
+        key = [0.0] * n
+        for j in part:
+            x = base_of[j] + pl[kind[j]]
+            for i in pre[j]:
+                if key[i] >= x:
+                    x = key[i] + 0.01
+            key[j] = x
+        return sorted(part, key=lambda j: key[j]), key
+
+    def run(seq, case, end, goal, why):
+        free, who = [0.0] * len(res), [-1] * len(res)
+        for j in seq:
+            q = qi[j]
+            t, c = free[q], who[q]
+            for i, d in near[j]:
+                if end[i] + d > t:
+                    t, c = end[i] + d, -2 - i
+            for b in bk[j]:
+                k = who[b]
+                if k >= 0 and qi[k] != q and free[b] + WAKE > t:
+                    t, c = free[b] + WAKE, k
+            end[j] = free[q] = t + case[j]
+            who[q], why[j] = j, c
+            for b in bk[j]:
+                free[b], who[b] = end[j], j
+        return max((end[j] + tasks[j]["lat"], j) for j in goal)
+
+    cases = [[t["durs"][c] for t in tasks] for c in range(len(CASES))]
+    for waves, free_waves, tries in TRIES:
+        ends, why = [[0.0] * n for _ in cases], {}
+        for case, end in zip(cases, ends):
+            run(order(range(n), place_of)[0], case, end, [n - 1], why)
+        if waves[-1] == RO - 1:
+            part = goal = [j for j in range(n) if wave[j] in waves]
+        else:
+            goal = [max(j for j in range(n) if tasks[j]["mark"] == "test" and wave[j] == waves[-1] + 1)]
+            part = [j for j in range(goal[0] + 1) if wave[j] >= waves[0]]
+        inside = set(part)
+        t0 = [min(end[j] for j in part) for end in ends]
+        for j in part:
+            out = [(i, d) for i, d in before[j] if i not in inside]
+            near[j] = [(i, d) for i, d in before[j] if i in inside] + sorted(out, key=lambda x: ends[0][x[0]] + x[1])[-1:]
+            pre[j] = [i for i in pre[j] if i in inside]
+        seq, key = order(part, place_of)
+        base = [run(seq, case, end, goal, why)[0] - t for case, end, t in zip(cases, ends, t0)]
+
+        def share(seq, c):
+            return (run(seq, cases[c], ends[c], goal, why)[0] - t0[c]) / base[c]
+        each = [1.0] * len(cases)
+        now = least = 1.5
+        best, left = place_of, tries
+        while left > 0:
+            c = rand(len(cases))
+            j, pairs = run(seq, cases[c], ends[c], goal, why)[1], []
+            while j in inside and why[j] != -1:
+                i = why[j]
+                if i >= 0 and i not in pre[j] and wave[i] in free_waves and wave[j] in free_waves:
+                    pairs.append((i, j))
+                j = i if i >= 0 else -2 - i
+            left -= 1
+            for _ in range(min(20, len(pairs))):
+                u, v = pairs[rand(len(pairs))]
+                pl, r = list(place_of), rand(10)
+                if r < 4:
+                    pl[kind[u]] = key[v] - origin[wave[u]] + (1.0, 100.0, 400.0, 1000.0, 2500.0)[rand(5)]
+                else:
+                    x = key[u] - (1.0, 100.0, 400.0)[rand(3)]
+                    pl[kind[v]] = x - origin[wave[v]]
+                    for i in pre[v]:
+                        if key[i] > x and wave[i] in free_waves:
+                            pl[kind[i]] = x - 1.0 - origin[wave[i]]
+                seq2, key2 = order(part, pl)
+                left -= 1
+                room = HEAT * left / tries * rand(100) / 100.0
+                mine = share(seq2, c)
+                if mine > each[c] + room:
+                    continue
+                r = [mine if k == c else share(seq2, k) for k in range(len(cases))]
+                new = sum(r) / len(r) + 0.5 * max(r)
+                if new < now + room:
+                    place_of, seq, key, now, each = pl, seq2, key2, new, r
+                    if new < least:
+                        best, least = pl, new
+                    break
+        place_of = best
+        near[:], pre[:] = before, [[i for i, _ in b] for b in before]
+    return order(range(n), place_of)[0]
 
 
 def rank_program(g, core, T, topo):
@@ -92,28 +338,101 @@ def rank_program(g, core, T, topo):
                     l[:] = [a for a in l if a[5] or a[2] != q or a[3] != sem or not (lo <= a[0] and a[1] <= hi)]
                 l.append([lo, hi, q, sem, val, isw])
 
+    def issue(q, reads, writes, call):
+        deps(q, reads, writes)
+        sem = CS[q]
+        cnt[sem] += 1
+        call().then_inc(T.sem[sem], 1)
+        note(q, reads, writes, sem, cnt[sem])
+
+    def engines(src, dst, rsem):
+        use = topo.engines(src, dst)
+        if rsem in QUARTER:
+            k, n = QUARTER.index(rsem), len(use) // 4
+            use = use[k * n:k * n + n]
+        return use
+
+    def arrive(src, region, rsem):
+        name, lo, hi = region
+        l = acc.setdefault(name, [])
+        l[:] = [a for a in l if not (lo <= a[0] and a[1] <= hi)]
+        l.append([lo, hi, "r", rsem, len(engines(src, core, rsem)), True])
+
+    tasks, before = [], []
+    seen, raised, group = {}, {}, {}
+
+    now = {"wave": -1}
+
+    def task(q, run, reads, writes, dur, lat=0.0, after=(), kind="", durs=None):
+        j, pre = len(tasks), {}
+        for lst, isw in ((reads, False), (writes, True)):
+            for name, lo, hi in lst:
+                for a, b, i, w in seen.get(name, []):
+                    if (isw or w) and a < hi and lo < b:
+                        pre[i] = 0.0 if name in PS and q == "p" == tasks[i]["q"] else WAKE
+        for lst, isw in ((reads, False), (writes, True)):
+            for name, lo, hi in lst:
+                l = seen.setdefault(name, [])
+                if isw:
+                    l[:] = [a for a in l if not (lo <= a[0] and a[1] <= hi)]
+                l.append((lo, hi, j, isw))
+        if kind:
+            starts, adds = group.setdefault(writes[0][0], ([], []))
+            if kind != "add":
+                for i in adds + (starts if kind == "open" else []):
+                    pre.setdefault(i, 0.0)
+                if kind == "open":
+                    starts[:], adds[:] = [], []
+            (adds if kind in ("add", "close") else starts).append(j)
+        for i in after:
+            pre.setdefault(i, 0.0)
+        before.append([(i, d + (tasks[i]["lat"] if d else 0.0)) for i, d in pre.items()])
+        w = now["wave"]
+        like = (q, tuple(sorted({r[0][:2 if lat else 9] for r in writes})), tuple(sorted({r[0][:2 if lat else 9] for r in reads})))
+        now[like] = now.get(like, 0) + 1
+        tasks.append({"q": q, "run": run, "dur": dur, "lat": lat, "banks": sorted({r[0] for r in reads + writes if r[0] in PS}),
+                      "durs": durs or [dur] * len(CASES), "wave": w, "kind": (1 if 0 < w < RO - 1 else w, like, now[like]), "mark": ""})
+        return j
+
+    lines = {}
+
+    def inturn(line):
+        j = len(tasks) - 1
+        if line in lines and lines[line] not in [i for i, _ in before[j]]:
+            before[j].append((lines[line], 0.0))
+        lines[line] = j
+
+    def behind(line):
+        j = len(tasks) - 1
+        if lines[line] not in [i for i, _ in before[j]]:
+            before[j].append((lines[line], 0.0))
+
+    def wide(name):
+        return 4 if SCRATCH[name][2] in ("float32", "int32") else 2
+
     def A(name, lo=0, hi=None, st=1):
         if hi is None:
             hi = T[name].shape[1]
         ap = T[name][:, lo:hi] if st == 1 else T[name][:, lo:hi:st]
-        return (ap, [(name, lo, hi)], [])
+        return (ap, [(name, lo, hi)], [], len(range(lo, hi, st)), wide(name), False)
 
-    def I(win, w, off, o0, o1, a=0):
-        return (T[win][:, a:a + w].indirect(T[off][:, o0:o1]), [(win, a, a + w)], [(off, o0, o1)])
+    def I(win, a, b, off, o0, o1):
+        return (T[win][:, a:b].indirect(T[off][:, o0:o1]), [(win, a, b)], [(off, o0, o1)], 16 * (o1 - o0), wide(win), True)
 
-    def op(q, out, ins, call, outs=()):
+    def op(q, out, ins, call, per=None):
         reads, writes = list(out[2]), list(out[1])
         for x in ins:
             reads += x[1] + x[2]
-        for x in outs:
-            writes += x[1]
-        deps(q, reads, writes)
-        sem = CS[q]
-        if FORCE and q == "v" and cnt[sem]:
-            need(q, sem, cnt[sem])
-        cnt[sem] += 1
-        call().then_inc(T.sem[sem], 1)
-        note(q, reads, writes, sem, cnt[sem])
+        n, fix = out[3], {"v": 50.0, "s": 65.0, "g": 170.0}[q]
+        durs = None
+        if out[5] or ins and ins[0][5]:
+            dur = fix + n * CYC * (SCATTER if out[5] else max(GATHER, min(per or 0, TWO)))
+            durs = [fix + n * CYC * (sc if out[5] else max(ga, min(per or 0, two))) for ga, sc, two in CASES]
+        elif q == "v":
+            dur = VFIX + CYC * max(64, n * (per or (0.5 if out[4] == 2 and (not ins or ins[0][4] == 2) else 1.0)))
+        else:
+            dur = fix + (SFIX if q == "s" else 0) + n * CYC * (1 if q == "s" else 2)
+        task(q, lambda: issue(q, reads, writes, call), reads, writes, dur, durs=durs)
 
     def u(x):
         return x[0] if isinstance(x, tuple) else x
@@ -122,7 +441,8 @@ def rank_program(g, core, T, topo):
         op("v", out, [in_], lambda: g.vector.tensor_copy(out=out[0], in_=in_[0]))
 
     def tt(out, a, b, o):
-        op("v", out, [a, b], lambda: g.vector.tensor_tensor(out=out[0], in0=a[0], in1=b[0], op=o))
+        psum = a[1][0][0] in PS or b[1][0][0] in PS
+        op("v", out, [a, b], lambda: g.vector.tensor_tensor(out=out[0], in0=a[0], in1=b[0], op=o), 1.0 if psum else 2.0)
 
     def ts(out, a, s1, o0, s2=None, o1=None):
         ins = [a] + [x for x in (s1, s2) if isinstance(x, tuple)]
@@ -134,20 +454,31 @@ def rank_program(g, core, T, topo):
     def ms(out, c):
         op("v", out, [], lambda: g.vector.memset(out[0], c))
 
-    def act(out, in_, f=AFT.Copy, bias=0.0, scale=1.0, total=None):
-        if total is not None:
-            op("s", out, [in_], lambda: g.scalar.activation(out=out[0], in_=in_[0], func=f, bias=bias, scale=scale, accum_out=total[0]), [total])
-        elif bias == 0.0 and scale == 1.0:
+    def act(out, in_, f=AFT.Copy, bias=0.0, scale=1.0):
+        if bias == 0.0 and scale == 1.0:
             op("s", out, [in_], lambda: g.scalar.activation(out=out[0], in_=in_[0], func=f))
         else:
             op("s", out, [in_], lambda: g.scalar.activation(out=out[0], in_=in_[0], func=f, bias=bias, scale=scale))
 
-    def mm(out, lhsT, rhs, st, sp):
-        op("p", out, [lhsT, rhs], lambda: g.tensor.matmul(out=out[0], lhsT=lhsT[0], rhs=rhs[0], start=st, stop=sp))
+    def shift(q, out, in_, c):
+        if q == "s":
+            act(out, in_, AFT.Copy, c)
+        else:
+            ts(out, in_, c, OPS.add)
+
+    def mms(calls, kind="sum"):
+        def one(out, l, r, st, sp):
+            issue("p", l[1] + r[1], out[1], lambda: g.tensor.matmul(out=out[0], lhsT=l[0], rhs=r[0], start=st, stop=sp))
+
+        def run():
+            for c in calls:
+                one(*c)
+        dur = sum(max(min(64, c[1][3]), c[2][3]) * c[2][4] ** 2 / 4 for c in calls) * PECYC
+        task("p", run, sorted({r for c in calls for r in c[1][1] + c[2][1]}), sorted({r for c in calls for r in c[0][1]}), dur, kind=kind)
 
     def msum(out, terms, st=True, sp=True):
-        for k, (l, r) in enumerate(terms):
-            mm(out, l, r, st and k == 0, sp and k == len(terms) - 1)
+        mms([(out, l, r, st and k == 0, sp and k == len(terms) - 1) for k, (l, r) in enumerate(terms)],
+            ("sum" if sp else "open") if st else "close" if sp else "add")
 
     def io(out, pat, base, cm=0, small=True):
         if small:
@@ -155,26 +486,49 @@ def rank_program(g, core, T, topo):
         else:
             op("g", out, [], lambda: g.iota(out[0], pat, base, cm))
 
-    def gsel(out, in_, pat, base, cm):
-        op("g", out, [in_], lambda: g.affine_select(out[0], in_[0], pat, OPS.is_equal, 0.0, base, cm))
+    def gcopy(out, in_):
+        op("g", out, [in_], lambda: g.affine_select(out[0], in_[0], [[0, out[3]]], OPS.is_equal, 0.0, 0, 0))
 
-    def dma(q, out_ap, in_ap, reads, writes, sem):
-        deps(q, reads, writes)
-        Q[q].dma_start(out=out_ap, in_=in_ap).then_inc(T.sem[sem], 16)
-        note(q, reads, writes, sem, 16)
+    last_dma = {}
 
-    def load(q, name, lo, hi, src, s0, sem):
-        dma(q, T[name][:, lo:hi], src[:, s0:s0 + hi - lo], [], [(name, lo, hi)], "ld_" + sem)
+    def moves(q, run, reads, writes, sem, nbytes, waits):
+        j = task(q, run, reads + [(s, 0, 1) for s, _ in waits], writes + [(sem, 0, 1)], 60.0,
+                 1700.0 + nbytes / RATE + (ONCE if q == "g" and q not in last_dma else 0.0))
+        if q in last_dma:
+            before[j].append(last_dma[q])
+        last_dma[q] = (j, nbytes / RATE)
 
-    def send(dst, outp, inp, rsem, lsem):
-        deps("g", inp[1], [])
-        rid, pid, _ = topo.addr(dst)
-        g.remote_dma(out_ap=outp[0], in_ap=inp[0], remote_sem=T.sem[rsem], local_sem=T.sem[lsem], pid=pid, routing_id=rid,
-                     dma_engine_mask=topo.mask(core, dst))
-        note("g", inp[1], [], lsem, len(topo.engines(core, dst)))
+    def dma(q, out_ap, in_ap, reads, writes, sem, nbytes, waits=()):
+        def run():
+            for s, v in waits:
+                need(q, s, v)
+            deps(q, reads, writes)
+            Q[q].dma_start(out=out_ap, in_=in_ap).then_inc(T.sem[sem], 16)
+            note(q, reads, writes, sem, 16)
+        moves(q, run, reads, writes, sem, nbytes, waits)
 
-    def arrive(src, outp, rsem):
-        acc.setdefault(outp[1][0][0], []).append([outp[1][0][1], outp[1][0][2], "r", rsem, len(topo.engines(src, core)), True])
+    def load(q, name, lo, hi, src, s0, sem, waits=()):
+        dma(q, T[name][:, lo:hi], src[:, s0:s0 + hi - lo], [], [(name, lo, hi)], "ld_" + sem, 128 * (hi - lo) * wide(name), waits)
+
+    def send(dst, outp, inp, rsem, lsem, waits=()):
+        def run():
+            for s, v in waits:
+                need("g", s, v)
+            deps("g", inp[1], [])
+            rid, pid, _ = topo.addr(dst)
+            use = engines(core, dst, rsem)
+            g.remote_dma(out_ap=outp[0], in_ap=inp[0], remote_sem=T.sem[rsem], local_sem=T.sem[lsem], pid=pid, routing_id=rid,
+                         dma_engine_mask=sum(1 << e for e in use))
+            note("g", inp[1], [], lsem, len(use))
+        moves("g", run, inp[1], outp[1], lsem, 128 * inp[3] * inp[4], waits)
+
+    def credit(w):
+        def run():
+            deps("g", [], [("F", AG, AE)])
+            rid, pid, _ = topo.addr(prv)
+            g.remote_sem_update(T.sem["cr%d" % w], T.sem["lc"], pid, rid, 1 << topo.engines(core, prv)[0])
+            arrive(prv, ("F", AG, AE), "gh%d" % (w + 1))
+        moves("g", run, [], [("F", AG, AE)], "cr%d" % w, 0, ())
 
     def EP(p, name="EP"):
         return A(name, 15 - p, 143 - p)
@@ -182,18 +536,13 @@ def rank_program(g, core, T, topo):
     def DP(p):
         return A("DPM", 128 * p, 128 * p + 128)
 
+    sent = len(topo.engines(core, prv))
     load("y", "BW", 8, 8 + XB[1], T.xb, 0, "xb0")
     load("s", "FI", 0, S, T.f0, 0, "f0")
     load("s", "BDI", 0, 16, T.bd, 0, "bd")
-    for k in (1, 2):
+    for k in (1, 2, 3):
         load("y", "BW", 8 + XB[k], 8 + XB[k + 1], T.xb, XB[k], "xb%d" % k)
-    load("s", "NA", 0, FIRST, T.nba, 0, "nba")
-    for k in range(3):
-        arrive(nxt, A("BW", HALO + XB[k], HALO + min(XB[k + 1], NH)), "hb%d" % k)
-    for h in range(4):
-        arrive(nxt, A("HR", 512 * h, 512 * h + 512), "hn%d" % h)
-    for w in range(RO):
-        arrive(prv, A("LG%d" % w), "gh%d" % w)
+    load("s", "NA", A0, FIRST, T.nba, 0, "nba")
 
     def numbers_out(k):
         n = min(XB[k + 1], NH)
@@ -202,22 +551,21 @@ def rank_program(g, core, T, topo):
     io(A("IP"), [[0, 1]], 0, 1, False)
     io(A("XG"), [[1, 144]], -15)
     io(A("CM"), [[1, 128]], 0)
-    io(A("DD"), [[1, 80]], VA + 1)
-    io(A("IDT"), [[1, 80], [80, 16]], 64)
-    numbers_out(0)
+    io(A("JJ"), [[1, CAP]], 0)
+    io(A("XL"), [[1, 48]], -15)
+    io(A("HE"), [[16, 8]], 0)
+    for a, n in UNITS:
+        io(A("CO", a, a + n), [[0, 8], [1, 2], [0, n // 16]], 0)
+    io(A("NA", 0, A0), [[1, CAP]], -A0, 0, False)
     ms(A("ZF"), 0.0)
     ts(A("LPI"), A("IP"), 15, OPS.bitwise_and)
     ts(A("GPI"), A("IP"), 112, OPS.bitwise_and)
     cp(A("PCF"), A("IP"))
-    ms(A("IND", S, 320), 0.0)
     cp(A("GPC"), A("GPI"))
     ts(A("LPC"), A("LPI"), 1.0, OPS.add)
-    ts(A("QE"), A("LPI"), 80.0, OPS.mult)
     ts(A("IDM"), A("CM"), A("PCF"), OPS.is_equal)
     ts(A("EP"), A("XG"), A("GPC"), OPS.is_equal)
     ts(A("XH", 0, 128), A("CM"), A("GPC"), OPS.subtract)
-    ts(A("DD"), A("DD"), A("QE"), OPS.add)
-    ts(A("PH"), A("IDM"), -32768.0, OPS.mult)
     ts(A("WK"), A("XH", 0, 128), A("LPC"), OPS.is_ge)
     ts(A("SAM"), A("XH", 0, 128), 15.5, OPS.is_lt)
     ts(A("IDL"), A("IDM"), A("LPC"), OPS.mult)
@@ -226,646 +574,433 @@ def rank_program(g, core, T, topo):
     ts(A("WK"), A("XH", 0, 128), -0.5, OPS.is_gt)
     cp(A("IDH"), A("IDM"))
     tt(A("LTM"), A("WK"), A("LM"), OPS.mult)
-    for a in range(S, 1792, 320):
-        act(A("F", a, min(a + 320, 1792)), A("ZF", 0, min(320, 1792 - a)))
-    act(A("KB"), A("ZF", 0, CAP), AFT.Copy, 131072.0)
-    for k in range(2):
-        act(A("PAD", 128 * k, 128 * k + 128), A("CM"), AFT.Copy, 1536.0 + 64 + 128 * k)
-    ts(A("IND", 0, S), A("FI"), 4095.0, OPS.not_equal)
-    for q in range(4):
-        mm(A("PM", 160, 240), EP(q), A("IND", 80 * q, 80 * q + 80), q == 0, q == 3)
-    ts(A("FI"), A("FI"), 1.0, OPS.add)
-    ms(A("ONE"), 1.0)
-    ts(A("EL"), A("PM", 160, 240), 0.5, OPS.is_lt)
-    ts(A("SU"), A("PM", 160, 240), 0.5, OPS.is_gt, 64.0, OPS.mult)
-
-    def ghosts_out(w):
-        ts(A("GS"), I("F", VA, "BDU", 0, 16), -2048.0, OPS.add, 0.0, OPS.max)
-        send(nxt, A("LG%d" % w), A("GS"), "gh%d" % w, "lg%d" % w)
-
-    def extract(w):
-        dma("y", T.WC[:], T.W[0:128:16, 0:4 * VA], [("W", 0, 4 * VA)], [("WC", 0, 320)], "xf%d" % w)
-
-    def extract_b(w):
-        dma("y", T.WD[:], T.WB[0:128:16, 0:VA], [("WB", 0, VA)], [("WD", 0, 80)], "xd%d" % w)
-
-    BASE = A("PM", 256, 257)
-
-    def select_z(w):
-        msum(A("PM", 160, 240), [(A("IDH"), A("KT", 80 * w - 80, 80 * w)), (A("PG"), A("EL")), (A("PH"), A("INF")), (A("PN"), A("SU"))]
-             + [(A("IDM"), A("WC", r, 320, 4)) for r in range(4)])
-
-    def select_1():
-        tt(A("EL"), A("PM", 160, 240), A("WD"), OPS.is_gt)
-
-    def select_2():
-        op("v", A("CU"), [A("EL"), A("ZF", 0, 80)], lambda: g.vector.tensor_tensor_scan(
-            out=T.CU[:], data0=T.EL[:], data1=T.ZF[:, 0:80], initial=0.0, op0=OPS.add, op1=OPS.add))
-        msum(A("PM", 0, 80), [(A("IDM"), A("DD")), (A("PH"), A("EL"))])
-        mm(BASE, A("TRI"), A("CU", 79, 80), True, True)
-
-    def select_3():
-        tt(A("MX"), A("PM", 0, 80), A("CU"), OPS.max)
-
-    def select_4():
-        ts(A("OU"), A("MX"), BASE, OPS.add)
-
-    def pads():
-        act(A("W", FR + 1, FR + CAP + 1), A("PAD"))
-        act(A("W", FV + 1, FV + CAP + 1), A("KB"))
-
-    def select_s():
-        act(I("W", FW, "OU", VFR, 80, FR), A("IDT", 16 * VFR, VA), AFT.Silu)
-
-    def select_v():
-        cp(I("W", FW, "OU", 0, VFR, FV), A("IDT", 0, 16 * VFR))
-
-    PART = ((0, SUB, "PM"), (SUB, CAP, "PL"))
-
-    def select_p(k):
-        a, b, bank = PART[k]
-        tt(A("FH", a, b), A("W", FR + 1 + a, FR + 1 + b), A("W", FV + 1 + a, FV + 1 + b), OPS.min)
-        msum(A(bank, 272 + a // 16, 272 + b // 16), [(DP(l), A("FH", a + l, b, 16)) for l in range(16)])
-
-    def select_b(k):
-        a, b, bank = PART[k]
-        ts(A("FRL", a // 16, b // 16), A(bank, 272 + a // 16, 272 + b // 16), 64.0, OPS.subtract)
-
-    def select_x(w, k):
-        a, b, bank = PART[k]
-        act(A("XR", 16 * a, 16 * b, 16), I("AW", 1792 if w else FIRST, "FRL", a // 16, b // 16))
-
-    def select_n(w, k):
-        a, b, bank = PART[k]
-        cp(A("NAU", a, b), I("NA", 1792 if w else FIRST, "FRL", a // 16, b // 16))
-
-    def state():
-        ts(A("INF"), A("MX"), BASE, OPS.add, CAP + 0.5, OPS.is_lt)
-
-    def xrep(q, s, ks=(8, 4, 2, 1)):
-        a, b = 16 * SUB * s, 16 * SUB * s + 16 * SUB
-        for k in ks:
-            if q == "g":
-                gsel(A("XR", a + k, b, 2 * k), A("XR", a, b, 2 * k), [[0, 8 * SUB // k]], 0, 0)
-            elif q == "s":
-                act(A("XR", a + k, b, 2 * k), A("XR", a, b, 2 * k))
-            else:
-                cp(A("XR", a + k, b, 2 * k), A("XR", a, b, 2 * k))
-
-    def relay_a():
-        cp(A("Ch"), A("NAU"))
-        for h in range(2):
-            for k in range(8):
-                mm(A("PT", 32 * k + 16 * h, 32 * k + 16 * h + 16), A("Ch", 128 * h, 128 * h + 128), A("IDH", 16 * k, 16 * k + 16), True, True)
-
-    def relay_b(h0, h1):
-        for h in range(h0, h1):
-            for k in range(8):
-                out = (T.PR[32 * (k // 2):32 * (k // 2) + 32, h:256:8], [("PR", h, 256)], [])
-                a = 48 * h + 16 - 16 * (k % 2)
-                mm(out, A("ZM", a, a + 32), A("Th", 32 * k, 32 * k + 32), k % 2 == 0, k % 2 == 1)
-
-    pads()
-    select_2()
-    ts(A("FI"), A("FI"), 4095, OPS.bitwise_and)
-    select_3()
-    cp(A("F", 0, S), A("FI"))
-    select_4()
-    cp(A("BDU"), A("BDI"))
-    select_s()
-    numbers_out(1)
-    ghosts_out(0)
-    numbers_out(2)
-    select_v()
-    need("y", "ld_xb2", 16)
-    load("y", "AW", 0, FIRST, T.xa, 0, "xa")
-    need("y", "lhb0", len(topo.engines(core, prv)))
-    for h in range(4):
-        load("y", "NW", 8 + 512 * h, 8 + 512 * h + 512, T.nbb, 512 * h, "nb%d" % h)
-    dma("y", T.W[0:128:16, 0:4 * VA], T.ZF[:], [("ZF", 0, 320)], [("W", 0, 4 * VA)], "zw")
-    io(A("XL"), [[1, 48]], -15)
-    io(A("HE"), [[16, 8]], 0)
-    io(A("CO"), [[0, 4], [1, 4], [0, 8]], 0)
-    io(A("NA", 1536, 1792), [[1, CAP]], 1536, 0, False)
+    for name, c in (("IDN", -1.0), ("PN", -2048.0), ("PG", 2.0 ** 18), ("PF", 2.0), ("IDB", 1.0), ("IDC", -1.0), ("PA", 2048.0),
+                    ("PB", 4096.0), ("I6", 6.0), ("I16", 16.0), ("I112", 112.0), ("IM", -1791.0)):
+        ts(A(name), A("IDH"), c, OPS.mult)
+    ts(A("DG"), A("CM", 1, 17), A("LPC"), OPS.is_equal)
+    ts(A("NLT"), A("LTM"), -1.0, OPS.mult)
+    ts(A("D6"), A("IDL"), 6.5, OPS.is_gt, 30000.0, OPS.mult)
+    ts(A("HI", 0, 128), A("XH", 0, 128), -0.5, OPS.is_gt)
+    tt(A("SAM"), A("HI", 0, 128), A("SAM"), OPS.mult)
     for p in range(16):
         ts(DP(p), A("IDL"), float(p + 1), OPS.is_equal)
-    state()
     tt(A("WK"), A("TRI"), A("IDH"), OPS.subtract)
     tt(A("LM"), A("LTM"), A("IDH"), OPS.subtract)
-    ms(A("EC"), C3)
-    ms(A("BW", 0, 8), 1024.0)
     ts(A("TF"), A("WK"), WZ, OPS.mult)
     ts(A("TL"), A("LM"), WZ, OPS.mult)
-    select_p(0)
-    select_p(1)
-    for name, c in (("PN", -2048.0), ("PG", 32768.0), ("PF", 4.0), ("IDN", -1.0), ("IDB", 1.0), ("IDC", -1.0),
-                    ("PA", 2048.0), ("PB", 4096.0)):
-        ts(A(name), A("IDH"), c, OPS.mult)
+    ts(A("HE"), A("HE"), A("GPC"), OPS.not_equal, 1000.0, OPS.mult)
+    ts(A("EQ"), A("EP"), 2.0, OPS.mult)
+    ts(A("HE"), A("HE"), A("LPC"), OPS.add)
+    ts(A("CF"), A("LPC"), WZ, OPS.mult)
+    ts(A("CG"), A("LPC"), -WZ, OPS.mult, 17 * WZ, OPS.add)
+    for h in range(8):
+        ts(A("ZM", 48 * h, 48 * h + 48), A("XL"), A("HE", h, h + 1), OPS.is_equal)
+    for buf, c in ((A("KC"), -27.0), (A("OH"), 1.0 / 256.0), (A("ONE"), 1.0), (A("EC"), C3), (A("BW", 0, 8), 1024.0), (A("NW", 0, 8), 4095),
+                   (A("AW", 0, A0), 0.0), (A("HS", 2047, 2048), 4095)):
+        ms(buf, c)
+    act(A("F", 0, A0), A("ZF", 0, A0))
+    for a in range(A0 + S, AG, 320):
+        act(A("F", a, min(a + 320, AG)), A("ZF", 0, min(320, AG - a)))
+    act(A("KB"), A("ZF", 0, CAP), AFT.Silu, 2.0 ** 22)
     for w in range(RO - 1):
-        act(A("KA", 512 * w, 512 * w + 512), A("F", 512, 1024), AFT.Copy, STAMP[w])
+        act(A("KA", CAP * w, CAP * w + CAP), A("ZF", 0, CAP), AFT.Copy, STAMP[w])
         act(A("KT", 80 * w, 80 * w + 80), A("ZF", 0, 80), AFT.Copy, -0.875 * STAMP[w])
-    select_b(0)
 
-    def constants():
-        ts(A("HE"), A("HE"), A("GPC"), OPS.not_equal, 1000.0, OPS.mult)
-        ts(A("EQ"), A("EP"), 2.0, OPS.mult)
-        ms(A("KC"), -27.0)
-        ts(A("HE"), A("HE"), A("LPC"), OPS.add)
-        ts(A("CF"), A("LPC"), WZ, OPS.mult)
-        ts(A("CG"), A("LPC"), -WZ, OPS.mult, 17 * WZ, OPS.add)
+    def extract(w):
+        for k, a in enumerate((0, WW)):
+            dma("y", T.WC[:, 224 * k:224 * k + 224], T.W[0:128:16, a:a + 2 * AE], [("W", a, a + 2 * AE)], [("WC", 224 * k, 224 * k + 224)],
+                ("xe%d", "xf%d")[k] % w, 114688)
+
+    def extract_b(w):
+        dma("y", T.WD[:], T.WB[0:128:16, 0:AE], [("WB", 0, AE)], [("WD", 0, 112)], "xd%d" % w, 57344)
+
+    Z = A("PM", 160, 240)
+
+    def flagged(w):
+        msum(Z, [(A("IDB"), A("KT", 80 * w - 80, 80 * w)), (A("PG"), A("INF")), (A("PN"), A("SU"))], True, False)
+        for k in range(2):
+            msum(Z, [(A("IDM"), A("WC", 224 * k + 32 + r, 224 * k + 192, 2)) for r in range(2)], False, k == 1)
+            behind("count")
+        inturn("flagged")
+        tt(A("EL", 0, 80), Z, A("WD", 16, 96), OPS.is_gt)
+        behind(ELAFTER)
+
+    def ranks(w):
+        if w:
+            flagged(w)
+        col, rank, over, upto = A("PM", 0, 96), A("PM", 256, 352), A("PM", 352, 432), A("PM", 464, 480)
+        msum(col, [(A("SAM"), A("EL"))])
+        op("v", A("CU"), [col, A("ZF", 0, 96)], lambda: g.vector.tensor_tensor_scan(
+            out=T.CU[:], data0=T.PM[:, 0:96], data1=T.ZF[:, 0:96], initial=0.0, op0=OPS.add, op1=OPS.add), 1.0)
+        tt(A("SH"), A("CU", 5, 96, 6), A("DG"), OPS.mult)
+        op("v", A("T0"), [A("SH")], lambda: g.vector.tensor_reduce(out=T.T0[:], in_=T.SH[:], axis=AXL.X, op=OPS.add))
+        ts(A("CA"), A("JJ"), A("T0"), OPS.is_ge)
+        msum(upto, [(DP(i), A("CU", i, 96, 6)) for i in range(6)] + [(A("D6"), A("ONE", 0, 16))])
+        msum(rank, [(A("IDH"), A("CU")), (A("NLT"), A("EL"))])
+        shift(SQ[0], A("TA"), upto, 0.0)
+        shift(SQ[1], A("GT"), rank, 0.0)
+        if w < RO - 1:
+            msum(over, [(A("IDH"), A("CU", 0, 80)), (A("NLT"), A("EL", 0, 80)), (A("PB"), A("EL", 0, 80))])
+            ts(A("INF"), over, 4096.0 + CAP + 0.5, OPS.is_gt)
+        six, c, cell, o = A(LB, 480, 496), A(LB, 496, 512), A(LB, 480, 496), 16 * (w % 2)
+
+        def counted(out, more=()):
+            msum(out, list(more) + [(EP(l), A("CA", l, CAP, 16)) for l in range(16)])
+        counted(six)
+        cp(A("SL"), six)
+        shift(SQ[2], A("SH"), six, 0.0)
+        tt(A("CA"), I("TA", 0, 16, "SL", 0, 16), A("JJ"), OPS.is_le)
+        counted(c, [(A("I6"), A("SH"))])
+        cp(A("SL"), c)
+        shift(SQ[3], A("CC"), c, 0.0)
+        ts(A("DH"), c, 79.5, OPS.is_gt, -96.0, OPS.mult)
+        tt(A("CA"), I("GT", 0, 96, "SL", 0, 16), A("JJ"), OPS.is_le)
+        counted(cell, [(A("I16"), A("CC")), (A("I16"), A("DH"))])
+        ts(A("FRL", o, o + 16), cell, float(A0), OPS.add)
+        shift(SQ[4], A("FH"), cell, float(A0))
+
+    def front(w):
+        end, o = AG if w else FIRST, 16 * (w % 2)
+        for a, b in ((0, SUB), (SUB, CAP)):
+            act(A("XR", 16 * a, 16 * b, 16), I("AW", 0, end, "FRL", o + a // 16, o + b // 16))
+            ts(A("NAU", a, b), I("NA", 0, end, "FRL", o + a // 16, o + b // 16), float(A0), OPS.add)
+
+    def xrep(q, s, k, n=1):
+        a, b = 16 * SUB * s, 16 * SUB * (s + n)
+        (gcopy if q == "g" else cp)(A("XR", a + k, b, 2 * k), A("XR", a, b, 2 * k))
+
+    def relay():
+        cp(A("Ch"), A("NAU"))
+        ts(A("HI"), A("NAU"), 1.0 / 16, OPS.mult, 1536.0 - 7.5 / 16, OPS.add)
+        for h in range(2):
+            mms([(A("PT", 32 * k + 16 * h, 32 * k + 16 * h + 16), A(x, 128 * h, 128 * h + 128), A(y, 16 * k, 16 * k + 16), x == "Ch", x == "HI")
+                 for k in range(8) for x, y in (("Ch", "I112"), ("HI", "IM"))])
+        act(A("Th"), A("PT", 0, 256), AFT.Copy, 1791.0 * 1536)
         for h in range(8):
-            ts(A("ZM", 48 * h, 48 * h + 48), A("XL"), A("HE", h, h + 1), OPS.is_equal)
-        ms(A("OH"), 1.0 / 256.0)
-        ms(A("NW", 0, 8), 4095)
-        ms(A("AW", 1536, 1792), 0.0)
+            mms([((T.PR[32 * (k // 2):32 * (k // 2) + 32, h:256:8], [("PR", 0, 256)]), A("ZM", 48 * h + 16 - 16 * (k % 2), 48 * h + 48 - 16 * (k % 2)),
+                  A("Th", 32 * k, 32 * k + 32), k % 2 == 0, k % 2 == 1) for k in range(8)])
+        act(A("LP"), A("PR", 0, 256))
 
-    def late_loads():
-        need("y", "lhn3", len(topo.engines(core, prv)))
-        dma("y", T.WB[0:128:16, 0:VA], T.ZF[0:32, :], [("ZF", 0, 320)], [("WB", 0, VA)], "zb")
-        load("y", "NA", FIRST, VA, T.nba, FIRST, "nba2")
-        load("y", "AW", FIRST, VA, T.xa, FIRST, "xa2")
+    def ghosts_out(w):
+        if SQ[5] == "s":
+            act(A("GS"), I("F", A0, AG, "BDU", 0, 16), AFT.Relu, -2048.0)
+        else:
+            ts(A("GS"), I("F", A0, AG, "BDU", 0, 16), -2048.0, OPS.add, 0.0, OPS.max)
+        send(nxt, A("F", AG, AE), A("GS"), "gh%d" % w, "lg%d" % w, [("cr%d" % (w - 1), 1)] if w else [])
 
-    def halo_out(h):
+    numbers_out(0)
+    ts(A("IND"), A("FI"), 4095.0, OPS.not_equal)
+    some = A("PM", 160, 160 + S // 16)
+    msum(some, [(EP(q), A("IND", q, S, 16)) for q in range(16)])
+    ts(A("EL", 0, S // 16), some, 0.5, OPS.is_lt)
+    ts(A("SU", 0, S // 16), some, 0.5, OPS.is_gt, 1024.0, OPS.mult)
+    ms(A("EL", S // 16, 96), 1.0)
+    ms(A("SU", S // 16, 80), 0.0)
+    ts(A("FI"), A("FI"), 1.0, OPS.add)
+    ts(A("FI"), A("FI"), 4095, OPS.bitwise_and)
+    cp(A("F", A0, A0 + S), A("FI"))
+    cp(A("BDU"), A("BDI"))
+    numbers_out(1)
+    numbers_out(2)
+    ghosts_out(0)
+    numbers_out(3)
+    op("v", (T.BW[:, 4103:4104], [("BW", 4096, 4104)], [], 1, 2, False), [], lambda: g.vector.memset(T.BW[:, 4103:4104], 1024.0))
+    load("y", "AW", A0, FIRST, T.xa, 0, "xa", [("ld_xb3", 16)])
+    for h in range(4):
+        load("y", "NW", 8 + 512 * h, 8 + 512 * h + 512, T.nbb, 512 * h, "nb%d" % h, [("lhb0", len(engines(core, prv, "hb0")))])
+    for k, a in enumerate((0, WW)):
+        dma("y", T.W[0:128:16, a:a + 2 * AE], T.ZF[:, 0:224], [("ZF", 0, 224)], [("W", a, a + 2 * AE)], "zw%d" % k, 114688)
+    for h in range(4):
         a = 512 * h
         ts(A("HS", a, a + 512 - h // 3), A("NW", 8 + a, 8 + a + 512 - h // 3), 2047.0, OPS.min, 2048.0, OPS.add)
-        send(prv, A("HR", a, a + 512), A("HS", a, a + 512), "hn%d" % h, "lhn%d" % h)
-
-    def halo_in(h):
-        a = 512 * h
-        cp(A("NW", HALO + a, HALO + a + 512), A("HR", a, a + 512))
+        send(prv, A("NW", HALO + a, HALO + a + 512), A("HS", a, a + 512), "hn%d" % h, "lhn%d" % h)
+    dma("y", T.WB[0:128:16, 0:AE], T.ZF[:, 0:112], [("ZF", 0, 112)], [("WB", 0, AE)], "zb", 57344, [("lhn3", sent)])
+    load("y", "NA", FIRST, AG, T.nba, FIRST - A0, "nba2")
+    load("y", "AW", FIRST, AG, T.xa, FIRST - A0, "xa2")
+    act(A("YF", A0, AG), A("AW", A0, AG), AFT.Copy, 256.0)
 
     def cb(t, X):
         return A("CB", 256 * t + CH * X, 256 * t + CH * X + CH)
 
-    def vv(t, X, l=0, st=1):
-        return A("VV", 256 * t + CH * X + l, 256 * t + CH * X + CH, st)
+    def vv(t, X):
+        return A("VV", 256 * t + CH * X, 256 * t + CH * X + CH)
 
     def pq(X, k, n=1):
         return A("PQ%d" % X, CH * k, CH * (k + n))
 
-    def sbank(s):
-        return A(("PC0", "PQ0", "PC1", "PQ1")[s], 384, 384 + SUB)
-
     def seeds(s):
-        a = SUB * s
-        if s == 0 and VSEED:
-            ts(A("SG", 0, 16 * VSEED), I("F", 1792, "NAU", 0, VSEED), -2048.0, OPS.add)
-            a = VSEED
-        act(A("SG", 16 * a, 16 * SUB * (s + 1)), I("F", 1792, "NAU", a, SUB * (s + 1)), AFT.Copy, -2048.0)
-
-    def diag(s):
-        a = SUB * s
-        for p in range(16):
-            mm(sbank(s), DP(p), A("SG", 16 * a + p, 16 * a + 1024, 16), p == 0, p == 15)
-
-    def slist(s):
-        if s == 3:
-            act(A("CL", SUB * s, SUB * s + SUB), sbank(s), AFT.Copy, 2048.0 + OFF)
-        else:
-            ts(A("CL", SUB * s, SUB * s + SUB), sbank(s), 2048.0 + OFF, OPS.add)
+        a, b, out = SUB * s, SUB * s + SUB, A(("PC0", "PQ0", "PC1", "PQ1")[s], 384, 384 + SUB)
+        m = a + (VSEED if s == 0 else 0)
+        if m > a:
+            ts(A("SG", 16 * a, 16 * m), I("F", 0, AE, "NAU", a, m), -2048.0, OPS.add)
+        act(A("SG", 16 * m, 16 * b), I("F", 0, AE, "NAU", m, b), AFT.Copy, -2048.0)
+        inturn("s")
+        tasks[-1]["mark"] = "seeds"
+        msum(out, [(DP(p), A("SG", 16 * a + p, 16 * b, 16)) for p in range(16)])
+        shift("s" if s == 3 else "v", A("CL", a, b), out, 2048.0 + OFF)
 
     def numbers(t, X):
-        if t == 0:
-            act(cb(t, X), A("CL", CH * X, CH * X + CH), AFT.Copy, -2048.0 - OFF)
+        shift(NUMQ[t], cb(t, X), A("CL", CH * X, CH * X + CH), -2048.0 - OFF)
+
+    turn = [0]
+
+    def compare(t, X, share, banks, between):
+        top = CH - 32 * share
+        for what, lo, hi in PIECES[0 if t + X == 0 else 1 if t == 0 else 2]:
+            a, b = CH * X + lo, CH * X + min(hi, top)
+            if a < b and what == "g":
+                tt(A("D", 16 * a, 16 * b), I("BW", 0, 4104, "CL", a, b), A("XR", 16 * a, 16 * b), OPS.subtract)
+                inturn("v")
+            elif a < b:
+                ts(A("D", 16 * a, 16 * b), A("D", 16 * a, 16 * b), A("EC"), OPS.add, A("EC"), OPS.is_equal)
+                inturn("v")
+                inturn("own test")
+                tasks[-1]["mark"] = "test" if t + X == 0 else ""
+        between()
+        for a in range(CH * X + top, CH * X + CH, 32):
+            turn[0] += 1
+            bank, got = A(banks[turn[0] % 2]), A("SG", 2560 + 512 * (turn[0] % 3), 3072 + 512 * (turn[0] % 3))
+            act(got, I("BW", 0, 4104, "CL", a, a + 32))
+            inturn("s")
+            msum(bank, [(A("IDC"), A("XR", 16 * a, 16 * a + 512))], True, False)
+            msum(bank, [(A("IDH"), got)], False, True)
+            if OUFIRST and banks[1] == "PT" and t == 2 and X:
+                behind("flagged")
+            ts(A("D", 16 * a, 16 * a + 512), bank, A("EC"), OPS.add, A("EC"), OPS.is_equal)
+            inturn("v")
+            if a == CH * X + top:
+                inturn("first test")
+        for lo, n in ENDS[X] if t == 2 and len(ENDS[X]) > 1 else ((0, SUB), (SUB, SUB)):
+            a = 16 * (CH * X + lo)
+            msum(A("PC%d" % X, lo, lo + n), [(A("IDH"), A("KC", 0, n))] + [(EP(p, "EQ"), A("D", a + p, a + 16 * n, 16)) for p in range(16)])
+        if t == 2 and KB_LATE:
+            behind("kept%d" % X)
+        if X == 0:
+            inturn("count")
+
+    def sign(t, a, n):
+        out, in_ = A("VV", 256 * t + a, 256 * t + a + n), A("PC%d" % (a // CH), a % CH, a % CH + n)
+        if SIGNQ[2 * t + a // CH] == "s":
+            act(out, in_, AFT.Sign)
         else:
-            ts(cb(t, X), A("CL", CH * X, CH * X + CH), -2048.0 - OFF, OPS.add)
-
-    def G(X, lo, hi):
-        a, b = CH * X + lo, CH * X + hi
-        tt(A("D", 16 * a, 16 * b), I("BW", 4104, "CL", a, b), A("XR", 16 * a, 16 * b), OPS.subtract)
-
-    def H(X, s, n=SUB):
-        a = 16 * (CH * X + SUB * s)
-        ts(A("D", a, a + 16 * n), A("D", a, a + 16 * n), A("EC"), OPS.add, A("EC"), OPS.is_equal)
-
-    def Gs(X, k):
-        a, b = CH * X + 32 * k, 2560 + 512 * (k - 1)
-        act(A("SG", b, b + 512), I("BW", 4104, "CL", a, a + 32))
-
-    def Gp(X, k, odd="PM"):
-        a, b = CH * X + 32 * k, 2560 + 512 * (k - 1)
-        msum(A(("PR", odd)[k % 2]), [(A("IDC"), A("XR", 16 * a, 16 * a + 512)), (A("IDH"), A("SG", b, b + 512))])
-
-    def Hs(X, k, odd="PM"):
-        a = 16 * (CH * X + 32 * k)
-        ts(A("D", a, a + 512), A(("PR", odd)[k % 2]), A("EC"), OPS.add, A("EC"), OPS.is_equal)
-
-    def count(X, s, n=SUB):
-        a, o = 16 * (CH * X + SUB * s), A("PC%d" % X, SUB * s, SUB * s + n)
-        msum(o, [(A("IDH"), A("KC", 0, n))] + [(EP(p, "EQ"), A("D", a + p, a + 16 * n, 16)) for p in range(16)])
-
-    def sign(t, X, q=None):
-        if (q or VVE[2 * t + X]) == "s":
-            act(vv(t, X), A("PC%d" % X, 0, CH), AFT.Sign)
-        else:
-            ts(vv(t, X), A("PC%d" % X, 0, CH), -1.0, OPS.max, 1.0, OPS.min)
-
-    def rank_p(t, X):
-        msum(pq(X, 0), [(A("IDH"), cb(t, X)), (A("TL" if t else "TF"), vv(t, X))])
+            ts(out, in_, -1.0, OPS.max, 1.0, OPS.min)
 
     def choose(t, X):
         a = CH * X
+        msum(pq(X, 0), [(A("IDH"), cb(t, X)), (A("TL" if t else "TF"), vv(t, X))])
         ts(A("SC", a, a + CH), pq(X, 0), A("CG" if t else "CF"), OPS.add, THR, OPS.min)
         msum(A("PL", 16 * t + 8 * X, 16 * t + 8 * X + 8), [(A("PB"), A("ONE", 0, 8))] * (2 - t)
              + [(EP(l), A("SC", a + l, a + CH, 16)) for l in range(16)])
 
-    def blist(t, X):
+    def onward(t, X):
         lo = 8 * X
         ts(A("UL", lo, lo + 8), A("PL", 16 * t + lo, 16 * t + lo + 8), 2048.0 + OFF - 15 * THR - 4096.0 * (2 - t), OPS.add, 4103.0, OPS.min)
+        ts(A("CL", CH * X, CH * X + CH), I("NW", 0, 4104, "UL", lo, lo + 8), 8.0, OPS.add)
+        numbers(t + 1, X)
 
-    def nbg(X):
-        lo = 8 * X
-        ts(A("CL", CH * X, CH * X + CH), I("NW", 4104, "UL", lo, lo + 8), 8.0, OPS.add)
-
-    def relu(t, X):
-        o = A("AB", 256 * X, 256 * X + 256)
-        if KE[2 * t + X] == "s":
-            act(o, pq(X, 1, 2), AFT.Relu, -2048.0)
+    def relu(t, X, out, in_):
+        if KEEPQ[2 * t + X] == "s":
+            act(out, in_, AFT.Relu, -2048.0)
         else:
-            ts(o, pq(X, 1, 2), -2048.0, OPS.add, 0.0, OPS.max)
+            ts(out, in_, -2048.0, OPS.add, 0.0, OPS.max)
 
-    def keep_a(X, idn):
+    def keep(X, idn):
         msum(pq(X, 1), [(idn, cb(0, X)), (A("PA"), vv(0, X)), (A("PN"), vv(1, X))])
         msum(pq(X, 2), [(idn, cb(1, X)), (A("PB"), vv(1, X))])
 
-    def keep_b(X):
-        a = 256 * X
-        msum(pq(X, 1), [(A("IDM"), A("AB", a, a + CH)), (A("IDM"), A("AB", a + CH, a + 2 * CH))], True, False)
+    def back(X, lo, n):
+        a = 256 * X + lo
+        msum(A("PQ%d" % X, CH + 2 * lo, CH + 2 * lo + n), [(A("IDM"), A("AB", a, a + n)), (A("IDM"), A("AB", a + CH, a + CH + n))], True, False)
 
-    def keep_c(X, idn):
-        mm(pq(X, 1), A("PN"), vv(2, X), False, True)
-        msum(pq(X, 2), [(idn, cb(2, X)), (A("PB"), vv(2, X))])
+    def kept(X):
+        relu(1, X, A("AB", 256 * X, 256 * X + 256), pq(X, 1, 2))
+        if KEEPQ[2 + X] == "s":
+            inturn("s")
+        back(X, *ENDS[X][0])
+        inturn("kept%d" % X)
 
-    def store(w, X, between=None):
-        a = 256 * X
-        old, new = A("AB", a, a + CH), A("AB", a + CH, a + 2 * CH)
+    def store(w, X, lo, n, idn):
+        a, b, c, o = CH + 2 * lo, 256 * X + 2 * lo, 512 + CH * X + lo, 16 * (w % 2) + 8 * X + lo // 16
+        if lo:
+            back(X, lo, n)
+        sign(2, CH * X + lo, n)
+        msum(A("PQ%d" % X, a, a + n), [(A("PN"), A("VV", c, c + n))], False, True)
+        msum(A("PQ%d" % X, a + n, a + 2 * n), [(idn, A("CB", c, c + n)), (A("PB"), A("VV", c, c + n))])
+        relu(2, X, A("AC", b, b + 2 * n), A("PQ%d" % X, a, a + 2 * n))
+        old, new = A("AC", b, b + n), A("AC", b + n, b + 2 * n)
         if w < RO - 1:
-            tt(I("F", 1792, "FRL", 8 * X, 8 * X + 8), old, new, OPS.add)
+            tt(I("F", 0, AG, "FRL", o, o + n // 16), old, new, OPS.add)
         else:
             ts(old, old, -1.0, OPS.mult, 4095.0, OPS.add)
-            between()
-            tt(I("YW", 1792, "FRL", 8 * X, 8 * X + 8), old, new, OPS.subtract)
+            tt(I("YW", 0, AG, "FRL", o, o + n // 16), old, new, OPS.subtract)
 
-    pend = []
-
-    def drain(n):
-        for _ in range(min(n, len(pend))):
-            pend.pop(0)()
-
-    def fails_p(X):
-        msum(A("PL", 48 + 8 * X, 56 + 8 * X), [(EP(l), vv(0, X, l, 16)) for l in range(16)])
-
-    def fails_s(w, X):
-        lo, hi, a = 8 * X, 8 * X + 8, CH * X
-        if X:
-            ts(A("FA", lo, hi), A("PL", 48 + lo, 48 + hi), -15.0, OPS.is_lt, 1792.0, OPS.mult)
+    def fails(w, a, n):
+        lo, hi, kk = a // 16, (a + n) // 16, n // 16
+        msum(A("PT", 272 + lo, 272 + hi), [(EP(l), A("VV", a + l, a + n, 16)) for l in range(16)])
+        if a >= CH:
+            ts(A("FA", lo, hi), A("PT", 272 + lo, 272 + hi), -15.0, OPS.is_lt, 1792.0, OPS.mult)
         else:
-            act(A("FA", lo, hi), A("PL", 48 + lo, 48 + hi), AFT.Relu, -896.0 * 14, -896.0)
-
-    def fails_m(w, X):
-        lo, hi, a = 8 * X, 8 * X + 8, CH * X
+            act(A("FA", lo, hi), A("PT", 272 + lo, 272 + hi), AFT.Relu, -896.0 * 14, -896.0)
         if w < RO - 1:
-            msum(A("PR", a, a + CH), [(A("PF"), A("LP", a, a + CH)), (A("IDH"), A("CO"))], True, False)
-            for p in range(16):
-                mm(A("PR", a + 8 * p, a + 8 * p + 8), A("PF"), A("FA", lo, hi), False, p == 15)
-        if X:
-            msum(A("PT", 256, 272), [(DP(l), A("FH", l, CAP, 16)) for l in range(16)] + [(A("IDH"), A("FA"))])
+            for p0, p1 in ((0, EARLY), (EARLY, 16)) if a == 0 and EARLY else ((0, 16),):
+                c0, c1 = a + kk * p0, a + kk * p1
+                msum(A("PR", c0, c1), [(A("PF"), A("LP", c0, c1)), (A("IDH"), A("CO", c0, c1))], True, False)
+                mms([(A("PR", a + kk * p, a + kk * p + kk), A("PF"), A("FA", lo, hi), False, p == p1 - 1) for p in range(p0, p1)], "close")
+                act(A("LU", a + kk * p0, a + kk * p1), A("PR", a + kk * p0, a + kk * p1))
+            flags(w, a, n, 0, 8 if a < CH else MID)
 
-    def fails_l(w, X):
-        a = CH * X
+    def flags(w, a, n, m0, m1):
+        for m in range(m0, m1):
+            b, c = a + n // 8 * m, a + n // 8 * (m + 1)
+            if a == 0 and m in VTAKES:
+                cp(I("W", WW * (m % 2), WW * (m % 2) + WW, "LU", b, c), A("KA", CAP * w, CAP * w + 2 * n))
+            else:
+                act(I("W", WW * (m % 2), WW * (m % 2) + WW, "LU", b, c), A("KA", CAP * w, CAP * w + 2 * n), AFT.Silu)
+                inturn("s")
+
+    def successes(w):
+        o = 16 * (w % 2)
+        msum(A("PT", 256, 272), [(A("IDH"), A("FH")), (A("IDH"), A("FA"))])
+        shift(LSQ, A("LSU", o, o + 16), A("PT", 256, 272), 0.0)
         if w < RO - 1:
-            act(A("LU", a, a + CH), A("PR", a, a + CH))
-            for m in range(4):
-                pend.append(lambda m=m: act(I("W", 14336, "LU", a + 32 * m, a + 32 * m + 32), A("KA", 512 * w, 512 * w + 512), AFT.Silu))
+            msum(A("PT", 304, 320), [(A("I112"), A("FH")), (A("IM"), A("CC")), (A("IM"), A("DH")), (A("IDH"), A("FA"))])
+            shift(LSQ, A("LSP"), A("PT", 304, 320), -1791.0 * 16)
+            msum(A("PT", 300, 301), [(A("OH"), A("FA", k, k + 1)) for k in range(16)])
+            shift(NUMQ[3], A("EI"), A("PT", 300, 301), 0.0)
+            ts(A("EO"), A("EI"), 1, OPS.bitwise_and)
 
-    def fails_b(w):
-        a = 16 * (w % 2)
-        act(A("LSU", a, a + 16), A("PT", 256, 272), AFT.Copy, -64.0)
+    def last_flags(w):
+        if WBQ == "v":
+            cp(I("WB", 0, 3584, "LSP", 0, 16), A("KB"))
+            extract_b(w + 1)
+        if WBQ == "e":
+            act(I("WB", 0, 3584, "LSP", 0, 16), A("KB"), AFT.Silu)
+            inturn("s")
+            extract_b(w + 1)
+        flags(w, CH, CH, MID, 8)
+        extract(w + 1)
+        if WBQ == "s":
+            act(I("WB", 0, 3584, "LSP", 0, 16), A("KB"), AFT.Silu)
+            inturn("s")
+            extract_b(w + 1)
 
-    def full(w):
-        act(I("WB", 3584, "LSU", 16 * (w % 2), 16 * (w % 2) + 16), A("KB"), AFT.Silu)
-        extract_b(w + 1)
+    moved, laid = [], []
 
-    xs = A("XR", 0, 4096, 16)
-
-    def update(lo, hi):
-        a, b = 16 * lo, 16 * hi
-        x = A("XR", 16 * a, 16 * b, 16)
-        return [lambda: tt(A("TI", lo, hi), A("PL", 32 + lo, 32 + hi), A("KM", lo, hi), OPS.min),
-                lambda: ts(A("TM", lo, hi), A("TI", lo, hi), 4095, OPS.bitwise_and),
-                lambda: ts(A("UF", lo, hi), A("TM", lo, hi), float(OFF), OPS.add),
-                lambda: tt(A("DX", a, b), I("BW", 4104, "UF", lo, hi), x, OPS.subtract),
-                lambda: ts(A("DC", a, b), A("DX", a, b), -2.0, OPS.max, 2.0, OPS.min),
-                lambda: tt(I("YA", 3584, "LSU", 16 + lo, 16 + hi), A("DC", a, b), x, OPS.add)]
-
-    def move_a():
-        act(A("DX"), I("BW", 4104, "UF", 0, 16))
-        msum(A("PT", CAP, 2 * CAP), [(A("IDC"), A("XS")), (A("IDB"), A("DX"))])
-
-    def move_b():
-        act(A("DX"), A("PT", CAP, 2 * CAP), AFT.Relu, 2.0)
-        act(A("DC"), A("PT", CAP, 2 * CAP), AFT.Relu, -2.0)
-
-    def move_c():
-        msum(A("PT", 0, CAP), [(A("IDB"), A("DX")), (A("IDC"), A("DC")), (A("IDB"), A("XS"))])
-        act(A("XN"), A("PT", 0, CAP), AFT.Copy, 254.0)
-
-    def move_d(w):
-        act(I("YF", 3584, "LSU", 16 * (w % 2), 16 * (w % 2) + 16), A("XN"), AFT.Silu)
+    def update(w, lo, hi):
+        a, b, o = 16 * lo, 16 * hi, 16 * (w % 2)
+        x = A("XR", 16 * a, 16 * b, 16) if w == RO - 1 else A("XS", 16 * o + a, 16 * o + b)
+        shift(SQ[6], A("KY", lo, hi), A("PL", lo, hi), 0.0)
+        tt(A("KM", lo, hi), A("PL", 16 + lo, 16 + hi), A("KY", lo, hi), OPS.min)
+        tt(A("TI", lo, hi), A("PL", 32 + lo, 32 + hi), A("KM", lo, hi), OPS.min)
+        ts(A("TM", lo, hi), A("TI", lo, hi), 4095, OPS.bitwise_and)
+        ts(A("UF", lo, hi), A("TM", lo, hi), float(OFF), OPS.add)
+        def move():
+            d, new = A(MB, 0, CAP), A(MB, 0, CAP)
+            act(A("DB"), I("BW", 0, 4104, "UF", lo, hi))
+            if w < RO - 2:
+                inturn("s")
+            msum(d, [(A("IDC"), x), (A("IDB"), A("DB"))])
+            act(A("DB"), d, AFT.Relu, 2.0)
+            act(A("DC"), d, AFT.Relu, -2.0)
+            msum(new, [(A("IDB"), A("DB")), (A("IDC"), A("DC")), (A("IDB"), x)])
+            act(A("XN"), new, AFT.Copy, 254.0)
+            act(I("YF", 0, 3584, "LSU", o, o + 16), A("XN"), AFT.Silu)
+            if w < RO - 2:
+                inturn("s")
+        if w < RO - 1:
+            moved.append(move)
+            return
+        tt(A("DB", a, b), I("BW", 0, 4104, "UF", lo, hi), x, OPS.subtract)
+        ts(A("DC", a, b), A("DB", a, b), -2.0, OPS.max, 2.0, OPS.min)
+        tt(I("YA", 0, 3584, "LSU", o + lo, o + hi), A("DC", a, b), x, OPS.add)
 
     def moved_out():
-        return [lambda: act(A("YF", 0, VA), A("YF", 0, VA), AFT.Copy, 1.5 * 2.0 ** 23 - 256.0),
-                lambda: act(A("YA", 0, VA), A("YF", 0, VA), AFT.Copy, -1.5 * 2.0 ** 23)]
-
-    def parity_p():
-        msum(A("PM", 300, 301), [(A("OH"), A("FA", k, k + 1)) for k in range(16)])
-
-    parity = [lambda: act(A("EI"), A("PM", 300, 301)),
-              lambda: ts(A("EO"), A("EI"), 1, OPS.bitwise_and),
-              lambda: act(A("EC"), A("EO"), AFT.Copy, C3, -8.0)]
+        act(A("YF", A0, AG), A("YF", A0, AG), AFT.Copy, 1.5 * 2.0 ** 23 - 256.0)
+        act(A("YA", A0, AG), A("YF", A0, AG), AFT.Copy, -1.5 * 2.0 ** 23)
 
     def old_out():
-        def piece(a, b):
+        act(A("SG", 0, VA), A("F", A0, AG), AFT.Copy, -2048.0)
+        act(A("SG", VA, 2 * VA), A("F", A0, AG), AFT.Relu, 1.0, -1.0)
+        for a, b in ((0, 512), (512, 1024), (1024, VA)):
             msum(A("PT", 0, b - a), [(A("IDH"), A("SG", a, b)), (A("PB"), A("SG", VA + a, VA + b))])
-            act(A("YW", a, b), A("PT", 0, b - a), AFT.Copy, 2047.0)
-        return [lambda: act(A("SG", 0, VA), A("F", 0, VA), AFT.Copy, -2048.0),
-                lambda: act(A("SG", VA, 2 * VA), A("F", 0, VA), AFT.Relu, 1.0, -1.0),
-                lambda: piece(0, 512), lambda: piece(512, 1024), lambda: piece(1024, VA)]
+            act(A("YW", A0 + a, A0 + b), A("PT", 0, b - a), AFT.Copy, 2047.0)
 
-    def HC(X, s):
-        H(X, s)
-        count(X, s)
-
-    def slot_last(t, X):
-        Y, idn = 1 - X, A("IDN")
-        G(Y, 0, 32)
-        sign(t, X)
-        Gp(Y, 2)
-        rank_p(t, X)
-        if t == 0:
-            fails_p(1)
-        G(Y, 32, 64)
-        choose(t, X)
-        Gp(Y, 3)
-        if t:
-            keep_a(X, idn)
-            relu(1, X)
-        Hs(Y, 2)
-        HC(Y, 0)
-        if t == 0 and X:
-            fails_s(RO - 1, 1)
-            fails_m(RO - 1, 1)
-            fails_b(RO - 1)
-        blist(t, X)
-        Hs(Y, 3)
-        nbg(X)
-        count(Y, 1)
-        if t:
-            keep_b(X)
-        if t and X:
-            cp(A("KY"), A("PL", 0, 16))
-        numbers(t + 1, X)
-        Gs(X, 2)
-        Gs(X, 3)
-        drain(1 if t and X else 2)
-        if t and X:
-            tt(A("KM"), A("PL", 16, 32), A("KY"), OPS.min)
-
+    ranks(0)
     for w in range(RO):
         last = w == RO - 1
-        more = (lambda f, *a: None) if last else (lambda f, *a: f(*a))
         idn = A("IDN") if last else A("IDH")
-        select_x(w, 0)
-        select_n(w, 0)
-        select_b(1)
-        if w == 0:
-            ms(A("HS", 2047, 2048), 4095)
-            constants()
-        act(A("F", VA, VA + 256), A("LG%d" % w))
-        select_x(w, 1)
-        xrep("g", 1)
-        xrep("g", 2)
-        xrep("v", 0, (8,))
-        seeds(0)
-        diag(0)
-        select_n(w, 1)
-        xrep("v", 0, (4,))
-        more(relay_a)
-        xrep("v", 0, (2,))
-        if w:
-            update(0, 16)[2]()
-        xrep("v", 0, (1,))
-        seeds(1)
-        more(act, A("Th"), A("PT", 0, 256))
-        if w == 0:
-            op("v", (T.BW[:, 4103:4104], [("BW", 4096, 4104)], []), [], lambda: g.vector.memset(T.BW[:, 4103:4104], 1024.0))
-        slist(0)
-        G(0, 0, 64)
-        diag(1)
-        seeds(2)
-        more(relay_b, 0, 5)
-        slist(1)
-        if w == 0:
-            halo_out(0)
-        HC(0, 0)
-        G(0, 64, 128)
-        if w == 0:
-            halo_out(1)
-        diag(2)
-        seeds(3)
-        more(relay_b, 5, 8)
-        xrep("s", 3, (8,))
-        numbers(0, 0)
-        xrep("s", 3, (4,))
-        more(act, A("LP"), A("PR", 0, 256))
-        xrep("s", 3, (2,))
-        slist(2)
-        diag(3)
-        slist(3)
-        HC(0, 1)
-        if w == 0:
-            halo_out(2)
-        for slot in range(4):
-            t, X = slot // 2, slot % 2
-            if slot == 0:
-                sign(0, 0)
-                xrep("s", 3, (1,))
-                numbers(0, 1)
-                fails_p(0)
-                rank_p(0, 0)
-                fails_s(w, 0)
-                fails_m(w, 0)
-                fails_l(w, 0)
-                if last:
-                    old, moved = old_out(), moved_out()
-                    pend.extend([move_a, old[0], move_b, old[1], lambda: (move_c(), move_d(RO - 2)), moved[0], old[2], moved[1],
-                                 old[3], old[4]])
-                    drain(2)
-            elif last:
-                slot_last(t, X)
-                continue
-            G(1 - X, 0, 48 if slot else 64)
-            if slot == 0:
-                if w == 0:
-                    halo_out(3)
-                    late_loads()
-            else:
-                sign(t, X)
-                if slot == 1:
-                    fails_p(1)
-                rank_p(t, X)
-            G(1 - X, 48 if slot else 64, 80)
-            if slot == 1:
-                fails_s(w, 1)
-            choose(t, X)
-            if slot == 1:
-                fails_m(w, 1)
-                drain(4)
-                fails_l(w, 1)
-                fails_b(w)
-            if t:
-                keep_a(X, idn)
-            G(1 - X, 80, 128)
-            blist(t, X)
-            HC(1 - X, 0)
-            if w == 0 and slot == 0:
-                HC(1, 1)
-                for h in range(4):
-                    halo_in(h)
-            nbg(X)
-            if last:
-                Gs(0, 2)
-                Gs(0, 3)
-                drain(2)
-            if w or slot:
-                HC(1 - X, 1)
-            if slot == 2:
-                more(parity_p)
-            numbers(t + 1, X)
+        now.clear()
+        now["wave"], turn[0] = w, 0
+        front(w)
+        for q, s, k, n in (("v", 0, 8, 1), ("v", 0, 4, 1), ("v", 0, 2, 1), ("v", 0, 1, 1), ("v", 1, 8, 1), ("v", 1, 4, 1), ("g", 2, 8, 2),
+                           ("g", 1, 2, 1), ("g", 2, 4, 2), ("g", 1, 1, 1), ("g", 2, 2, 1), ("g", 3, 2, 1), ("g", 2, 1, 1), ("g", 3, 1, 1)):
+            xrep(q, s, k, n)
+        for s in range(4):
+            seeds(s)
         if last:
-            break
-        drain(99)
-        more(extract, w + 1)
-        more(full, w)
-        relu(1, 0)
-        keep_b(0)
-        sign(2, 0)
-        keep_c(0, idn)
-        rank_p(2, 0)
-        relu(1, 1)
-        keep_b(1)
-        if w:
-            move_a()
-        parity[0]()
-        relu(2, 0)
-        act(A("KY"), A("PL", 0, 16))
-        if w:
-            move_b()
-        more(pads)
-        if w == 0:
-            act(A("YF", 0, VA), A("AW", 0, VA), AFT.Copy, 256.0)
-        G(1, 0, 128)
-        parity[1]()
-        select_z(w + 1)
-        if w:
-            move_c()
-            move_d(w - 1)
-        HC(1, 0)
-        if ORDER == 2:
-            HC(1, 1)
-            select_1()
-            tt(A("KM"), A("PL", 16, 32), A("KY"), OPS.min)
-            select_2()
-            store(w, 0)
-            sign(2, 1)
-            select_3()
-            keep_c(1, idn)
-            rank_p(2, 1)
-            choose(2, 0)
-            select_4()
-            parity[2]()
-            select_s()
-            state()
-        elif ORDER == 0:
-            select_1()
-            H(1, 1)
-            select_2()
-            count(1, 1)
-            store(w, 0)
-            select_3()
-            tt(A("KM"), A("PL", 16, 32), A("KY"), OPS.min)
-            select_4()
-            parity[2]()
-            select_s()
-            sign(2, 1)
-            keep_c(1, idn)
-            rank_p(2, 1)
-            choose(2, 0)
-            state()
-        else:
-            HC(1, 1)
-            select_1()
-            store(w, 0)
-            select_2()
-            sign(2, 1)
-            keep_c(1, idn)
-            rank_p(2, 1)
-            select_3()
-            choose(2, 0)
-            select_4()
-            parity[2]()
-            select_s()
-            tt(A("KM"), A("PL", 16, 32), A("KY"), OPS.min)
-            state()
-        relu(2, 1)
-        choose(2, 1)
-        store(w, 1)
-        ghosts_out(w + 1)
-        select_v()
-        update(0, 16)[0]()
-        act(A("XS"), xs)
-        select_p(0)
-        select_p(1)
-        update(0, 16)[1]()
-        select_b(0)
+            moved.pop()()
+            moved_out()
+        if not last:
+            credit(w)
+            relay()
+            gcopy(A("XS", CAP * (w % 2), CAP * (w % 2) + CAP), A("XR", 0, 4096, 16))
+        for t in range(3):
+            for X in range(2):
+                if t == 0:
+                    numbers(0, X)
+                compare(t, X, (SHARE_LAST if last else SHARE)[2 * t + X], ("PR", "PM") if last else ("PR", "PT"),
+                        (lambda: ranks(w + 1)) if t == 2 and X and not last else (lambda: None))
+                if t < 2:
+                    sign(t, CH * X, CH)
+                if t == 0:
+                    fails(w, CH * X, CH)
+                if t == 2 and X == 0 and LATE and not last:
+                    last_flags(w)
+                if t == 2:
+                    if X == 0:
+                        kept(1)
+                    for lo, n in ENDS[X]:
+                        store(w, X, lo, n, idn)
+                choose(t, X)
+                if t < 2:
+                    onward(t, X)
+                if t == 1:
+                    keep(X, idn)
+                if t == 1 and X == 0:
+                    kept(0)
+                    if not last and not LATE:
+                        last_flags(w)
+            if t == 0:
+                successes(w)
+                if last:
+                    old_out()
+        if not last:
+            ghosts_out(w + 1)
+            if moved:
+                moved.pop()()
+            act(A("EC"), A("EO"), AFT.Copy, C3, -8.0)
+            update(w, 0, 16)
+    dma("y", T.yf[:], T.YW[:, A0:AG], [("YW", A0, AG)], [], "oy", 655360)
+    update(RO - 1, 0, 8)
+    update(RO - 1, 8, 16)
+    dma("y", T.ya[:], T.YA[:, A0:AG], [("YA", A0, AG)], [], "oa", 327680)
 
-    first, second = update(0, 8), update(8, 16)
-    G(1, 0, 32)
-    sign(2, 0, "v")
-    Gp(1, 2)
-    keep_c(0, idn)
-    rank_p(2, 0)
-    Gp(1, 3)
-    relu(2, 0)
-    drain(99)
-    G(1, 32, 64)
-    choose(2, 0)
-    Hs(1, 2)
-    HC(1, 0)
-    first[0]()
-    Hs(1, 3)
-    count(1, 1)
-    first[1]()
-    store(w, 0, first[2])
-    first[3]()
-    sign(2, 1)
-    keep_c(1, idn)
-    rank_p(2, 1)
-    first[4]()
-    relu(2, 1)
-    first[5]()
-    choose(2, 1)
-    store(w, 1, lambda: None)
-    dma("y", T.yf[:], T.YW[:, 0:VA], [("YW", 0, VA)], [], "oy")
-    for f in second:
-        f()
-    dma("y", T.ya[:], T.YA[:, 0:VA], [("YA", 0, VA)], [], "oa")
+    for k in range(4):
+        arrive(nxt, ("BW", HALO + XB[k], HALO + min(XB[k + 1], NH)), "hb%d" % k)
+    for h in range(4):
+        arrive(nxt, ("NW", HALO + 512 * h, HALO + 512 * h + 512), "hn%d" % h)
+    arrive(prv, ("F", AG, AE), "gh0")
+    if not ORDER:
+        ORDER["calls"] = arrange(tasks, before)
+    for j in ORDER["calls"]:
+        tasks[j]["run"]()
 
     need("y", "oy", 16)
     need("y", "oa", 16)
     for w in range(RO):
-        need("g", "lg%d" % w, 16)
+        need("g", "lg%d" % w, len(engines(core, nxt, "gh%d" % w)))
+    need("g", "lc", RO - 1)
     for s in HALOS:
-        need("g", "l" + s, len(topo.engines(core, prv)))
+        need("g", "l" + s, len(engines(core, prv, s)))
     for s in ("cv", "cs", "cp", "cg"):
         need("y", s, cnt[s])

from concourse.mybir import AluOpType as OPS, ActivationFunctionType as AFT, AxisListType as AXL

VA, OB, CAP, S, RO = 1280, 2048, 256, 272, 6
CH, SUB = 128, 64
OFF = 7
HALO = OB + 1 + OFF
NH = 2047
A0, AG, AE = CAP, CAP + VA, 2 * CAP + VA
FIRST = A0 + S + CAP
C4 = 1.5 * 2.0 ** 26
C3 = C4 + 8.0
WZ, THR = 16384.0, 18432.0

DTS = {"b": "bfloat16", "f": "float32", "h": "float16", "i": "int32", "u": "uint16"}
BUFS = """AW1536b YA3584b BW4104b NW4104i HS2048i NA1536i F1792f FI272i BDI16i BDU16u IND272h W14336f WB3584f YF3584f XN256f
WC448f WD112f EL96h CU96h INF80h SU80h KT400b ZF320f FH16h FRL32u NAU256u JJ256h CA256h TA16f GT96f SL16u SH16h CC16h DH16h LSP16u
HI256h DG16h T0X1f D6X128h NLT128h I6X128h I16X128h I112X128h IM128h
Ch256h Th256h LP256h LU256u SG4096h CB768h CL256u XR4096b D4096h VV768h SC256h AB512f AC512f KY16f KM16f TI16i TM16i UL16u UF16u FA16h
LSU32u XS512b IDB128b IDC128b EI1i EO1i EC1f DB256b DC256b GS256f YW1536f IP1i LPI1i GPI1i PCF1f LPC1f GPC1f CF1f CG1f
LM128h CM128f XG144f XH144h EP144h EQ144h SAM128h IDM128f IDH128h IDN128h IDL128h TRI128h LTM128h WK128h TF128h TL128h
PA128h PB128h PN128h PG128b PF128h ONE128h KC128h CO256h OH128h ZM384h XL48h HE8f DPM2048h KA1280f KB256f"""
WW = 7168
FR, FV, FW = 0, 1544, 1544
STAMP = [32.0 * 8 ** w for w in range(RO - 1)]
SCRATCH = {}
for _b in BUFS.split():
    _n = _b.rstrip("bfhiu").rstrip("0123456789")
    SCRATCH[_n.rstrip("X")] = ("sbuf", [128, int(_b[len(_n):-1])], DTS[_b[-1]])
PS = ("PC0", "PC1", "PQ0", "PQ1", "PL", "PR", "PM", "PT")
for _n in PS:
    SCRATCH[_n] = ("psum", [128, 512], "float32")
XB = (0, 512, 1024, 1536, OB)
LOADS = ["f0", "bd", "xb0", "xb1", "xb2", "xb3", "nba", "xa", "nb0", "nb1", "nb2", "nb3", "nba2", "xa2"]
HALOS = ["hb0", "hb1", "hb2", "hb3", "hn0", "hn1", "hn2", "hn3"]
QUARTER = ["hb0", "hb1", "hb2", "gh0"]
SEMAPHORES = (["cv", "cs", "cp", "cg", "oy", "oa", "lc"] + HALOS + ["l" + n for n in HALOS] + ["ld_" + n for n in LOADS]
              + ["zw0", "zw1", "zw2", "zb"] + [k + str(w) for k in ("gh", "lg", "cr", "xe", "xf", "xv", "xd") for w in range(RO)])

SIGNQ = "svvvvs"
KEEPQ = "..ssss"
SHARE = (0, 0, 0, 0, 1, 2)
SHARE_LAST = (0, 2, 2, 2, 2, 2)
VSEED = 24
VFR = 16
WBQ = "s"
VFL = 0
UNITS = ((0, 128), (128, 128))
PIECES = ((("g", 0, 64), ("h", 0, 64), ("g", 64, 128), ("h", 64, 128)),
          (("g", 0, 64), ("g", 64, 80), ("g", 80, 128), ("h", 0, 64), ("h", 64, 128)),
          (("g", 0, 48), ("g", 48, 80), ("g", 80, 128), ("h", 0, 64), ("h", 64, 128)))
PASSES = 3

CYC, GATHER, PECYC = 0.83, 1.56, 0.45
SCATTER = 3.8
WAKE = 150.0
TWO = 1.8
VTAKES = ()
MID = 6
ENDS = (((0, 128),), ((0, 128),))
MB = "PT"
SQ = "sssssss"
NUMQ = "svsv"
KB_LATE = 1
LB = "PC0"
RATE = 300.0
ONCE = 5000.0
LATE = 1
OUFIRST = 0
ELAFTER = "own test"
LSQ = "v"
EARLY = 2
AHEAD = 8
RERUN = (1,)
SHORT = 300.0
SLACK = 3000.0
FIT = 100.0
WEIGH = 1.0
CASES = ((1.56, 3.8, 0.0), (1.4, 5.3, 0.0), (1.95, 2.2, 0.0), (1.15, 2.0, 0.0))
TRIES = (((1, 2), (1, 2, 3, 4), 26000), ((-1, 0), (-1, 0), 5000), ((4, 5), (5,), 6000))
HEAT = 0.002
VFIX, SFIX = 25.0, 35.0
SEED = 1
ORDER = {}


def place(tasks, before, seq):
    start, busy = {}, {}
    for j in seq:
        q, dur, banks = tasks[j]["q"], tasks[j]["dur"], tasks[j]["banks"]
        t = max([start[i] + tasks[i]["dur"] + d for i, d in before[j]] + [0.0])
        moved = True
        while moved:
            moved = False
            for r in [q] + banks:
                l = busy.setdefault(r, [])
                k = len(l)
                while k and l[k - 1][1] + WAKE > t:
                    k -= 1
                for a, b, q2 in l[k:]:
                    pad = WAKE if q2 != q else 0.0
                    if a - pad >= t + dur:
                        break
                    if t < b + pad:
                        t, moved = b + pad, True
        start[j] = t
        for r in [q] + banks:
            l = busy[r]
            k = len(l)
            while k and l[k - 1][0] > t:
                k -= 1
            l.insert(k, (t, t + dur, q))
    return start


def run_through(tasks, before, after, way):
    n = len(tasks)
    end, free, bank, seq = {}, {}, {}, []
    left = [len(b) for b in before]
    mine = {q: sorted([j for j in range(n) if tasks[j]["q"] == q], key=lambda j: -way[j]) for q in "vspgy"}
    for q in mine:
        free[q] = 0.0

    def ready(j, memo):
        if j not in memo:
            t = free[tasks[j]["q"]]
            for i, d in before[j]:
                t = max(t, (end[i] if i in end else ready(i, memo) + tasks[i]["dur"]) + d)
            for r in tasks[j]["banks"]:
                if r in bank and bank[r][1] != tasks[j]["q"]:
                    t = max(t, bank[r][0] + WAKE)
            memo[j] = t
        return memo[j]

    while len(seq) < n:
        memo, pick = {}, None
        for q in sorted(mine, key=lambda q: free[q]):
            near = mine[q][:AHEAD]
            if not near:
                continue
            goal = max(near, key=lambda j: way[j] - WEIGH * ready(j, memo))
            open_ = [j for j in near if not left[j]]
            first = min([ready(j, memo) for j in open_] + [ready(goal, memo)])
            short = [j for j in open_ if tasks[j]["dur"] < SHORT and ready(j, memo) <= first + 1.0 and way[j] > way[goal] - SLACK]
            fits = [j for j in open_ if ready(j, memo) + tasks[j]["dur"] <= ready(goal, memo) + FIT]
            j = max(short, key=lambda j: way[j]) if short else max(fits, key=lambda j: way[j] - WEIGH * ready(j, memo)) if fits else goal
            if not left[j] and (pick is None or ready(j, memo) < pick[0]):
                pick = (ready(j, memo), j)
        if pick is None:
            pick = min((ready(j, memo), j) for q in mine for j in mine[q] if not left[j])
        t, j = pick
        q = tasks[j]["q"]
        end[j] = free[q] = t + tasks[j]["dur"]
        for r in tasks[j]["banks"]:
            bank[r] = (end[j], q)
        for k, _ in after[j]:
            left[k] -= 1
        mine[q].remove(j)
        seq.append(j)
    return seq


def arrange(tasks, before):
    n = len(tasks)
    after = [[] for _ in range(n)]
    for j in range(n):
        for i, d in before[j]:
            after[i].append((j, d))
    way = [0.0] * n
    for i in range(n - 1, -1, -1):
        way[i] = tasks[i]["dur"] + max([way[j] + d for j, d in after[i]] + [tasks[i]["lat"]])
    start = place(tasks, before, run_through(tasks, before, after, way))
    best = start
    for k in range(PASSES):
        back = place(tasks, after, sorted(range(n), key=lambda j: -start[j] - tasks[j]["dur"]))
        way = [back[j] + tasks[j]["dur"] for j in range(n)]
        start = place(tasks, before, run_through(tasks, before, after, way) if k in RERUN else sorted(range(n), key=lambda j: -way[j]))
        if max(start.values()) < max(best.values()):
            best = start
    ORDER["span"] = max(best.values())
    return polish(tasks, before, best)


def polish(tasks, before, start):
    n, res = len(tasks), {}
    qi = [res.setdefault(t["q"], len(res)) for t in tasks]
    bk = [[res.setdefault(b, len(res)) for b in t["banks"]] for t in tasks]
    kinds = {}
    wave, kind = [t["wave"] for t in tasks], [kinds.setdefault(t["kind"], len(kinds)) for t in tasks]
    near, pre = list(before), [[i for i, _ in b] for b in before]
    head = [min(start[j] for j in range(n) if tasks[j]["mark"] == "seeds" and wave[j] == w) for w in range(RO)]
    origin = {w: head[1] + (w - 1) * (head[3] - head[2]) for w in range(1, RO)}
    origin[0], origin[-1] = head[0], 0.0
    base_of, place_of = [origin[w] for w in wave], [0.0] * len(kinds)
    for j in sorted(range(n), key=lambda j: wave[j] == 2):
        place_of[kind[j]] = start[j] - (head[wave[j]] if wave[j] >= 0 else 0.0)
    seed = [SEED]

    def rand(k):
        seed[0] = (seed[0] * 1103515245 + 12345) % 2147483648
        return (seed[0] >> 8) % k

    def order(part, pl):
        key = [0.0] * n
        for j in part:
            x = base_of[j] + pl[kind[j]]
            for i in pre[j]:
                if key[i] >= x:
                    x = key[i] + 0.01
            key[j] = x
        return sorted(part, key=lambda j: key[j]), key

    def run(seq, case, end, goal, why):
        free, who = [0.0] * len(res), [-1] * len(res)
        for j in seq:
            q = qi[j]
            t, c = free[q], who[q]
            for i, d in near[j]:
                if end[i] + d > t:
                    t, c = end[i] + d, -2 - i
            for b in bk[j]:
                k = who[b]
                if k >= 0 and qi[k] != q and free[b] + WAKE > t:
                    t, c = free[b] + WAKE, k
            end[j] = free[q] = t + case[j]
            who[q], why[j] = j, c
            for b in bk[j]:
                free[b], who[b] = end[j], j
        return max((end[j] + tasks[j]["lat"], j) for j in goal)

    cases = [[t["durs"][c] for t in tasks] for c in range(len(CASES))]
    for waves, free_waves, tries in TRIES:
        ends, why = [[0.0] * n for _ in cases], {}
        for case, end in zip(cases, ends):
            run(order(range(n), place_of)[0], case, end, [n - 1], why)
        if waves[-1] == RO - 1:
            part = goal = [j for j in range(n) if wave[j] in waves]
        else:
            goal = [max(j for j in range(n) if tasks[j]["mark"] == "test" and wave[j] == waves[-1] + 1)]
            part = [j for j in range(goal[0] + 1) if wave[j] >= waves[0]]
        inside = set(part)
        t0 = [min(end[j] for j in part) for end in ends]
        for j in part:
            out = [(i, d) for i, d in before[j] if i not in inside]
            near[j] = [(i, d) for i, d in before[j] if i in inside] + sorted(out, key=lambda x: ends[0][x[0]] + x[1])[-1:]
            pre[j] = [i for i in pre[j] if i in inside]
        seq, key = order(part, place_of)
        base = [run(seq, case, end, goal, why)[0] - t for case, end, t in zip(cases, ends, t0)]

        def share(seq, c):
            return (run(seq, cases[c], ends[c], goal, why)[0] - t0[c]) / base[c]
        each = [1.0] * len(cases)
        now = least = 1.5
        best, left = place_of, tries
        while left > 0:
            c = rand(len(cases))
            j, pairs = run(seq, cases[c], ends[c], goal, why)[1], []
            while j in inside and why[j] != -1:
                i = why[j]
                if i >= 0 and i not in pre[j] and wave[i] in free_waves and wave[j] in free_waves:
                    pairs.append((i, j))
                j = i if i >= 0 else -2 - i
            left -= 1
            for _ in range(min(20, len(pairs))):
                u, v = pairs[rand(len(pairs))]
                pl, r = list(place_of), rand(10)
                if r < 4:
                    pl[kind[u]] = key[v] - origin[wave[u]] + (1.0, 100.0, 400.0, 1000.0, 2500.0)[rand(5)]
                else:
                    x = key[u] - (1.0, 100.0, 400.0)[rand(3)]
                    pl[kind[v]] = x - origin[wave[v]]
                    for i in pre[v]:
                        if key[i] > x and wave[i] in free_waves:
                            pl[kind[i]] = x - 1.0 - origin[wave[i]]
                seq2, key2 = order(part, pl)
                left -= 1
                room = HEAT * left / tries * rand(100) / 100.0
                mine = share(seq2, c)
                if mine > each[c] + room:
                    continue
                r = [mine if k == c else share(seq2, k) for k in range(len(cases))]
                new = sum(r) / len(r) + 0.5 * max(r)
                if new < now + room:
                    place_of, seq, key, now, each = pl, seq2, key2, new, r
                    if new < least:
                        best, least = pl, new
                    break
        place_of = best
        near[:], pre[:] = before, [[i for i, _ in b] for b in before]
    return order(range(n), place_of)[0]


def rank_program(g, core, T, topo):
    rank = T.rank_of(core)
    if rank is None:
        return
    nxt, prv = T.cores[(rank + 1) % 4], T.cores[(rank + 3) % 4]
    Q = {"v": g.vector, "s": g.scalar, "p": g.tensor, "g": g, "y": g.sync}
    CS = {"v": "cv", "s": "cs", "p": "cp", "g": "cg"}
    cnt = {"cv": 0, "cs": 0, "cp": 0, "cg": 0}
    known = {q: {} for q in Q}
    clocks = {}
    acc = {}

    def need(q, sem, val):
        if known[q].get(sem, 0) >= val:
            return
        Q[q].wait_ge(T.sem[sem], val)
        known[q][sem] = val
        for s2, v2 in clocks.get((sem, val), {}).items():
            if known[q].get(s2, 0) < v2:
                known[q][s2] = v2

    def deps(q, reads, writes):
        want = {}
        for lst, isw in ((reads, False), (writes, True)):
            for name, lo, hi in lst:
                ps = name in PS
                for a in acc.get(name, []):
                    if not ps and (a[1] <= lo or hi <= a[0]):
                        continue
                    if ps and a[2] == q and (q == "p" or not a[5]) or not (isw or a[5] or ps):
                        continue
                    if want.get(a[3], 0) < a[4]:
                        want[a[3]] = a[4]
        for sem in sorted(want):
            need(q, sem, want[sem])

    def note(q, reads, writes, sem, val):
        c = dict(known[q])
        c[sem] = val
        clocks[(sem, val)] = c
        for lst, isw in ((reads, False), (writes, True)):
            for name, lo, hi in lst:
                l = acc.setdefault(name, [])
                if isw or name in PS:
                    l[:] = [a for a in l if not (name in PS or (lo <= a[0] and a[1] <= hi))]
                else:
                    l[:] = [a for a in l if a[5] or a[2] != q or a[3] != sem or not (lo <= a[0] and a[1] <= hi)]
                l.append([lo, hi, q, sem, val, isw])

    def issue(q, reads, writes, call):
        deps(q, reads, writes)
        sem = CS[q]
        cnt[sem] += 1
        call().then_inc(T.sem[sem], 1)
        note(q, reads, writes, sem, cnt[sem])

    def engines(src, dst, rsem):
        use = topo.engines(src, dst)
        if rsem in QUARTER:
            k, n = QUARTER.index(rsem), len(use) // 4
            use = use[k * n:k * n + n]
        return use

    def arrive(src, region, rsem):
        name, lo, hi = region
        l = acc.setdefault(name, [])
        l[:] = [a for a in l if not (lo <= a[0] and a[1] <= hi)]
        l.append([lo, hi, "r", rsem, len(engines(src, core, rsem)), True])

    tasks, before = [], []
    seen, raised, group = {}, {}, {}

    now = {"wave": -1}

    def task(q, run, reads, writes, dur, lat=0.0, after=(), kind="", durs=None):
        j, pre = len(tasks), {}
        for lst, isw in ((reads, False), (writes, True)):
            for name, lo, hi in lst:
                for a, b, i, w in seen.get(name, []):
                    if (isw or w) and a < hi and lo < b:
                        pre[i] = 0.0 if name in PS and q == "p" == tasks[i]["q"] else WAKE
        for lst, isw in ((reads, False), (writes, True)):
            for name, lo, hi in lst:
                l = seen.setdefault(name, [])
                if isw:
                    l[:] = [a for a in l if not (lo <= a[0] and a[1] <= hi)]
                l.append((lo, hi, j, isw))
        if kind:
            starts, adds = group.setdefault(writes[0][0], ([], []))
            if kind != "add":
                for i in adds + (starts if kind == "open" else []):
                    pre.setdefault(i, 0.0)
                if kind == "open":
                    starts[:], adds[:] = [], []
            (adds if kind in ("add", "close") else starts).append(j)
        for i in after:
            pre.setdefault(i, 0.0)
        before.append([(i, d + (tasks[i]["lat"] if d else 0.0)) for i, d in pre.items()])
        w = now["wave"]
        like = (q, tuple(sorted({r[0][:2 if lat else 9] for r in writes})), tuple(sorted({r[0][:2 if lat else 9] for r in reads})))
        now[like] = now.get(like, 0) + 1
        tasks.append({"q": q, "run": run, "dur": dur, "lat": lat, "banks": sorted({r[0] for r in reads + writes if r[0] in PS}),
                      "durs": durs or [dur] * len(CASES), "wave": w, "kind": (1 if 0 < w < RO - 1 else w, like, now[like]), "mark": ""})
        return j

    lines = {}

    def inturn(line):
        j = len(tasks) - 1
        if line in lines and lines[line] not in [i for i, _ in before[j]]:
            before[j].append((lines[line], 0.0))
        lines[line] = j

    def behind(line):
        j = len(tasks) - 1
        if lines[line] not in [i for i, _ in before[j]]:
            before[j].append((lines[line], 0.0))

    def wide(name):
        return 4 if SCRATCH[name][2] in ("float32", "int32") else 2

    def A(name, lo=0, hi=None, st=1):
        if hi is None:
            hi = T[name].shape[1]
        ap = T[name][:, lo:hi] if st == 1 else T[name][:, lo:hi:st]
        return (ap, [(name, lo, hi)], [], len(range(lo, hi, st)), wide(name), False)

    def I(win, a, b, off, o0, o1):
        return (T[win][:, a:b].indirect(T[off][:, o0:o1]), [(win, a, b)], [(off, o0, o1)], 16 * (o1 - o0), wide(win), True)

    def op(q, out, ins, call, per=None):
        reads, writes = list(out[2]), list(out[1])
        for x in ins:
            reads += x[1] + x[2]
        n, fix = out[3], {"v": 50.0, "s": 65.0, "g": 170.0}[q]
        durs = None
        if out[5] or ins and ins[0][5]:
            dur = fix + n * CYC * (SCATTER if out[5] else max(GATHER, min(per or 0, TWO)))
            durs = [fix + n * CYC * (sc if out[5] else max(ga, min(per or 0, two))) for ga, sc, two in CASES]
        elif q == "v":
            dur = VFIX + CYC * max(64, n * (per or (0.5 if out[4] == 2 and (not ins or ins[0][4] == 2) else 1.0)))
        else:
            dur = fix + (SFIX if q == "s" else 0) + n * CYC * (1 if q == "s" else 2)
        task(q, lambda: issue(q, reads, writes, call), reads, writes, dur, durs=durs)

    def u(x):
        return x[0] if isinstance(x, tuple) else x

    def cp(out, in_):
        op("v", out, [in_], lambda: g.vector.tensor_copy(out=out[0], in_=in_[0]))

    def tt(out, a, b, o):
        psum = a[1][0][0] in PS or b[1][0][0] in PS
        op("v", out, [a, b], lambda: g.vector.tensor_tensor(out=out[0], in0=a[0], in1=b[0], op=o), 1.0 if psum else 2.0)

    def ts(out, a, s1, o0, s2=None, o1=None):
        ins = [a] + [x for x in (s1, s2) if isinstance(x, tuple)]
        if o1 is None:
            op("v", out, ins, lambda: g.vector.tensor_scalar(out=out[0], in0=a[0], scalar1=u(s1), scalar2=None, op0=o0))
        else:
            op("v", out, ins, lambda: g.vector.tensor_scalar(out=out[0], in0=a[0], scalar1=u(s1), scalar2=u(s2), op0=o0, op1=o1))

    def ms(out, c):
        op("v", out, [], lambda: g.vector.memset(out[0], c))

    def act(out, in_, f=AFT.Copy, bias=0.0, scale=1.0):
        if bias == 0.0 and scale == 1.0:
            op("s", out, [in_], lambda: g.scalar.activation(out=out[0], in_=in_[0], func=f))
        else:
            op("s", out, [in_], lambda: g.scalar.activation(out=out[0], in_=in_[0], func=f, bias=bias, scale=scale))

    def shift(q, out, in_, c):
        if q == "s":
            act(out, in_, AFT.Copy, c)
        else:
            ts(out, in_, c, OPS.add)

    def mms(calls, kind="sum"):
        def one(out, l, r, st, sp):
            issue("p", l[1] + r[1], out[1], lambda: g.tensor.matmul(out=out[0], lhsT=l[0], rhs=r[0], start=st, stop=sp))

        def run():
            for c in calls:
                one(*c)
        dur = sum(max(min(64, c[1][3]), c[2][3]) * c[2][4] ** 2 / 4 for c in calls) * PECYC
        task("p", run, sorted({r for c in calls for r in c[1][1] + c[2][1]}), sorted({r for c in calls for r in c[0][1]}), dur, kind=kind)

    def msum(out, terms, st=True, sp=True):
        mms([(out, l, r, st and k == 0, sp and k == len(terms) - 1) for k, (l, r) in enumerate(terms)],
            ("sum" if sp else "open") if st else "close" if sp else "add")

    def io(out, pat, base, cm=0, small=True):
        if small:
            op("g", out, [], lambda: g.iota(out[0], pat, base, cm, allow_small_or_imprecise_dtypes=True))
        else:
            op("g", out, [], lambda: g.iota(out[0], pat, base, cm))

    def gcopy(out, in_):
        op("g", out, [in_], lambda: g.affine_select(out[0], in_[0], [[0, out[3]]], OPS.is_equal, 0.0, 0, 0))

    last_dma = {}

    def moves(q, run, reads, writes, sem, nbytes, waits):
        j = task(q, run, reads + [(s, 0, 1) for s, _ in waits], writes + [(sem, 0, 1)], 60.0,
                 1700.0 + nbytes / RATE + (ONCE if q == "g" and q not in last_dma else 0.0))
        if q in last_dma:
            before[j].append(last_dma[q])
        last_dma[q] = (j, nbytes / RATE)

    def dma(q, out_ap, in_ap, reads, writes, sem, nbytes, waits=()):
        def run():
            for s, v in waits:
                need(q, s, v)
            deps(q, reads, writes)
            Q[q].dma_start(out=out_ap, in_=in_ap).then_inc(T.sem[sem], 16)
            note(q, reads, writes, sem, 16)
        moves(q, run, reads, writes, sem, nbytes, waits)

    def load(q, name, lo, hi, src, s0, sem, waits=()):
        dma(q, T[name][:, lo:hi], src[:, s0:s0 + hi - lo], [], [(name, lo, hi)], "ld_" + sem, 128 * (hi - lo) * wide(name), waits)

    def send(dst, outp, inp, rsem, lsem, waits=()):
        def run():
            for s, v in waits:
                need("g", s, v)
            deps("g", inp[1], [])
            rid, pid, _ = topo.addr(dst)
            use = engines(core, dst, rsem)
            g.remote_dma(out_ap=outp[0], in_ap=inp[0], remote_sem=T.sem[rsem], local_sem=T.sem[lsem], pid=pid, routing_id=rid,
                         dma_engine_mask=sum(1 << e for e in use))
            note("g", inp[1], [], lsem, len(use))
        moves("g", run, inp[1], outp[1], lsem, 128 * inp[3] * inp[4], waits)

    def credit(w):
        def run():
            deps("g", [], [("F", AG, AE)])
            rid, pid, _ = topo.addr(prv)
            g.remote_sem_update(T.sem["cr%d" % w], T.sem["lc"], pid, rid, 1 << topo.engines(core, prv)[0])
            arrive(prv, ("F", AG, AE), "gh%d" % (w + 1))
        moves("g", run, [], [("F", AG, AE)], "cr%d" % w, 0, ())

    def EP(p, name="EP"):
        return A(name, 15 - p, 143 - p)

    def DP(p):
        return A("DPM", 128 * p, 128 * p + 128)

    sent = len(topo.engines(core, prv))
    load("y", "BW", 8, 8 + XB[1], T.xb, 0, "xb0")
    load("s", "FI", 0, S, T.f0, 0, "f0")
    load("s", "BDI", 0, 16, T.bd, 0, "bd")
    for k in (1, 2, 3):
        load("y", "BW", 8 + XB[k], 8 + XB[k + 1], T.xb, XB[k], "xb%d" % k)
    load("s", "NA", A0, FIRST, T.nba, 0, "nba")

    def numbers_out(k):
        n = min(XB[k + 1], NH)
        send(prv, A("BW", HALO + XB[k], HALO + n), A("BW", 8 + XB[k], 8 + n), "hb%d" % k, "lhb%d" % k)

    io(A("IP"), [[0, 1]], 0, 1, False)
    io(A("XG"), [[1, 144]], -15)
    io(A("CM"), [[1, 128]], 0)
    io(A("JJ"), [[1, CAP]], 0)
    io(A("XL"), [[1, 48]], -15)
    io(A("HE"), [[16, 8]], 0)
    for a, n in UNITS:
        io(A("CO", a, a + n), [[0, 8], [1, 2], [0, n // 16]], 0)
    io(A("NA", 0, A0), [[1, CAP]], -A0, 0, False)
    ms(A("ZF"), 0.0)
    ts(A("LPI"), A("IP"), 15, OPS.bitwise_and)
    ts(A("GPI"), A("IP"), 112, OPS.bitwise_and)
    cp(A("PCF"), A("IP"))
    cp(A("GPC"), A("GPI"))
    ts(A("LPC"), A("LPI"), 1.0, OPS.add)
    ts(A("IDM"), A("CM"), A("PCF"), OPS.is_equal)
    ts(A("EP"), A("XG"), A("GPC"), OPS.is_equal)
    ts(A("XH", 0, 128), A("CM"), A("GPC"), OPS.subtract)
    ts(A("WK"), A("XH", 0, 128), A("LPC"), OPS.is_ge)
    ts(A("SAM"), A("XH", 0, 128), 15.5, OPS.is_lt)
    ts(A("IDL"), A("IDM"), A("LPC"), OPS.mult)
    tt(A("TRI"), A("WK"), A("SAM"), OPS.mult)
    ts(A("LM"), A("XH", 0, 128), 2.0, OPS.add, A("LPC"), OPS.is_le)
    ts(A("WK"), A("XH", 0, 128), -0.5, OPS.is_gt)
    cp(A("IDH"), A("IDM"))
    tt(A("LTM"), A("WK"), A("LM"), OPS.mult)
    for name, c in (("IDN", -1.0), ("PN", -2048.0), ("PG", 2.0 ** 18), ("PF", 2.0), ("IDB", 1.0), ("IDC", -1.0), ("PA", 2048.0),
                    ("PB", 4096.0), ("I6", 6.0), ("I16", 16.0), ("I112", 112.0), ("IM", -1791.0)):
        ts(A(name), A("IDH"), c, OPS.mult)
    ts(A("DG"), A("CM", 1, 17), A("LPC"), OPS.is_equal)
    ts(A("NLT"), A("LTM"), -1.0, OPS.mult)
    ts(A("D6"), A("IDL"), 6.5, OPS.is_gt, 30000.0, OPS.mult)
    ts(A("HI", 0, 128), A("XH", 0, 128), -0.5, OPS.is_gt)
    tt(A("SAM"), A("HI", 0, 128), A("SAM"), OPS.mult)
    for p in range(16):
        ts(DP(p), A("IDL"), float(p + 1), OPS.is_equal)
    tt(A("WK"), A("TRI"), A("IDH"), OPS.subtract)
    tt(A("LM"), A("LTM"), A("IDH"), OPS.subtract)
    ts(A("TF"), A("WK"), WZ, OPS.mult)
    ts(A("TL"), A("LM"), WZ, OPS.mult)
    ts(A("HE"), A("HE"), A("GPC"), OPS.not_equal, 1000.0, OPS.mult)
    ts(A("EQ"), A("EP"), 2.0, OPS.mult)
    ts(A("HE"), A("HE"), A("LPC"), OPS.add)
    ts(A("CF"), A("LPC"), WZ, OPS.mult)
    ts(A("CG"), A("LPC"), -WZ, OPS.mult, 17 * WZ, OPS.add)
    for h in range(8):
        ts(A("ZM", 48 * h, 48 * h + 48), A("XL"), A("HE", h, h + 1), OPS.is_equal)
    for buf, c in ((A("KC"), -27.0), (A("OH"), 1.0 / 256.0), (A("ONE"), 1.0), (A("EC"), C3), (A("BW", 0, 8), 1024.0), (A("NW", 0, 8), 4095),
                   (A("AW", 0, A0), 0.0), (A("HS", 2047, 2048), 4095)):
        ms(buf, c)
    act(A("F", 0, A0), A("ZF", 0, A0))
    for a in range(A0 + S, AG, 320):
        act(A("F", a, min(a + 320, AG)), A("ZF", 0, min(320, AG - a)))
    act(A("KB"), A("ZF", 0, CAP), AFT.Silu, 2.0 ** 22)
    for w in range(RO - 1):
        act(A("KA", CAP * w, CAP * w + CAP), A("ZF", 0, CAP), AFT.Copy, STAMP[w])
        act(A("KT", 80 * w, 80 * w + 80), A("ZF", 0, 80), AFT.Copy, -0.875 * STAMP[w])

    def extract(w):
        for k, a in enumerate((0, WW)):
            dma("y", T.WC[:, 224 * k:224 * k + 224], T.W[0:128:16, a:a + 2 * AE], [("W", a, a + 2 * AE)], [("WC", 224 * k, 224 * k + 224)],
                ("xe%d", "xf%d")[k] % w, 114688)

    def extract_b(w):
        dma("y", T.WD[:], T.WB[0:128:16, 0:AE], [("WB", 0, AE)], [("WD", 0, 112)], "xd%d" % w, 57344)

    Z = A("PM", 160, 240)

    def flagged(w):
        msum(Z, [(A("IDB"), A("KT", 80 * w - 80, 80 * w)), (A("PG"), A("INF")), (A("PN"), A("SU"))], True, False)
        for k in range(2):
            msum(Z, [(A("IDM"), A("WC", 224 * k + 32 + r, 224 * k + 192, 2)) for r in range(2)], False, k == 1)
            behind("count")
        inturn("flagged")
        tt(A("EL", 0, 80), Z, A("WD", 16, 96), OPS.is_gt)
        behind(ELAFTER)

    def ranks(w):
        if w:
            flagged(w)
        col, rank, over, upto = A("PM", 0, 96), A("PM", 256, 352), A("PM", 352, 432), A("PM", 464, 480)
        msum(col, [(A("SAM"), A("EL"))])
        op("v", A("CU"), [col, A("ZF", 0, 96)], lambda: g.vector.tensor_tensor_scan(
            out=T.CU[:], data0=T.PM[:, 0:96], data1=T.ZF[:, 0:96], initial=0.0, op0=OPS.add, op1=OPS.add), 1.0)
        tt(A("SH"), A("CU", 5, 96, 6), A("DG"), OPS.mult)
        op("v", A("T0"), [A("SH")], lambda: g.vector.tensor_reduce(out=T.T0[:], in_=T.SH[:], axis=AXL.X, op=OPS.add))
        ts(A("CA"), A("JJ"), A("T0"), OPS.is_ge)
        msum(upto, [(DP(i), A("CU", i, 96, 6)) for i in range(6)] + [(A("D6"), A("ONE", 0, 16))])
        msum(rank, [(A("IDH"), A("CU")), (A("NLT"), A("EL"))])
        shift(SQ[0], A("TA"), upto, 0.0)
        shift(SQ[1], A("GT"), rank, 0.0)
        if w < RO - 1:
            msum(over, [(A("IDH"), A("CU", 0, 80)), (A("NLT"), A("EL", 0, 80)), (A("PB"), A("EL", 0, 80))])
            ts(A("INF"), over, 4096.0 + CAP + 0.5, OPS.is_gt)
        six, c, cell, o = A(LB, 480, 496), A(LB, 496, 512), A(LB, 480, 496), 16 * (w % 2)

        def counted(out, more=()):
            msum(out, list(more) + [(EP(l), A("CA", l, CAP, 16)) for l in range(16)])
        counted(six)
        cp(A("SL"), six)
        shift(SQ[2], A("SH"), six, 0.0)
        tt(A("CA"), I("TA", 0, 16, "SL", 0, 16), A("JJ"), OPS.is_le)
        counted(c, [(A("I6"), A("SH"))])
        cp(A("SL"), c)
        shift(SQ[3], A("CC"), c, 0.0)
        ts(A("DH"), c, 79.5, OPS.is_gt, -96.0, OPS.mult)
        tt(A("CA"), I("GT", 0, 96, "SL", 0, 16), A("JJ"), OPS.is_le)
        counted(cell, [(A("I16"), A("CC")), (A("I16"), A("DH"))])
        ts(A("FRL", o, o + 16), cell, float(A0), OPS.add)
        shift(SQ[4], A("FH"), cell, float(A0))

    def front(w):
        end, o = AG if w else FIRST, 16 * (w % 2)
        for a, b in ((0, SUB), (SUB, CAP)):
            act(A("XR", 16 * a, 16 * b, 16), I("AW", 0, end, "FRL", o + a // 16, o + b // 16))
            ts(A("NAU", a, b), I("NA", 0, end, "FRL", o + a // 16, o + b // 16), float(A0), OPS.add)

    def xrep(q, s, k, n=1):
        a, b = 16 * SUB * s, 16 * SUB * (s + n)
        (gcopy if q == "g" else cp)(A("XR", a + k, b, 2 * k), A("XR", a, b, 2 * k))

    def relay():
        cp(A("Ch"), A("NAU"))
        ts(A("HI"), A("NAU"), 1.0 / 16, OPS.mult, 1536.0 - 7.5 / 16, OPS.add)
        for h in range(2):
            mms([(A("PT", 32 * k + 16 * h, 32 * k + 16 * h + 16), A(x, 128 * h, 128 * h + 128), A(y, 16 * k, 16 * k + 16), x == "Ch", x == "HI")
                 for k in range(8) for x, y in (("Ch", "I112"), ("HI", "IM"))])
        act(A("Th"), A("PT", 0, 256), AFT.Copy, 1791.0 * 1536)
        for h in range(8):
            mms([((T.PR[32 * (k // 2):32 * (k // 2) + 32, h:256:8], [("PR", 0, 256)]), A("ZM", 48 * h + 16 - 16 * (k % 2), 48 * h + 48 - 16 * (k % 2)),
                  A("Th", 32 * k, 32 * k + 32), k % 2 == 0, k % 2 == 1) for k in range(8)])
        act(A("LP"), A("PR", 0, 256))

    def ghosts_out(w):
        if SQ[5] == "s":
            act(A("GS"), I("F", A0, AG, "BDU", 0, 16), AFT.Relu, -2048.0)
        else:
            ts(A("GS"), I("F", A0, AG, "BDU", 0, 16), -2048.0, OPS.add, 0.0, OPS.max)
        send(nxt, A("F", AG, AE), A("GS"), "gh%d" % w, "lg%d" % w, [("cr%d" % (w - 1), 1)] if w else [])

    numbers_out(0)
    ts(A("IND"), A("FI"), 4095.0, OPS.not_equal)
    some = A("PM", 160, 160 + S // 16)
    msum(some, [(EP(q), A("IND", q, S, 16)) for q in range(16)])
    ts(A("EL", 0, S // 16), some, 0.5, OPS.is_lt)
    ts(A("SU", 0, S // 16), some, 0.5, OPS.is_gt, 1024.0, OPS.mult)
    ms(A("EL", S // 16, 96), 1.0)
    ms(A("SU", S // 16, 80), 0.0)
    ts(A("FI"), A("FI"), 1.0, OPS.add)
    ts(A("FI"), A("FI"), 4095, OPS.bitwise_and)
    cp(A("F", A0, A0 + S), A("FI"))
    cp(A("BDU"), A("BDI"))
    numbers_out(1)
    numbers_out(2)
    ghosts_out(0)
    numbers_out(3)
    op("v", (T.BW[:, 4103:4104], [("BW", 4096, 4104)], [], 1, 2, False), [], lambda: g.vector.memset(T.BW[:, 4103:4104], 1024.0))
    load("y", "AW", A0, FIRST, T.xa, 0, "xa", [("ld_xb3", 16)])
    for h in range(4):
        load("y", "NW", 8 + 512 * h, 8 + 512 * h + 512, T.nbb, 512 * h, "nb%d" % h, [("lhb0", len(engines(core, prv, "hb0")))])
    for k, a in enumerate((0, WW)):
        dma("y", T.W[0:128:16, a:a + 2 * AE], T.ZF[:, 0:224], [("ZF", 0, 224)], [("W", a, a + 2 * AE)], "zw%d" % k, 114688)
    for h in range(4):
        a = 512 * h
        ts(A("HS", a, a + 512 - h // 3), A("NW", 8 + a, 8 + a + 512 - h // 3), 2047.0, OPS.min, 2048.0, OPS.add)
        send(prv, A("NW", HALO + a, HALO + a + 512), A("HS", a, a + 512), "hn%d" % h, "lhn%d" % h)
    dma("y", T.WB[0:128:16, 0:AE], T.ZF[:, 0:112], [("ZF", 0, 112)], [("WB", 0, AE)], "zb", 57344, [("lhn3", sent)])
    load("y", "NA", FIRST, AG, T.nba, FIRST - A0, "nba2")
    load("y", "AW", FIRST, AG, T.xa, FIRST - A0, "xa2")
    act(A("YF", A0, AG), A("AW", A0, AG), AFT.Copy, 256.0)

    def cb(t, X):
        return A("CB", 256 * t + CH * X, 256 * t + CH * X + CH)

    def vv(t, X):
        return A("VV", 256 * t + CH * X, 256 * t + CH * X + CH)

    def pq(X, k, n=1):
        return A("PQ%d" % X, CH * k, CH * (k + n))

    def seeds(s):
        a, b, out = SUB * s, SUB * s + SUB, A(("PC0", "PQ0", "PC1", "PQ1")[s], 384, 384 + SUB)
        m = a + (VSEED if s == 0 else 0)
        if m > a:
            ts(A("SG", 16 * a, 16 * m), I("F", 0, AE, "NAU", a, m), -2048.0, OPS.add)
        act(A("SG", 16 * m, 16 * b), I("F", 0, AE, "NAU", m, b), AFT.Copy, -2048.0)
        inturn("s")
        tasks[-1]["mark"] = "seeds"
        msum(out, [(DP(p), A("SG", 16 * a + p, 16 * b, 16)) for p in range(16)])
        shift("s" if s == 3 else "v", A("CL", a, b), out, 2048.0 + OFF)

    def numbers(t, X):
        shift(NUMQ[t], cb(t, X), A("CL", CH * X, CH * X + CH), -2048.0 - OFF)

    turn = [0]

    def compare(t, X, share, banks, between):
        top = CH - 32 * share
        for what, lo, hi in PIECES[0 if t + X == 0 else 1 if t == 0 else 2]:
            a, b = CH * X + lo, CH * X + min(hi, top)
            if a < b and what == "g":
                tt(A("D", 16 * a, 16 * b), I("BW", 0, 4104, "CL", a, b), A("XR", 16 * a, 16 * b), OPS.subtract)
                inturn("v")
            elif a < b:
                ts(A("D", 16 * a, 16 * b), A("D", 16 * a, 16 * b), A("EC"), OPS.add, A("EC"), OPS.is_equal)
                inturn("v")
                inturn("own test")
                tasks[-1]["mark"] = "test" if t + X == 0 else ""
        between()
        for a in range(CH * X + top, CH * X + CH, 32):
            turn[0] += 1
            bank, got = A(banks[turn[0] % 2]), A("SG", 2560 + 512 * (turn[0] % 3), 3072 + 512 * (turn[0] % 3))
            act(got, I("BW", 0, 4104, "CL", a, a + 32))
            inturn("s")
            msum(bank, [(A("IDC"), A("XR", 16 * a, 16 * a + 512))], True, False)
            msum(bank, [(A("IDH"), got)], False, True)
            if OUFIRST and banks[1] == "PT" and t == 2 and X:
                behind("flagged")
            ts(A("D", 16 * a, 16 * a + 512), bank, A("EC"), OPS.add, A("EC"), OPS.is_equal)
            inturn("v")
            if a == CH * X + top:
                inturn("first test")
        for lo, n in ENDS[X] if t == 2 and len(ENDS[X]) > 1 else ((0, SUB), (SUB, SUB)):
            a = 16 * (CH * X + lo)
            msum(A("PC%d" % X, lo, lo + n), [(A("IDH"), A("KC", 0, n))] + [(EP(p, "EQ"), A("D", a + p, a + 16 * n, 16)) for p in range(16)])
        if t == 2 and KB_LATE:
            behind("kept%d" % X)
        if X == 0:
            inturn("count")

    def sign(t, a, n):
        out, in_ = A("VV", 256 * t + a, 256 * t + a + n), A("PC%d" % (a // CH), a % CH, a % CH + n)
        if SIGNQ[2 * t + a // CH] == "s":
            act(out, in_, AFT.Sign)
        else:
            ts(out, in_, -1.0, OPS.max, 1.0, OPS.min)

    def choose(t, X):
        a = CH * X
        msum(pq(X, 0), [(A("IDH"), cb(t, X)), (A("TL" if t else "TF"), vv(t, X))])
        ts(A("SC", a, a + CH), pq(X, 0), A("CG" if t else "CF"), OPS.add, THR, OPS.min)
        msum(A("PL", 16 * t + 8 * X, 16 * t + 8 * X + 8), [(A("PB"), A("ONE", 0, 8))] * (2 - t)
             + [(EP(l), A("SC", a + l, a + CH, 16)) for l in range(16)])

    def onward(t, X):
        lo = 8 * X
        ts(A("UL", lo, lo + 8), A("PL", 16 * t + lo, 16 * t + lo + 8), 2048.0 + OFF - 15 * THR - 4096.0 * (2 - t), OPS.add, 4103.0, OPS.min)
        ts(A("CL", CH * X, CH * X + CH), I("NW", 0, 4104, "UL", lo, lo + 8), 8.0, OPS.add)
        numbers(t + 1, X)

    def relu(t, X, out, in_):
        if KEEPQ[2 * t + X] == "s":
            act(out, in_, AFT.Relu, -2048.0)
        else:
            ts(out, in_, -2048.0, OPS.add, 0.0, OPS.max)

    def keep(X, idn):
        msum(pq(X, 1), [(idn, cb(0, X)), (A("PA"), vv(0, X)), (A("PN"), vv(1, X))])
        msum(pq(X, 2), [(idn, cb(1, X)), (A("PB"), vv(1, X))])

    def back(X, lo, n):
        a = 256 * X + lo
        msum(A("PQ%d" % X, CH + 2 * lo, CH + 2 * lo + n), [(A("IDM"), A("AB", a, a + n)), (A("IDM"), A("AB", a + CH, a + CH + n))], True, False)

    def kept(X):
        relu(1, X, A("AB", 256 * X, 256 * X + 256), pq(X, 1, 2))
        if KEEPQ[2 + X] == "s":
            inturn("s")
        back(X, *ENDS[X][0])
        inturn("kept%d" % X)

    def store(w, X, lo, n, idn):
        a, b, c, o = CH + 2 * lo, 256 * X + 2 * lo, 512 + CH * X + lo, 16 * (w % 2) + 8 * X + lo // 16
        if lo:
            back(X, lo, n)
        sign(2, CH * X + lo, n)
        msum(A("PQ%d" % X, a, a + n), [(A("PN"), A("VV", c, c + n))], False, True)
        msum(A("PQ%d" % X, a + n, a + 2 * n), [(idn, A("CB", c, c + n)), (A("PB"), A("VV", c, c + n))])
        relu(2, X, A("AC", b, b + 2 * n), A("PQ%d" % X, a, a + 2 * n))
        old, new = A("AC", b, b + n), A("AC", b + n, b + 2 * n)
        if w < RO - 1:
            tt(I("F", 0, AG, "FRL", o, o + n // 16), old, new, OPS.add)
        else:
            ts(old, old, -1.0, OPS.mult, 4095.0, OPS.add)
            tt(I("YW", 0, AG, "FRL", o, o + n // 16), old, new, OPS.subtract)

    def fails(w, a, n):
        lo, hi, kk = a // 16, (a + n) // 16, n // 16
        msum(A("PT", 272 + lo, 272 + hi), [(EP(l), A("VV", a + l, a + n, 16)) for l in range(16)])
        if a >= CH:
            ts(A("FA", lo, hi), A("PT", 272 + lo, 272 + hi), -15.0, OPS.is_lt, 1792.0, OPS.mult)
        else:
            act(A("FA", lo, hi), A("PT", 272 + lo, 272 + hi), AFT.Relu, -896.0 * 14, -896.0)
        if w < RO - 1:
            for p0, p1 in ((0, EARLY), (EARLY, 16)) if a == 0 and EARLY else ((0, 16),):
                c0, c1 = a + kk * p0, a + kk * p1
                msum(A("PR", c0, c1), [(A("PF"), A("LP", c0, c1)), (A("IDH"), A("CO", c0, c1))], True, False)
                mms([(A("PR", a + kk * p, a + kk * p + kk), A("PF"), A("FA", lo, hi), False, p == p1 - 1) for p in range(p0, p1)], "close")
                act(A("LU", a + kk * p0, a + kk * p1), A("PR", a + kk * p0, a + kk * p1))
            flags(w, a, n, 0, 8 if a < CH else MID)

    def flags(w, a, n, m0, m1):
        for m in range(m0, m1):
            b, c = a + n // 8 * m, a + n // 8 * (m + 1)
            if a == 0 and m in VTAKES:
                cp(I("W", WW * (m % 2), WW * (m % 2) + WW, "LU", b, c), A("KA", CAP * w, CAP * w + 2 * n))
            else:
                act(I("W", WW * (m % 2), WW * (m % 2) + WW, "LU", b, c), A("KA", CAP * w, CAP * w + 2 * n), AFT.Silu)
                inturn("s")

    def successes(w):
        o = 16 * (w % 2)
        msum(A("PT", 256, 272), [(A("IDH"), A("FH")), (A("IDH"), A("FA"))])
        shift(LSQ, A("LSU", o, o + 16), A("PT", 256, 272), 0.0)
        if w < RO - 1:
            msum(A("PT", 304, 320), [(A("I112"), A("FH")), (A("IM"), A("CC")), (A("IM"), A("DH")), (A("IDH"), A("FA"))])
            shift(LSQ, A("LSP"), A("PT", 304, 320), -1791.0 * 16)
            msum(A("PT", 300, 301), [(A("OH"), A("FA", k, k + 1)) for k in range(16)])
            shift(NUMQ[3], A("EI"), A("PT", 300, 301), 0.0)
            ts(A("EO"), A("EI"), 1, OPS.bitwise_and)

    def last_flags(w):
        if WBQ == "v":
            cp(I("WB", 0, 3584, "LSP", 0, 16), A("KB"))
            extract_b(w + 1)
        if WBQ == "e":
            act(I("WB", 0, 3584, "LSP", 0, 16), A("KB"), AFT.Silu)
            inturn("s")
            extract_b(w + 1)
        flags(w, CH, CH, MID, 8)
        extract(w + 1)
        if WBQ == "s":
            act(I("WB", 0, 3584, "LSP", 0, 16), A("KB"), AFT.Silu)
            inturn("s")
            extract_b(w + 1)

    moved, laid = [], []

    def update(w, lo, hi):
        a, b, o = 16 * lo, 16 * hi, 16 * (w % 2)
        x = A("XR", 16 * a, 16 * b, 16) if w == RO - 1 else A("XS", 16 * o + a, 16 * o + b)
        shift(SQ[6], A("KY", lo, hi), A("PL", lo, hi), 0.0)
        tt(A("KM", lo, hi), A("PL", 16 + lo, 16 + hi), A("KY", lo, hi), OPS.min)
        tt(A("TI", lo, hi), A("PL", 32 + lo, 32 + hi), A("KM", lo, hi), OPS.min)
        ts(A("TM", lo, hi), A("TI", lo, hi), 4095, OPS.bitwise_and)
        ts(A("UF", lo, hi), A("TM", lo, hi), float(OFF), OPS.add)
        def move():
            d, new = A(MB, 0, CAP), A(MB, 0, CAP)
            act(A("DB"), I("BW", 0, 4104, "UF", lo, hi))
            if w < RO - 2:
                inturn("s")
            msum(d, [(A("IDC"), x), (A("IDB"), A("DB"))])
            act(A("DB"), d, AFT.Relu, 2.0)
            act(A("DC"), d, AFT.Relu, -2.0)
            msum(new, [(A("IDB"), A("DB")), (A("IDC"), A("DC")), (A("IDB"), x)])
            act(A("XN"), new, AFT.Copy, 254.0)
            act(I("YF", 0, 3584, "LSU", o, o + 16), A("XN"), AFT.Silu)
            if w < RO - 2:
                inturn("s")
        if w < RO - 1:
            moved.append(move)
            return
        tt(A("DB", a, b), I("BW", 0, 4104, "UF", lo, hi), x, OPS.subtract)
        ts(A("DC", a, b), A("DB", a, b), -2.0, OPS.max, 2.0, OPS.min)
        tt(I("YA", 0, 3584, "LSU", o + lo, o + hi), A("DC", a, b), x, OPS.add)

    def moved_out():
        act(A("YF", A0, AG), A("YF", A0, AG), AFT.Copy, 1.5 * 2.0 ** 23 - 256.0)
        act(A("YA", A0, AG), A("YF", A0, AG), AFT.Copy, -1.5 * 2.0 ** 23)

    def old_out():
        act(A("SG", 0, VA), A("F", A0, AG), AFT.Copy, -2048.0)
        act(A("SG", VA, 2 * VA), A("F", A0, AG), AFT.Relu, 1.0, -1.0)
        for a, b in ((0, 512), (512, 1024), (1024, VA)):
            msum(A("PT", 0, b - a), [(A("IDH"), A("SG", a, b)), (A("PB"), A("SG", VA + a, VA + b))])
            act(A("YW", A0 + a, A0 + b), A("PT", 0, b - a), AFT.Copy, 2047.0)

    ranks(0)
    for w in range(RO):
        last = w == RO - 1
        idn = A("IDN") if last else A("IDH")
        now.clear()
        now["wave"], turn[0] = w, 0
        front(w)
        for q, s, k, n in (("v", 0, 8, 1), ("v", 0, 4, 1), ("v", 0, 2, 1), ("v", 0, 1, 1), ("v", 1, 8, 1), ("v", 1, 4, 1), ("g", 2, 8, 2),
                           ("g", 1, 2, 1), ("g", 2, 4, 2), ("g", 1, 1, 1), ("g", 2, 2, 1), ("g", 3, 2, 1), ("g", 2, 1, 1), ("g", 3, 1, 1)):
            xrep(q, s, k, n)
        for s in range(4):
            seeds(s)
        if last:
            moved.pop()()
            moved_out()
        if not last:
            credit(w)
            relay()
            gcopy(A("XS", CAP * (w % 2), CAP * (w % 2) + CAP), A("XR", 0, 4096, 16))
        for t in range(3):
            for X in range(2):
                if t == 0:
                    numbers(0, X)
                compare(t, X, (SHARE_LAST if last else SHARE)[2 * t + X], ("PR", "PM") if last else ("PR", "PT"),
                        (lambda: ranks(w + 1)) if t == 2 and X and not last else (lambda: None))
                if t < 2:
                    sign(t, CH * X, CH)
                if t == 0:
                    fails(w, CH * X, CH)
                if t == 2 and X == 0 and LATE and not last:
                    last_flags(w)
                if t == 2:
                    if X == 0:
                        kept(1)
                    for lo, n in ENDS[X]:
                        store(w, X, lo, n, idn)
                choose(t, X)
                if t < 2:
                    onward(t, X)
                if t == 1:
                    keep(X, idn)
                if t == 1 and X == 0:
                    kept(0)
                    if not last and not LATE:
                        last_flags(w)
            if t == 0:
                successes(w)
                if last:
                    old_out()
        if not last:
            ghosts_out(w + 1)
            if moved:
                moved.pop()()
            act(A("EC"), A("EO"), AFT.Copy, C3, -8.0)
            update(w, 0, 16)
    dma("y", T.yf[:], T.YW[:, A0:AG], [("YW", A0, AG)], [], "oy", 655360)
    update(RO - 1, 0, 8)
    update(RO - 1, 8, 16)
    dma("y", T.ya[:], T.YA[:, A0:AG], [("YA", A0, AG)], [], "oa", 327680)

    for k in range(4):
        arrive(nxt, ("BW", HALO + XB[k], HALO + min(XB[k + 1], NH)), "hb%d" % k)
    for h in range(4):
        arrive(nxt, ("NW", HALO + 512 * h, HALO + 512 * h + 512), "hn%d" % h)
    arrive(prv, ("F", AG, AE), "gh0")
    if not ORDER:
        ORDER["calls"] = arrange(tasks, before)
    for j in ORDER["calls"]:
        tasks[j]["run"]()

    need("y", "oy", 16)
    need("y", "oa", 16)
    for w in range(RO):
        need("g", "lg%d" % w, len(engines(core, nxt, "gh%d" % w)))
    need("g", "lc", RO - 1)
    for s in HALOS:
        need("g", "l" + s, len(engines(core, prv, s)))
    for s in ("cv", "cs", "cp", "cg"):
        need("y", s, cnt[s])
